import numpy as np, ml_dtypes
CORES = [40,41,42,43,44,45,46,47]
N = 8
BF = ml_dtypes.bfloat16
def gentries(a):
    return np.ascontiguousarray(a.reshape(8, 16, -1).transpose(0, 2, 1)).reshape(8, -1)
def gtable(e):
    e = np.asarray(e); return np.ascontiguousarray(e.reshape(8, -1, 16).transpose(0, 2, 1)).reshape(128, -1).astype(np.int32)
W, NB, R, H = 2048, 16, 3, 3
KAP = (101, 1303, 2717, 3911)
def spot(u, l):
    return ((u * u >> 5) + 37 * u + KAP[l]) & (W - 1)
def figures(x, n):
    return np.take_along_axis(x, n.reshape(8, 1, -1), 2).reshape((8, 16) + n.shape[1:])
def witness(x, w, F):
    w = w.reshape(8, 16, 1, 1, 1)
    for l in range(4):
        h = F.shape[3] >> 1
        a, b = F[:, :, :, :h], F[:, :, :, h:]
        u = np.add.reduce(w * np.abs(a - b), axis=1) & (W - 1)
        F = figures(x, spot(u, l))
    return F[:, :, :, 0]
def judge(x, w, n):
    F = figures(x, n)
    col = witness(x, w, F); row = witness(x, w, F.transpose(0, 1, 2, 4, 3))
    return col, np.add.reduce(np.abs(col - row), axis=1), np.add.reduce(col, axis=1), np.add.reduce(row, axis=1)
def readings(x, w, n):
    x8 = np.broadcast_to(x, (8, 16, W)); w8 = np.broadcast_to(w, (8, 16))
    return np.ascontiguousarray(witness(x8, w8, figures(x8, n.reshape(8, -1, 16, 1)))[..., 0].transpose(1, 0, 2)).reshape(16, -1)
def parts(rng):
    x = rng.integers(0, 256, (N, 8, 16, W)); w = rng.integers(0, 256, (N, 8, 16)); th = rng.integers(800, 2000, (N, 8, 16))
    return x, w, th, rng.integers(0, W, (N, 8, NB * 256)), rng.integers(0, W, (N, 8, NB * 256))
def pack(x, w, th, b, c):
    return {"xf": np.ascontiguousarray(x.reshape(N, 128, W)).astype(np.float32).astype(BF), "bn": np.stack([gtable(a) for a in b]), "cn": np.stack([gtable(a) for a in c]),
            "wt": np.ascontiguousarray(w.reshape(N, 128, 1)).astype(np.int32), "th": np.ascontiguousarray(th.reshape(N, 128, 1)).astype(np.int32)}
def setup_inputs(rng):
    return pack(*parts(rng))
def setup_inputs_spread(rng):
    x, w, th, b, c = parts(rng)
    s = np.exp2(8.5 * rng.random((N, 8, 1, W))) * (rng.random((N, 8, 1, W)) > 0.0625)
    x = np.minimum((s * rng.random((N, 8, 16, W))).astype(np.int64), 255)
    w = np.minimum(np.exp2(8 * rng.random((N, 8, 16))).astype(np.int64) - rng.integers(0, 2, (N, 8, 16)), 255)
    th = np.minimum(np.exp2(11 * rng.random((N, 8, 16))).astype(np.int64), 4080)
    b = np.minimum((W * rng.random(b.shape) ** 3).astype(np.int64), W - 1); c = np.minimum((W * rng.random(c.shape) ** 2).astype(np.int64), W - 1)
    b[:, 1::2] = W - 1 - b[:, 1::2]; c[:, ::3] = W - 1 - c[:, ::3]
    return pack(x, w, th, b, c)
def setup_inputs_ends(rng):
    x = 255 * rng.integers(0, 2, (N, 8, 16, W)); w = 255 * rng.integers(0, 2, (N, 8, 16)); th = 4080 * rng.integers(0, 2, (N, 8, 16))
    w[:, 0, 0] = 0; w[:, 0, 15] = 255; th[:, 0, 0] = 0; th[:, 0, 15] = 4080
    b, c = [np.where(rng.random((N, 8, NB * 256)) < 0.8, (W - 1) * rng.integers(0, 2, (N, 8, NB * 256)), rng.integers(0, W, (N, 8, NB * 256))) for i in range(2)]
    for g in (2, 5, 7):
        x[:, g] = 255 * rng.integers(0, 2, (N, 1, W)); w[:, g] = 255
    for q in range(0, N - 1, 2): w[q, 7, q] = 0
    for q in range(N):
        for g in (2, 5, 7):
            u = 255 * int(np.add.reduce(w[q, g])) & (W - 1)
            x[q, g, :, 0] = 0; x[q, g, :, W - 1] = 255
            for l in range(4): x[q, g, :, spot(0, l)] = 0
            for l in range(4): x[q, g, :, spot(u, l)] = 255
    bb = b.reshape(N, 8, NB, 16, 16)
    bb[:, 7, :, :, 0] = 0; bb[:, 7, NB - 1] = 0; bb[:, 7, NB - 1, 0, 15] = W - 1; bb[:, 7, NB - 1, 1, 0] = W - 1
    th[:, 7, 15] = 0; th[N - 1, 7, 15] = 4080
    return pack(x, w, th, bb.reshape(N, 8, NB * 256), c)
def setup_inputs_corners(rng):
    x, w, th, b, c = parts(rng)
    for q in range(N):
        for g in range(8):
            k = (g + q) % 8
            if k == 0: w[q, g] = 0
            if k == 1: w[q, g] = 255
            if k == 2: w[q, g] = 16 * rng.integers(1, 16, 16); th[q, g] = 0
            if k == 3: th[q, g] = 4080
            if k == 4: b[q, g] = np.repeat(rng.choice(np.array([0, 1, W - 1, W >> 1]), NB), 256); c[q, g] = rng.permutation(NB * 256) % W
            if k == 5: b[q, g] = np.arange(NB * 256) % W; c[q, g] = W - 1 - b[q, g]
            if k == 6: w[q, g] = 0; w[q, g, 15] = 255
            if k == 7: x[q, g] = 255 * rng.integers(0, 2, (1, W))
    return pack(x, w, th, b, c)
def setup_inputs_full(rng):
    x, w, th, b, c = parts(rng); bb = b.reshape(N, 8, NB, 16, 16); z = spot(0, 3)
    for q in range(N):
        for g in range(8):
            k = (g + q) % 8
            if k < 4: th[q, g] = rng.integers(0, 256, 16)
            if k < 3:
                w[q, g, 0] |= 1; x[q, g, :, z] = rng.integers(240, 256, 16)
                n = rng.integers(0, W, (512, 16)); f = readings(x[q, g], w[q, g], n)
                s = np.add.reduce(f, axis=0); d = np.add.reduce(w[q, g][:, None] * f, axis=0) & (NB - 1)
                for v, p in enumerate(rng.permutation(NB)):
                    turn = k == 1 or (k == 2 and p % 2 == 1)
                    i = int(np.argmax(np.where(d == v, -s if turn else s, -5000)))
                    bb[q, g, p] = n[i][:, None] if turn else rng.integers(0, W, (1, 16))
                    bb[q, g, p, :, 0] = n[i]
            if k == 3:
                w[q, g] = 255; x[q, g, :, z] = 255; x[q, g, rng.permutation(16)[:2 + q], z] = 254
                bb[q, g, :, :, 0] = rng.integers(0, W, (NB, 1))
            if k == 4: x[q, g] = rng.integers(235, 256, (16, W)); w[q, g] = rng.integers(253, 256, 16)
            if k == 7: x[q, g] = rng.integers(246, 256, (16, W)); w[q, g] = rng.integers(240, 256, 16)
            if k == 5 or k == 6:
                e = int(rng.choice(np.array([8, 24, 60, 90])))
                x[q, g] = np.abs(255 * rng.integers(0, 2, (1, W)) - rng.integers(0, e + 1, (16, W))); w[q, g] = rng.integers(240, 256, 16)
        col, D, A, E = judge(x[q], w[q], bb[q])
        i = np.argmax(np.where(D >= 2304, rng.random(D.shape), -1.0), axis=1)
        t = np.take_along_axis(D - (A & 15), i[:, None, :], 1)[:, 0] - rng.integers(0, 2, (8, 16))
        for g in range(8):
            k = (g + q) % 8
            if k > 3: th[q, g] = np.minimum(np.maximum(t[g], 0), 4080)
            if k == 4 or k == 7: th[q, g, ::2] = rng.integers(0, 16, 8)
    return pack(x, w, th, bb.reshape(N, 8, NB * 256), c)
def setup_inputs_ties(rng):
    x, w, th, b, c = parts(rng)
    base = rng.integers(0, 256, (N, 16, 1)); order = np.argsort(rng.random((N, 16, W)), axis=1)
    x[:, 6] = np.take_along_axis(np.ascontiguousarray(np.broadcast_to(base, (N, 16, W))), order, 1)
    x[:, 4, :, 1::2] = x[:, 4, :, 0::2]
    bb = b.reshape(N, 8, NB, 16, 16)
    s = bb[:, 1, ::3].copy(); bb[:, 1, ::3] = np.triu(s) + np.swapaxes(np.triu(s, 1), -1, -2)
    bb[:, 2, :, :, 0] = bb[:, 2, :1, :, 0].copy()
    for q in range(N):
        col, D, A, E = judge(x[q], w[q], bb[q])
        v = np.take_along_axis(D - (A & 15), rng.integers(0, NB, (8, 1, 16)), 1)[:, 0]
        th[q] = np.minimum(np.maximum(v + rng.choice(np.array([-1, 0, 0, 1]), (8, 16)), 0), 4080)
    th[:, 6, 1::2] = 0
    return pack(x, w, th, bb.reshape(N, 8, NB * 256), c)
def check_inputs(d):
    bad = []
    for k, lo, hi in (("xf", 0, 255), ("bn", 0, W - 1), ("cn", 0, W - 1), ("wt", 0, 255), ("th", 0, 4080)):
        v = np.asarray(d[k]).astype(np.float64)
        if not (np.min(v) >= lo and np.max(v) <= hi): bad.append("range of " + k)
        if np.any(v != np.floor(v)): bad.append("whole numbers of " + k)
    return bad
def reference(xf, bn, cn, wt, th):
    x = np.asarray(xf).astype(np.float32).astype(np.int64).reshape(N, 8, 16, W); w = wt.astype(np.int64).reshape(N, 8, 16); lim = th.astype(np.int64).reshape(N, 8, 16)
    b = np.stack([gentries(a) for a in bn]).astype(np.int64).reshape(N, 8, NB, 16, 16)
    c = np.stack([gentries(a) for a in cn]).astype(np.int64).reshape(N, 8, NB, 16, 16)
    cnt = np.zeros((N, 8, NB, 16), np.int64); low = np.tril(np.ones((NB, NB), bool), -1)
    for t in range(R):
        for a in range(N):
            q = (a - H * t) % N
            col, D, A, E = judge(x[a], w[a], b[q])
            qr = D > lim[a][:, None, :] + (A & 15); cnt[a] += qr
            d = np.add.reduce(w[a][:, :, None] * col[:, :, :, 0], axis=1) & (NB - 1)
            act = ~np.any((d[:, :, None] == d[:, None, :]) & low, axis=2)
            for g in range(8):
                for k in np.flatnonzero(act[g]):
                    one, two = b[q, g, k], c[a, g, d[g, k]]
                    j = np.flatnonzero(qr[g, k] & (A[g, k] <= E[g, k])); v = one[:, j]; one[:, j] = two[:, j]; two[:, j] = v
                    j = np.flatnonzero(qr[g, k] & (A[g, k] > E[g, k])); v = one[j]; one[j] = two[j]; two[j] = v
    yb = np.stack([gtable(b[(a - H * (R - 1)) % N].reshape(8, -1)) for a in range(N)]); yc = np.stack([gtable(e.reshape(8, -1)) for e in c])
    return {"yb": yb.astype(np.float32), "yc": yc.astype(np.float32), "yq": np.ascontiguousarray(cnt.transpose(0, 1, 3, 2)).reshape(N, 128, NB).astype(np.float32)}

@@ -1,0 +1,543 @@
+import numpy as np
+from concourse.mybir import dt, AluOpType, AxisListType, ActivationFunctionType
+import comms_topo
+
+OP = AluOpType
+AF = ActivationFunctionType
+R, NB, HOP = 3, 16, 3
+KAP = (101, 1303, 2717, 3911)
+W = 2048
+
+SCRATCH = {
+    "xw": ("sbuf", [128, 2048], "bfloat16"),
+    "tu": ("sbuf", [128, 128], "int32"),
+    "tv": ("sbuf", [128, 128], "int32"),
+    "tf": ("sbuf", [128, 128], "float32"),
+    "tp": ("sbuf", [128, 128], "int32"),
+    "tq": ("sbuf", [128, 128], "int32"),
+    "bni": ("sbuf", [128, 16, 16], "int32"),
+    "cni": ("sbuf", [128, 256], "int32"),
+    "wti": ("sbuf", [128, 1], "int32"),
+    "thi": ("sbuf", [128, 1], "int32"),
+    "cw": ("sbuf", [128, 4096], "float32"),
+    "pi": ("sbuf", [128, 8], "int32"),
+    "pj": ("sbuf", [128, 8], "int32"),
+    "icol": ("sbuf", [128, 8], "float32"),
+    "wcol": ("sbuf", [128, 8], "float32"),
+    "th16": ("sbuf", [128, 8], "float32"),
+    "ones": ("sbuf", [128, 128], "bfloat16"),
+    "m1": ("sbuf", [128, 128], "bfloat16"),
+    "bo": ("sbuf", [128, 128], "bfloat16"),
+    "bo256": ("sbuf", [128, 128], "bfloat16"),
+    "bow": ("sbuf", [128, 128], "bfloat16"),
+    "ident": ("sbuf", [128, 128], "bfloat16"),
+    "nident": ("sbuf", [128, 128], "bfloat16"),
+    "zw": ("sbuf", [128, 144], "bfloat16"),
+    "z1": ("sbuf", [128, 144], "bfloat16"),
+    "z16": ("sbuf", [128, 144], "bfloat16"),
+    "prow": ("sbuf", [128, 128], "float32"),
+    "cmpc": ("sbuf", [128, 256], "float32"),
+    "bli": ("sbuf", [128, 16], "int32"),
+    "bl": ("sbuf", [128, 16], "uint16"),
+    "zero": ("sbuf", [128, 8], "float32"),
+    "bo16": ("sbuf", [128, 128], "bfloat16"),
+    "oh": ("sbuf", [128, 24], "bfloat16"),
+    "ex": ("sbuf", [128, 16], "float32"),
+    "qs": ("sbuf", [128, 16], "float32"),
+    "qf": ("sbuf", [128, 16], "float32"),
+}
+SCRATCH["xt"] = ("sbuf", [128, 4 * W], "bfloat16")
+SCRATCH["xa"] = ("sbuf", [128, 512], "int32")
+SCRATCH["xb"] = ("sbuf", [128, 512], "int32")
+SCRATCH["xl"] = ("sbuf", [128, 512], "uint16")
+for _t in range(R):
+    SCRATCH["qr%d" % _t] = ("sbuf", [128, 16], "float32")
+    for _h in range(2):
+        SCRATCH["lt%d%d" % (_t, _h)] = ("sbuf", [128, 128], "uint16")
+        SCRATCH["bn%d%d" % (_t, _h)] = ("sbuf", [128, 128], "float32")
+        SCRATCH["b3%d%d" % (_t, _h)] = ("sbuf", [128, 8, 16], "float32")
+        if _t < R - 1:
+            SCRATCH["ls%d%d" % (_t, _h)] = ("sbuf", [128, 128], "uint16")
+for _h in range(2):
+    for _n, _s, _d in (("fa", [128, 1024], "bfloat16"), ("dc", [128, 1024], "bfloat16"), ("ac", [128, 1024], "bfloat16"),
+                       ("ar", [128, 2, 8, 64], "bfloat16"), ("i1", [128, 128], "int32"),
+                       ("j0", [128, 16, 8], "int32"), ("j1", [128, 16, 4], "int32"), ("j2", [128, 16, 2], "int32"), ("j3", [128, 2, 8], "int32"),
+                       ("la", [128, 64], "uint16"), ("lb", [128, 64], "uint16"),
+                       ("wc", [128, 128], "bfloat16"), ("da", [128, 2, 128], "bfloat16"),
+                       ("ii", [128, 16], "int32"), ("id", [128, 16], "int32"), ("ce", [128, 8], "bfloat16"),
+                       ("go", [128, 8], "uint16"), ("so", [128, 8], "uint16"),
+                       ("tb", [128, 128], "float32"), ("cp", [128, 128], "float32"), ("ms", [128, 128], "float32"),
+                       ("t16", [128, 8], "float32"), ("ta", [128, 8], "float32"), ("qa", [128, 8], "float32"), ("sg", [128, 8], "float32"),
+                       ("zz", [128, 8], "float32"), ("ee", [128, 256], "bfloat16")):
+        SCRATCH["%s_%d" % (_n, _h)] = ("sbuf", _s, _d)
+    for _n in ("S", "F", "X", "Y"):
+        SCRATCH["%s_%d" % (_n, _h)] = ("psum", [128, 512], "float32")
+
+DMAS = ["ld%d" % _k for _k in range(8)] + ["st%d" % _k for _k in range(4)]
+SEMAPHORES = ["V", "A", "P", "G", "sent"] + DMAS + ["%s%d%d" % (_a, _t, _h) for _a in ("al", "ab") for _t in (1, 2) for _h in (0, 1)]
+
+COSTS = ({"cy": 0.00083, "V": 0.03, "A": 0.05, "P": 0.0005, "g": 1.5, "s": 3.8, "hop": 0.09},
+         {"cy": 0.00083, "V": 0.05, "A": 0.065, "P": 0.00075, "g": 1.5, "s": 3.8, "hop": 0.07},
+         {"cy": 0.00083, "V": 0.02, "A": 0.03, "P": 0.00042, "g": 1.3, "s": 3.0, "hop": 0.12},
+         {"cy": 0.00083, "V": 0.03, "A": 0.04, "P": 0.0005, "g": 1.9, "s": 5.0, "hop": 0.07})
+
+
+def cost(q, n, c):
+    if q not in ("A", "V", "P"):
+        return n
+    if q == "P":
+        return n * c["P"]
+    if isinstance(n, tuple):
+        return (0.065 if q == "A" else 0.05) + n[1] * c[n[0]] * c["cy"]
+    return c[q] + max(64, n) * c["cy"]
+
+
+CH = (2, 4, 2, 1)
+SPLIT = (0,)
+SEED, TRIES = 11, 12000
+
+
+def build(core, T, topo, VEC):
+    ops, lastw, readers, banks = [], {}, {}, {}
+
+    def add(q, fn, rd=(), wr=(), bk=(), c=0.1, sem=None, n=1, note=""):
+        deps, order = set(), set()
+        for k in rd:
+            if k in lastw:
+                deps.add(lastw[k])
+        for k in wr:
+            if k in lastw:
+                deps.add(lastw[k])
+            deps.update(readers.get(k, ()))
+        for b in bk:
+            for e, o in banks.get(b, {}).items():
+                if e != q:
+                    deps.add(o)
+                else:
+                    order.add(o)
+        me = len(ops)
+        for k in wr:
+            lastw[k], readers[k] = me, []
+        for k in rd:
+            readers.setdefault(k, []).append(me)
+        for b in bk:
+            banks.setdefault(b, {})[q] = me
+        deps.discard(me)
+        ops.append({"cls": 0, "q": q, "fn": fn, "deps": deps, "order": order - deps, "c": c, "sem": sem, "n": n, "note": note})
+        return me
+
+    def V(fn, rd, wr, n, bk=(), note=""):
+        return add("V", fn, rd, wr, bk, n, note=note)
+
+    def A(fn, rd, wr, n, bk=(), note=""):
+        return add("A", fn, rd, wr, bk, n, note=note)
+
+    def P(fn, rd, wr, n, bk=(), note=""):
+        return add("P", fn, rd, wr, bk, n, note=note)
+
+    def G(fn, rd, wr, c, note=""):
+        return add("G", fn, rd, wr, (), c, note=note)
+
+    def load(q, k, out, in_, wr, c):
+        add(q, lambda e: e.dma_start(out, in_), (), wr, (), c, sem="ld%d" % k, n=16, note="load")
+
+    gat = lambda n: ("g", n)
+
+    def gather_on(e, out, ind):
+        if e is VEC[0]:
+            return e.tensor_copy(out, ind)
+        return e.activation(out, ind, AF.Identity)
+
+    def either(fn, rd, wr, n, note):
+        add("AV", fn, rd, wr, (), n, note=note)
+
+    load("Y", 0, T.bni[:, :, :], T.bn[:, :], ("bni",), 2.2)
+    load("Q", 1, T.xw[:, 0:W], T.xf[:, :], ("xw",), 4.0)
+    load("Y", 2, T.wti[:, :], T.wt[:, :], ("wti",), 2.5)
+    load("Y", 3, T.thi[:, :], T.th[:, :], ("thi",), 2.5)
+    load("Q", 5, T.cni[:, :], T.cn[:, :], ("cni",), 6.0)
+
+    G(lambda e: e.iota(T.pi[:, 0:1], [[0, 1]], 0, 1), (), ("pi",), 0.2)
+    G(lambda e: e.iota(T.tu[:, :], [[16, 128]], 0, 1), (), ("tu",), 0.34)
+    G(lambda e: e.iota(T.bli[:, :], [[0, 2], [1, 8]], 0, 0), (), ("bli",), 0.2)
+    G(lambda e: e.iota(T.prow[:, :], [[0, 8], [1, 16]], 0, 0, allow_small_or_imprecise_dtypes=True), (), ("prow",), 0.4)
+    V(lambda e: e.memset(T.ones[:, :], 1.0), (), ("ones",), 128)
+    G(lambda e: e.affine_select(T.ident[:, :], T.ones[:, :], [[-1, 128]], OP.is_equal, 0.0, 0, 1), ("ones",), ("ident",), 0.4)
+    G(lambda e: e.affine_select(T.m1[:, :], T.ones[:, :], [[-16, 8], [0, 16]], OP.is_ge, 0.0, 0, 1), ("ones",), ("m1",), 0.4)
+    G(lambda e: e.affine_select(T.bo[:, :], T.m1[:, :], [[16, 8], [0, 16]], OP.is_ge, 0.0, 15, -1), ("m1",), ("bo",), 0.4)
+    V(lambda e: e.memset(T.zw[:, :], 0.0), (), ("zw",), 144)
+    V(lambda e: e.memset(T.z1[:, :], 0.0), (), ("z1",), 144)
+    V(lambda e: e.memset(T.z16[:, :], 0.0), (), ("z16",), 144)
+    V(lambda e: e.memset(T.zero[:, :], 0.0), (), ("zero",), 8)
+    V(lambda e: e.memset(T.oh[:, 0:1], 0.0), (), ("ohz",), 8)
+
+    def lists_in(h):
+        for ph in range(2):
+            V(lambda e, ph=ph: e.tensor_copy(T["lt0%d" % h][:, 64 * ph:64 * ph + 64], T.bni[:, 8 * h:8 * h + 8, 8 * ph:8 * ph + 8]),
+              ("bni",), ("lt0%d%d" % (h, ph),), 64)
+
+    def charts_in(h):
+        V(lambda e: e.tensor_copy(T["bn0%d" % h][:, :], T.bni[:, 8 * h:8 * h + 8, :]), ("bni",), ("bn0%d" % h,), 128)
+    lists_in(0)
+    V(lambda e: e.tensor_scalar(T.pj[:, 0:1], T.pi[:, 0:1], 15, None, OP.bitwise_and), ("pi",), ("pj",), 8)
+    V(lambda e: e.tensor_copy(T.icol[:, 0:1], T.pj[:, 0:1]), ("pj",), ("icol",), 8)
+    V(lambda e: e.tensor_tensor(T.wcol[:, 4:5], T.pi[:, 0:1], T.icol[:, 0:1], OP.subtract), ("pi", "icol"), ("p16",), 8)
+    V(lambda e: e.tensor_scalar(T.tv[:, :], T.tu[:, :], T.wcol[:, 4:5], None, OP.subtract), ("tu", "p16"), ("tv",), 128)
+    V(lambda e: e.tensor_scalar(T.tf[:, :], T.tv[:, :], 1184.0, None, OP.add), ("tv",), ("tf",), 128)
+    V(lambda e: e.tensor_tensor(T.tp[:, :], T.tv[:, :], T.tf[:, :], OP.mult), ("tv", "tf"), ("tp",), 256)
+    V(lambda e: e.tensor_scalar(T.tq[:, :], T.tp[:, :], 5, W - 1, OP.arith_shift_right, OP.bitwise_and), ("tp",), ("tq",), 128)
+    for l in range(4):
+        ls_ = slice(128 * l, 128 * l + 128)
+        V(lambda e, l=l, s=ls_: e.tensor_scalar(T.xa[:, s], T.tq[:, :], float(KAP[l] % W), None, OP.add), ("tq",), ("xa%d" % l,), 128)
+        V(lambda e, l=l, s=ls_: e.tensor_scalar(T.xb[:, s], T.xa[:, s], W - 1, None, OP.bitwise_and), ("xa%d" % l,), ("xb%d" % l,), 128)
+        V(lambda e, l=l, s=ls_: e.tensor_copy(T.xl[:, s], T.xb[:, s]), ("xb%d" % l,), ("xl%d" % l,), 128)
+        for c in range(4):
+            either(lambda e, l=l, c=c: gather_on(e, T.xt[:, W * l + 512 * c:W * l + 512 * c + 512], T.xw[:, :].indirect(T.xl[:, 128 * l + 32 * c:128 * l + 32 * c + 32])),
+                   ("xw", "xl%d" % l), ("x%d%d" % (l, c),), gat(512), "table")
+    V(lambda e: e.tensor_scalar(T.nident[:, :], T.ident[:, :], -1.0, None, OP.mult), ("ident",), ("nident",), 64)
+    V(lambda e: e.tensor_copy(T.wcol[:, 0:1], T.wti[:, :]), ("wti",), ("wcol",), 8)
+    V(lambda e: e.tensor_scalar(T.zw[:, 15:128:16], T.bo[:, 0:128:16], T.wcol[:, 0:1], None, OP.mult), ("bo", "wcol"), ("zw",), 8)
+    lists_in(1)
+    V(lambda e: e.tensor_scalar(T.th16[:, 0:1], T.thi[:, :], 0.0625, None, OP.mult), ("thi",), ("th16",), 8)
+    V(lambda e: e.tensor_copy(T.bl[:, :], T.bli[:, :]), ("bli",), ("bl",), 16)
+    V(lambda e: e.tensor_copy(T.z1[:, 15:128:16], T.bo[:, 0:128:16]), ("bo",), ("z1",), 8)
+    V(lambda e: e.tensor_scalar(T.z16[:, 15:128:16], T.bo[:, 0:128:16], 0.0625, None, OP.mult), ("bo",), ("z16",), 8)
+    V(lambda e: e.tensor_scalar(T.bow[:, :], T.bo[:, :], T.wcol[:, 0:1], None, OP.mult), ("bo", "wcol"), ("bow",), 64)
+    V(lambda e: e.tensor_scalar(T.bo256[:, :], T.bo[:, :], 256.0, None, OP.mult), ("bo",), ("bo256",), 64)
+    V(lambda e: e.tensor_scalar(T.bo16[:, :], T.bo[:, :], T.icol[:, 0:1], 16.0, OP.mult, OP.mult), ("bo", "icol"), ("bo16",), 64)
+    V(lambda e: e.memset(T.cmpc[:, 128:256], -0.25), (), ("cmpc",), 128)
+    V(lambda e: e.tensor_scalar(T.cmpc[:, 0:128], T.prow[:, :], T.icol[:, 0:1], 0.25, OP.not_equal, OP.add), ("prow", "icol"), ("cmpc2",), 128)
+    charts_in(0)
+    charts_in(1)
+    V(lambda e: e.tensor_copy(T.cw[:, 0:256], T.cni[:, :]), ("cni",), ("cw",), 256)
+
+    def half(t, h):
+        B = lambda n: T["%s_%d" % (n, h)]
+        K = lambda n: "%s_%d" % (n, h)
+        S, F, X, Y = B("S"), B("F"), B("X"), B("Y")
+        lt, bn = T["lt%d%d" % (t, h)], T["bn%d%d" % (t, h)]
+        win = T.xw[:, 0:W]
+        fa, dc, ac, ar = B("fa"), B("dc"), B("ac"), B("ar")
+        zs = lambda z, i: z[:, 15 - i:143 - i]
+
+        def of(keys, c, ch):
+            return keys if ch == 1 or len(keys) == 1 else (keys[2 * c // ch],)
+
+        def gather_pair(la, lb, ka, kb, n, w, wk, ch):
+            m = n // ch
+            for c in range(ch):
+                either(lambda e, c=c: gather_on(e, fa[:, m * c:m * c + m], w.indirect(la[:, m * c // 16:(m * c + m) // 16])),
+                       of(ka, c, ch) + wk, (K("fa%d" % c),), gat(m), "gA")
+            for c in range(ch):
+                V(lambda e, c=c: e.tensor_tensor(dc[:, m * c:m * c + m], w.indirect(lb[:, m * c // 16:(m * c + m) // 16]), fa[:, m * c:m * c + m], OP.subtract),
+                  of(kb, c, ch) + wk + (K("fa%d" % c),), (K("dc%d" % c),), gat(m), note="gB")
+            for c in range(ch):
+                A(lambda e, c=c: e.activation(ac[:, m * c:m * c + m], dc[:, m * c:m * c + m], AF.Abs), (K("dc%d" % c),), (K("ac%d" % c),), m, note="abs")
+            return tuple(K("fa%d" % c) for c in range(ch)), tuple(K("dc%d" % c) for c in range(ch)), tuple(K("ac%d" % c) for c in range(ch))
+
+        def weigh(l, n, keys):
+            for s, (c0, c1) in parts(l, n):
+                out = psum_of(s, c1 - c0)
+
+                def fn(e, out=out, c0=c0, c1=c1):
+                    for i in range(16):
+                        o = e.matmul(out, zs(T.zw, i), ac[:, 16 * c0 + i:16 * c1:16], i == 0, i == 15)
+                    return o
+                ch = len(keys)
+                ks = keys if ch == 1 or len(parts(l, n)) == 1 else keys[s * ch // 2:(s + 1) * ch // 2]
+                P(fn, ks + ("zw",), (K("S%d" % s),), 16 * max(64, c1 - c0), (K("S"),) if s == 0 else (K("F"),), note="weigh")
+
+        def parts(l, n):
+            return ((0, (0, n // 2)), (1, (n // 2, n))) if l in SPLIT else ((0, (0, n)),)
+
+        def psum_of(s, n):
+            return S[:, 0:n] if s == 0 else F[:, 256:256 + n]
+
+        def index(l, n):
+            i1, j, m = B("i1"), B("j%d" % l), n // 16
+            for s, (c0, c1) in parts(l, n):
+                bank = (K("S"),) if s == 0 else (K("F"),)
+                src = psum_of(s, c1 - c0)
+                ks = (K("S%d" % s),)
+                V(lambda e, src=src, c0=c0, c1=c1: e.tensor_copy(i1[:, c0:c1], src), ks, (K("i1%d" % s),), c1 - c0, bank, note="i1")
+                rows_ = slice(c0 // m, c1 // m) if l < 3 else slice(c0 // 8, c1 // 8)
+                V(lambda e, c0=c0, c1=c1, rows_=rows_: e.tensor_scalar(j[:, rows_, :], i1[:, c0:c1], W - 1, None, OP.bitwise_and),
+                  (K("i1%d" % s),), (K("j%d" % s),), c1 - c0, note="i2")
+                for x, name in enumerate(("la", "lb")):
+                    if l == 3 and len(parts(l, n)) == 2 and x != s:
+                        continue
+                    wr = tuple(K("%s%d" % (name, y)) for y in ((0, 1) if l == 3 or len(parts(l, n)) == 1 else (s,)))
+                    if l < 3:
+                        V(lambda e, c0=c0, c1=c1, x=x, name=name, rows_=rows_: e.tensor_copy(B(name)[:, c0 // 2:c1 // 2], j[:, rows_, x * (m // 2):(x + 1) * (m // 2)]),
+                          (K("j%d" % s),), wr, (c1 - c0) // 2, note="i6")
+                    else:
+                        V(lambda e, x=x, name=name: e.tensor_copy(B(name)[:, 0:8], j[:, x, :]), (K("j%d" % s),), wr, 8, note="i6")
+            return T.xt[:, W * l:W * l + W], tuple("x%d%d" % (l, c) for c in range(4))
+
+        fk, dk, ak = gather_pair(lt[:, 0:64], lt[:, 64:128], ("lt%d%d0" % (t, h),), ("lt%d%d1" % (t, h),), 1024, win, ("xw",), CH[0])
+
+        def rows(bank, srcs):
+            def fn(e):
+                for c in range(8):
+                    lst = [(T.ident, s[:, c:1024:16]) for s in srcs] + [(T.nident, s[:, c + 8:1024:16]) for s in srcs]
+                    for i, (w, r) in enumerate(lst):
+                        o = e.matmul(bank[:, c:512:8], w[:, :], r, i == 0, i == len(lst) - 1)
+                return o
+            return fn
+        P(rows(X, (fa,)), fk + ("ident", "nident"), (K("X"),), 1024, (K("X"),), note="row0")
+        P(rows(Y, (fa, dc)), fk + dk + ("ident", "nident"), (K("Y"),), 2048, (K("Y"),), note="row1")
+        for ph, (bank, kk) in enumerate(((X, K("X")), (Y, K("Y")))):
+            A(lambda e, ph=ph, bank=bank: e.activation(ar[:, ph, :, :], bank[:, :], AF.Abs), (kk,), (K("ar%d" % ph),), 512, (kk,), note="absr")
+        sep = 0 in SPLIT
+        kr, br = (K("S1"), (K("F"),)) if sep else (K("S0"), (K("S"),))
+
+        def wcol(e):
+            for i in range(16):
+                o = e.matmul(S[:, 0:64], zs(T.zw, i), ac[:, i:1024:16], i == 0, i == 15)
+            return o
+        P(wcol, ak + ("zw",), (K("S0"),), 1024, (K("S"),), note="weigh")
+
+        def wrow(e):
+            for ph in range(2):
+                for pl in range(8):
+                    o = e.matmul(psum_of(1, 64) if sep else S[:, 64:128], zs(T.zw, 8 * ph + pl), ar[:, ph, :, 8 * pl:8 * pl + 8], ph + pl == 0, 8 * ph + pl == 15)
+            return o
+        P(wrow, ("zw", K("ar0"), K("ar1")), (kr,), 1024, br, note="weighr")
+        w, wk = index(0, 128)
+        for l, n in ((1, 1024), (2, 512), (3, 256)):
+            fk, dk, ak = gather_pair(B("la"), B("lb"), (K("la0"), K("la1")), (K("lb0"), K("lb1")), n, w, wk, CH[l])
+            weigh(l, n // 16, ak)
+            w, wk = index(l, n // 16)
+        wc, da, ii, id_ = B("wc"), B("da"), B("ii"), B("id")
+        Fa, FaK = B("Y"), (K("Y"),)
+        A(lambda e: e.activation(wc[:, :], w.indirect(B("la")[:, 0:8]), AF.Identity), wk + (K("la0"),), (K("wc"),), gat(128), note="gWC")
+        V(lambda e: e.tensor_tensor(da[:, 0, :], w.indirect(B("lb")[:, 0:8]), wc[:, :], OP.subtract), wk + (K("lb0"), K("wc")), (K("dw"),), gat(128), note="gWR")
+        A(lambda e: e.activation(da[:, 1, :], da[:, 0, :], AF.Abs), (K("dw"),), (K("aw"),), 128, note="absW")
+        P(lambda e: e.matmul(F[:, 0:8], T.bow[:, :], wc[:, 0:128:16], True, True), (K("wc"), "bow"), (K("Fd"),), 64, (K("F"),), note="donor")
+
+        def asum(e):
+            for i in range(16):
+                o = e.matmul(Fa[:, 48:56], zs(T.z1, i), wc[:, i:128:16], i == 0, i == 15)
+            return o
+        P(asum, (K("wc"), "z1"), (K("Fa"),), 1024, FaK, note="A")
+        V(lambda e: e.tensor_copy(ii[:, 0:8], F[:, 0:8]), (K("Fd"),), (K("ii"),), 8, (K("F"),), note="f1")
+        V(lambda e: e.tensor_scalar(id_[:, 0:8], ii[:, 0:8], 15, None, OP.bitwise_and), (K("ii"),), (K("id"),), 8, note="f2")
+        V(lambda e: e.tensor_copy(ii[:, 8:16], Fa[:, 48:56]), (K("Fa"),), (K("iia"),), 8, FaK, note="f1a")
+        V(lambda e: e.tensor_scalar(id_[:, 8:16], ii[:, 8:16], 15, None, OP.bitwise_and), (K("iia"),), (K("ida"),), 8, note="f2a")
+        V(lambda e: e.tensor_scalar(T.oh[:, 8 * h + 1:8 * h + 9], id_[:, 0:8], T.icol[:, 0:1], None, OP.is_equal), (K("id"), "icol"), ("oh%d" % h,), 8, note="oh")
+        V(lambda e: e.tensor_tensor_scan(T.ex[:, 8 * h:8 * h + 8], T.oh[:, 8 * h:8 * h + 8], T.zero[:, 0:8], T.ex[:, 7:8] if h else 0.0, OP.add, OP.add),
+          ("ohz", "oh0", "zero") + (("oh1", "ex0") if h else ()), ("ex%d" % h,), 8, note="scan")
+        V(lambda e: e.tensor_tensor(B("ce")[:, :], T.oh[:, 8 * h + 1:8 * h + 9], T.ex[:, 8 * h:8 * h + 8], OP.mult), ("oh%d" % h, "ex%d" % h), (K("ce"),), 16, note="ce")
+        P(lambda e: e.matmul(F[:, 32:40], T.bo256[:, :], B("ce")[:, :], True, True), (K("ce"), "bo256"), (K("Fc"),), 64, (K("F"),), note="cnt")
+        V(lambda e: e.tensor_scalar(B("go")[:, :], id_[:, 0:8], 16.0, T.icol[:, 0:1], OP.mult, OP.add), (K("id"), "icol"), (K("go"),), 8, note="go")
+        V(lambda e: e.tensor_scalar(B("t16")[:, :], id_[:, 8:16], 0.0625, T.th16[:, 0:1], OP.mult, OP.add), (K("ida"), "th16"), (K("t16"),), 8, note="t16")
+        V(lambda e: e.tensor_tensor(B("tb")[:, :], T.cw[:, 0:256].indirect(B("go")[:, :]), bn[:, :], OP.subtract), ("cw", K("go"), "bn%d%d" % (t, h)), (K("tb"),), gat(128), note="T")
+        V(lambda e: e.tensor_tensor(B("ta")[:, :], B("t16")[:, :], F[:, 32:40], OP.add), (K("t16"), K("Fc")), (K("ta"),), 8, (K("F"),), note="ta")
+
+        def dsum(e):
+            for i in range(16):
+                o = e.matmul(S[:, 384:400], zs(T.z16, i), da[:, :, i:128:16], i == 0, i == 15)
+            return o
+        P(dsum, (K("dw"), K("aw"), "z16"), (K("Sd"),), 1024, (K("S"),), note="D")
+        V(lambda e: e.tensor_scalar(B("sg")[:, :], S[:, 384:392], 0.0, 0.5, OP.is_lt, OP.subtract), (K("Sd"),), (K("sg"),), 8, (K("S"),), note="sg")
+        V(lambda e: e.tensor_tensor(B("qa")[:, :], S[:, 392:400], B("ta")[:, :], OP.is_gt), (K("Sd"), K("ta")), (K("qa"),), 8, (K("S"),), note="qa")
+        V(lambda e: e.tensor_tensor(B("zz")[:, :], B("sg")[:, :], B("qa")[:, :], OP.mult), (K("sg"), K("qa")), (K("zz"),), 16, note="zz")
+        V(lambda e: e.tensor_tensor(B("ee")[:, :], B("zz")[:, 0:8].indirect(T.bl[:, :]), T.cmpc[:, :], OP.is_ge), (K("zz"), "bl", "cmpc", "cmpc2"), (K("ee"),), gat(256), note="ee")
+
+        def xm(e):
+            e.matmul(X[:, 0:128], T.bo[:, :], B("ee")[:, 0:128], True, False)
+            return e.matmul(X[:, 0:128], T.ident[:, :], B("ee")[:, 128:256], False, True)
+        P(xm, (K("ee"), "bo", "ident"), (K("X"),), 256, (K("X"),), note="X")
+        A(lambda e: e.activation(Y[:, 0:128], X[:, 0:128], AF.Square, bias=-1.0), (K("X"),), (K("Y"),), 128, (K("X"), K("Y")), note="M")
+        last = t == R - 1
+        b3 = T["b3%d%d" % (t, h)]
+        kb3 = "b3%d%d" % (t, h)
+        mt = B("ms")[:, :] if last else Y[:, 128:256]
+        V(lambda e: e.tensor_tensor(mt, B("tb")[:, :], Y[:, 0:128], OP.mult), (K("tb"), K("Y")), (K("ms") if last else K("MT"),), 128, (K("Y"),), note="MT")
+        V(lambda e: e.tensor_tensor(b3[:, :, :], bn[:, :], mt, OP.add), ("bn%d%d" % (t, h), K("ms") if last else K("MT")), (kb3,), 256 if last else 128, () if last else (K("Y"),), note="B")
+        if t < R - 1:
+            ls = T["ls%d%d" % (t, h)]
+            for ph in range(2):
+                V(lambda e, ph=ph: e.tensor_copy(ls[:, 64 * ph:64 * ph + 64], b3[:, :, 8 * ph:8 * ph + 8]), (kb3,), ("ls%d%d%d" % (t, h, ph),), 64, note="ls")
+            dst = T.cores[(T.rank_of(core) + HOP) % len(T.cores)]
+            rid, pid, _ = topo.addr(dst)
+            mask = 0
+            for en in topo.engines(core, dst)[::2]:
+                mask |= 1 << en
+            ne = len(topo.engines(core, dst)[::2])
+            o = add("G", lambda e: e.remote_dma(T["lt%d%d" % (t + 1, h)][:, :], ls[:, :], T.sem["al%d%d" % (t + 1, h)], T.sem["sent"], pid, rid, mask),
+                    ("ls%d%d0" % (t, h), "ls%d%d1" % (t, h)), (), (), 0.3, sem="-sent", n=ne, note="send")
+            arr = add(None, None, (), ("lt%d%d0" % (t + 1, h), "lt%d%d1" % (t + 1, h)), (), 2.0, sem="al%d%d" % (t + 1, h), n=ne)
+            ops[arr]["order"].add(o)
+            o = add("G", lambda e: e.remote_dma(T["bn%d%d" % (t + 1, h)][:, :], b3[:, :, :], T.sem["ab%d%d" % (t + 1, h)], T.sem["sent"], pid, rid, mask),
+                    (kb3,), (), (), 0.3, sem="-sent", n=ne, note="send2")
+            ops[o]["order"].add(arr - 1)
+            arr = add(None, None, (), ("bn%d%d" % (t + 1, h),), (), 2.5, sem="ab%d%d" % (t + 1, h), n=ne)
+            ops[arr]["order"].add(o)
+        else:
+            add("Y", lambda e: e.dma_start(T.yb[:, 128 * h:128 * h + 128], b3[:, :, :]), (kb3,), (), (), 2.0, sem="st%d" % h, n=16)
+        A(lambda e: e.activation(B("cp")[:, :], T.cw[:, 0:256].indirect(B("go")[:, :]), AF.Identity), ("cw", K("go")), (K("cp"),), gat(128), note="CP")
+        if not last:
+            A(lambda e: e.activation(B("ms")[:, :], Y[:, 128:256], AF.Identity), (K("MT"),), (K("ms"),), 128, (K("Y"),), note="MS")
+
+        def smat(e):
+            e.matmul(F[:, 40:48], T.bo16[:, :], T.oh[:, 8 * h + 1:8 * h + 9], True, False)
+            return e.matmul(F[:, 40:48], T.bo256[:, :], B("ce")[:, :], False, True)
+        P(smat, (K("ce"), "oh%d" % h, "bo16", "bo256"), (K("Fs"),), 128, (K("F"),), note="so_p")
+        V(lambda e: e.tensor_scalar(B("so")[:, :], F[:, 40:48], T.icol[:, 0:1], None, OP.add), (K("Fs"), "icol"), (K("so"),), 8, (K("F"),), note="so")
+        V(lambda e: e.tensor_tensor(T.cw[:, :].indirect(B("so")[:, :]), B("cp")[:, :], B("ms")[:, :], OP.subtract), (K("cp"), K("ms"), K("so")), ("cw",), ("s", 128), note="scatter")
+        V(lambda e: e.tensor_tensor(T["qr%d" % t][:, 8 * h:8 * h + 8], S[:, 392:400], B("t16")[:, :], OP.is_gt), (K("Sd"), K("t16")), ("qr%d%d" % (t, h),), 8, (K("S"),), note="qr")
+
+    for t in range(R):
+        for h in range(2):
+            k0 = len(ops)
+            half(t, h)
+            for o in ops[k0:]:
+                o["cls"] = 2 * t + h
+        if t == 1:
+            V(lambda e: e.tensor_tensor(T.qs[:, :], T.qr0[:, :], T.qr1[:, :], OP.add), ("qr00", "qr01", "qr10", "qr11"), ("qs",), 32)
+    V(lambda e: e.tensor_tensor(T.qf[:, :], T.qs[:, :], T.qr2[:, :], OP.add), ("qs", "qr20", "qr21"), ("qf",), 32)
+    add("Y", lambda e: e.dma_start(T.yq[:, :], T.qf[:, :]), ("qf",), (), (), 2.0, sem="st2", n=16)
+    add("Q", lambda e: e.dma_start(T.yc[:, :], T.cw[:, 0:256]), ("cw",), (), (), 2.0, sem="st3", n=16)
+    return ops
+
+
+def schedule(ops, tries):
+    n = len(ops)
+    c = [[{q: cost(q, o["c"], C) for q in (("A", "V") if o["q"] == "AV" else (o["q"],))} for o in ops] for C in COSTS]
+    deps = [(tuple(sorted(o["deps"])), tuple(sorted(o["order"]))) for o in ops]
+    succ, needs = [[] for _ in range(n)], [len(a) + len(b) for a, b in deps]
+    for i, (a, b) in enumerate(deps):
+        for d in a:
+            succ[d].append((i, COSTS[0]["hop"]))
+        for d in b:
+            succ[d].append((i, 0.0))
+    way = [0.0] * n
+    for i in range(n - 1, -1, -1):
+        way[i] = min(c[0][i].values()) + max([way[s] + h for s, h in succ[i]] or [0.0])
+    first = [i for i in range(n) if needs[i] == 0]
+    free_to_choose = [i for i in range(n) if ops[i]["q"] == "AV"]
+
+    def listed(shift, pick):
+        rank = [s - w for s, w in zip(shift, way)]
+        est, free, order, need, ready, c0 = [0.0] * n, dict.fromkeys("AVPGYQ", 0.0), [], needs[:], first[:], c[0]
+        while ready:
+            b0, b1, bi = 1e9, 0.0, -1
+            for i in ready:
+                q = pick[i]
+                r = est[i]
+                if q is not None and free[q] > r:
+                    r = free[q]
+                if r < b0 - 0.005 or (r < b0 + 0.005 and rank[i] < b1):
+                    b0, b1, bi = r, rank[i], i
+            q = pick[bi]
+            r = est[bi] if q is None else max(est[bi], free[q])
+            ready.remove(bi)
+            order.append(bi)
+            x = c0[bi][q]
+            if q is not None:
+                free[q] = r + (0.06 if q in "YQ" else x)
+            for s, h in succ[bi]:
+                if r + x + h > est[s]:
+                    est[s] = r + x + h
+                need[s] -= 1
+                if need[s] == 0:
+                    ready.append(s)
+        return order
+
+    def spans(order, pick):
+        out = []
+        for C, cc in zip(COSTS, c):
+            hop, done, free = C["hop"], [0.0] * n, dict.fromkeys("AVPGYQ", 0.0)
+            for i in order:
+                r = 0.0
+                a, b = deps[i]
+                for d in a:
+                    if done[d] > r:
+                        r = done[d]
+                r = r + hop if a else r
+                for d in b:
+                    if done[d] > r:
+                        r = done[d]
+                q = pick[i]
+                x = cc[i][q]
+                if q is not None:
+                    if free[q] > r:
+                        r = free[q]
+                    free[q] = r + (0.06 if q in "YQ" else x)
+                done[i] = r + x
+            out.append(max(done))
+        return out, done
+
+    rng = np.random.default_rng(SEED)
+    shift, pick = [0.0] * n, ["A" if o["q"] == "AV" else o["q"] for o in ops]
+    order = listed(shift, pick)
+    base = spans(order, pick)[0]
+    cur, best = 1.0, (1.0, order, list(pick), base)
+    for k in range(tries):
+        s2, p2 = list(shift), list(pick)
+        for i in rng.integers(0, n, int(rng.choice([1, 2, 4, 10, 25]))):
+            s2[i] = float(4 * rng.normal())
+        if rng.random() < 0.3:
+            for i in rng.choice(free_to_choose, int(rng.integers(1, 3))):
+                p2[i] = "V" if p2[i] == "A" else "A"
+        order = listed(s2, p2)
+        sp = spans(order, p2)[0]
+        f = sum(a / b for a, b in zip(sp, base)) / len(sp)
+        if f < cur + 0.0004 * (1 - k / tries) * rng.random():
+            cur, shift, pick = f, s2, p2
+            if f < best[0]:
+                best = (f, order, p2, sp)
+    _, order, pick, sp = best
+    return order, spans(order, pick)[1], pick, (base, sp)
+
+
+_CACHE = {}
+
+
+def rank_program(g, core, T, topo):
+    if T.rank_of(core) is None:
+        return
+    ops = build(core, T, topo, [g.vector])
+    if "order" not in _CACHE:
+        _CACHE["order"] = schedule(ops, TRIES)
+    order, done, pick, _ = _CACHE["order"]
+    for i, o in enumerate(ops):
+        o["q"] = pick[i]
+    eng = {"V": g.vector, "A": g.scalar, "P": g.tensor, "G": g, "Y": g.sync, "Q": g.scalar}
+    queue = {"V": "V", "A": "A", "Q": "A", "P": "P", "G": "G", "Y": "Y"}
+    total, at, clock = {}, {}, {}
+    known = {q: {} for q in ("V", "A", "P", "G", "Y")}
+    for i in order:
+        o = ops[i]
+        if o["q"] is None:
+            at[i] = (o["sem"], o["n"])
+            clock[i] = {o["sem"]: o["n"]}
+            continue
+        qn = queue[o["q"]]
+        e = eng[o["q"]]
+        kn = known[qn]
+        for d in sorted(o["deps"], key=lambda d: -done[d]):
+            s, c = at[d]
+            if kn.get(s, 0) < c:
+                e.wait_ge(T.sem[s], c)
+                for s2, c2 in clock[d].items():
+                    kn[s2] = max(kn.get(s2, 0), c2)
+        ins = o["fn"](e)
+        if o["sem"] is None:
+            s, n = o["q"], 1
+            total[s] = total.get(s, 0) + n
+            ins.then_inc(T.sem[s], n)
+        elif o["sem"] == "-sent":
+            s = "sent"
+            total[s] = total.get(s, 0) + o["n"]
+        else:
+            s, n = o["sem"], o["n"]
+            total[s] = total.get(s, 0) + n
+            ins.then_inc(T.sem[s], n)
+        at[i] = (s, total[s])
+        clock[i] = dict(kn)
+        clock[i][s] = total[s]
+    for s, c in total.items():
+        if known["G"].get(s, 0) < c:
+            g.wait_ge(T.sem[s], c)

@@ -9,77 +9,79 @@ KAP = (101, 1303, 2717, 3911)
 W = 2048
 
 SCRATCH = {
-    "xw": ("sbuf", [128, 2048], "bfloat16"),
-    "tu": ("sbuf", [128, 128], "int32"),
-    "tv": ("sbuf", [128, 128], "int32"),
-    "tf": ("sbuf", [128, 128], "float32"),
-    "tp": ("sbuf", [128, 128], "int32"),
-    "tq": ("sbuf", [128, 128], "int32"),
-    "bni": ("sbuf", [128, 16, 16], "int32"),
+    "xw": ("sbuf", [128, W], "bfloat16"),
+    "xt": ("sbuf", [128, 4 * W], "bfloat16"),
+    "tu": ("sbuf", [128, 128], "float32"),
+    "sq": ("sbuf", [128, 128], "float32"),
+    "xa": ("sbuf", [128, 4, 128], "int32"),
+    "xb": ("sbuf", [128, 4, 128], "int32"),
+    "xl": ("sbuf", [128, 4 * 128], "uint16"),
+    "bni": ("sbuf", [128, 256], "int32"),
     "cni": ("sbuf", [128, 256], "int32"),
     "wti": ("sbuf", [128, 1], "int32"),
     "thi": ("sbuf", [128, 1], "int32"),
-    "cw": ("sbuf", [128, 4096], "float32"),
     "pi": ("sbuf", [128, 8], "int32"),
     "pj": ("sbuf", [128, 8], "int32"),
-    "icol": ("sbuf", [128, 8], "float32"),
-    "wcol": ("sbuf", [128, 8], "float32"),
-    "th16": ("sbuf", [128, 8], "float32"),
+    "pf": ("sbuf", [128, 8], "float32"),
+    "col": ("sbuf", [128, 16], "float32"),
     "ones": ("sbuf", [128, 128], "bfloat16"),
     "m1": ("sbuf", [128, 128], "bfloat16"),
     "bo": ("sbuf", [128, 128], "bfloat16"),
-    "bo256": ("sbuf", [128, 128], "bfloat16"),
+    "bo64": ("sbuf", [128, 128], "bfloat16"),
+    "nbo64": ("sbuf", [128, 128], "bfloat16"),
     "bow": ("sbuf", [128, 128], "bfloat16"),
     "ident": ("sbuf", [128, 128], "bfloat16"),
     "nident": ("sbuf", [128, 128], "bfloat16"),
     "zw": ("sbuf", [128, 144], "bfloat16"),
-    "z1": ("sbuf", [128, 144], "bfloat16"),
+    "zn": ("sbuf", [128, 144], "bfloat16"),
     "z16": ("sbuf", [128, 144], "bfloat16"),
     "prow": ("sbuf", [128, 128], "float32"),
-    "cmpc": ("sbuf", [128, 256], "float32"),
-    "bli": ("sbuf", [128, 16], "int32"),
-    "bl": ("sbuf", [128, 16], "uint16"),
-    "zero": ("sbuf", [128, 8], "float32"),
-    "bo16": ("sbuf", [128, 128], "bfloat16"),
-    "oh": ("sbuf", [128, 24], "bfloat16"),
-    "ex": ("sbuf", [128, 16], "float32"),
+    "cmpc": ("sbuf", [128, 128], "float32"),
+    "diag": ("sbuf", [128, 16], "bfloat16"),
+    "cini": ("sbuf", [128, 32], "bfloat16"),
+    "tini": ("sbuf", [128, 16], "bfloat16"),
+    "bli": ("sbuf", [128, 8], "int32"),
+    "bl": ("sbuf", [128, 8], "uint16"),
+    "pmi": ("sbuf", [128, 8], "int32"),
+    "pm": ("sbuf", [128, 8], "uint16"),
+    "nn": ("sbuf", [128, 24], "bfloat16"),
+    "nd": ("sbuf", [128, 16], "bfloat16"),
+    "ns": ("sbuf", [128, 8], "float32"),
+    "sp": ("sbuf", [128, 16], "bfloat16"),
+    "inv": ("sbuf", [128, 16], "uint16"),
+    "ms": ("sbuf", [128, 272], "float32"),
     "qs": ("sbuf", [128, 16], "float32"),
     "qf": ("sbuf", [128, 16], "float32"),
 }
-SCRATCH["xt"] = ("sbuf", [128, 4 * W], "bfloat16")
-SCRATCH["xa"] = ("sbuf", [128, 512], "int32")
-SCRATCH["xb"] = ("sbuf", [128, 512], "int32")
-SCRATCH["xl"] = ("sbuf", [128, 512], "uint16")
 for _t in range(R):
     SCRATCH["qr%d" % _t] = ("sbuf", [128, 16], "float32")
+    SCRATCH["cw%d" % (_t + 1)] = ("sbuf", [128, 256], "float32")
     for _h in range(2):
         SCRATCH["lt%d%d" % (_t, _h)] = ("sbuf", [128, 128], "uint16")
-        SCRATCH["bn%d%d" % (_t, _h)] = ("sbuf", [128, 128], "float32")
-        SCRATCH["b3%d%d" % (_t, _h)] = ("sbuf", [128, 8, 16], "float32")
+        SCRATCH["b3%d%d" % (_t, _h)] = ("sbuf", [128, 128], "float32")
+        if _t > 0:
+            SCRATCH["bn%d%d" % (_t, _h)] = ("sbuf", [128, 128], "float32")
         if _t < R - 1:
             SCRATCH["ls%d%d" % (_t, _h)] = ("sbuf", [128, 128], "uint16")
 for _h in range(2):
     for _n, _s, _d in (("fa", [128, 1024], "bfloat16"), ("dc", [128, 1024], "bfloat16"), ("ac", [128, 1024], "bfloat16"),
-                       ("ar", [128, 2, 8, 64], "bfloat16"), ("i1", [128, 128], "int32"),
-                       ("j0", [128, 16, 8], "int32"), ("j1", [128, 16, 4], "int32"), ("j2", [128, 16, 2], "int32"), ("j3", [128, 2, 8], "int32"),
-                       ("la", [128, 64], "uint16"), ("lb", [128, 64], "uint16"),
-                       ("wc", [128, 128], "bfloat16"), ("da", [128, 2, 128], "bfloat16"),
-                       ("ii", [128, 16], "int32"), ("id", [128, 16], "int32"), ("ce", [128, 8], "bfloat16"),
-                       ("go", [128, 8], "uint16"), ("so", [128, 8], "uint16"),
-                       ("tb", [128, 128], "float32"), ("cp", [128, 128], "float32"), ("ms", [128, 128], "float32"),
-                       ("t16", [128, 8], "float32"), ("ta", [128, 8], "float32"), ("qa", [128, 8], "float32"), ("sg", [128, 8], "float32"),
+                       ("ar", [128, 2, 512], "bfloat16"), ("ia", [128, 128], "int32"), ("ib", [128, 128], "int32"), ("lu", [128, 128], "uint16"),
+                       ("wd", [128, 3, 128], "bfloat16"), ("qi", [128, 32], "int32"), ("fr", [128, 32], "float32"),
+                       ("go", [128, 8], "uint16"), ("sn", [128, 8], "bfloat16"), ("tb", [128, 128], "float32"),
                        ("zz", [128, 8], "float32"), ("ee", [128, 256], "bfloat16")):
         SCRATCH["%s_%d" % (_n, _h)] = ("sbuf", _s, _d)
-    for _n in ("S", "F", "X", "Y"):
+    for _n in ("S", "F"):
         SCRATCH["%s_%d" % (_n, _h)] = ("psum", [128, 512], "float32")
+    for _n in ("X", "Y"):
+        SCRATCH["%s_%d" % (_n, _h)] = ("psum", [128, 8, 64], "float32")
 
 DMAS = ["ld%d" % _k for _k in range(8)] + ["st%d" % _k for _k in range(4)]
 SEMAPHORES = ["V", "A", "P", "G", "sent"] + DMAS + ["%s%d%d" % (_a, _t, _h) for _a in ("al", "ab") for _t in (1, 2) for _h in (0, 1)]
 
-COSTS = ({"cy": 0.00083, "V": 0.03, "A": 0.05, "P": 0.0005, "g": 1.5, "s": 3.8, "hop": 0.09},
-         {"cy": 0.00083, "V": 0.05, "A": 0.065, "P": 0.00075, "g": 1.5, "s": 3.8, "hop": 0.07},
-         {"cy": 0.00083, "V": 0.02, "A": 0.03, "P": 0.00042, "g": 1.3, "s": 3.0, "hop": 0.12},
-         {"cy": 0.00083, "V": 0.03, "A": 0.04, "P": 0.0005, "g": 1.9, "s": 5.0, "hop": 0.07})
+COSTS = ({"cy": 0.00083, "V": 0.03, "A": 0.05, "P": 0.0005, "g": 1.5, "hop": 0.09},
+         {"cy": 0.00083, "V": 0.05, "A": 0.065, "P": 0.00075, "g": 1.5, "hop": 0.07},
+         {"cy": 0.00083, "V": 0.02, "A": 0.03, "P": 0.00042, "g": 1.3, "hop": 0.12},
+         {"cy": 0.00083, "V": 0.03, "A": 0.04, "P": 0.0005, "g": 1.9, "hop": 0.07})
 
 
 def cost(q, n, c):
@@ -88,13 +90,17 @@ def cost(q, n, c):
     if q == "P":
         return n * c["P"]
     if isinstance(n, tuple):
+        if n[0] == "h":
+            return c[q] + max(64, n[1] if q == "A" else n[1] // 2) * c["cy"]
         return (0.065 if q == "A" else 0.05) + n[1] * c[n[0]] * c["cy"]
     return c[q] + max(64, n) * c["cy"]
 
 
-CH = (2, 4, 2, 1)
-SPLIT = (0,)
-SEED, TRIES = 11, 12000
+CH = (2, 2, 1, 1)
+RELU = ()
+BPS = True
+PERIOD, LAG, STRETCH = 20.0, 6.0, 1.15
+SEED, TRIES = 1, 12000
 
 
 def build(core, T, topo, VEC):
@@ -123,7 +129,7 @@ def build(core, T, topo, VEC):
         for b in bk:
             banks.setdefault(b, {})[q] = me
         deps.discard(me)
-        ops.append({"cls": 0, "q": q, "fn": fn, "deps": deps, "order": order - deps, "c": c, "sem": sem, "n": n, "note": note})
+        ops.append({"q": q, "fn": fn, "deps": deps, "order": order - deps, "c": c, "sem": sem, "n": n, "note": note})
         return me
 
     def V(fn, rd, wr, n, bk=(), note=""):
@@ -139,7 +145,7 @@ def build(core, T, topo, VEC):
         return add("G", fn, rd, wr, (), c, note=note)
 
     def load(q, k, out, in_, wr, c):
-        add(q, lambda e: e.dma_start(out, in_), (), wr, (), c, sem="ld%d" % k, n=16, note="load")
+        return add(q, lambda e: e.dma_start(out, in_), (), wr, (), c, sem="ld%d" % k, n=16, note="load")
 
     gat = lambda n: ("g", n)
 
@@ -148,217 +154,241 @@ def build(core, T, topo, VEC):
             return e.tensor_copy(out, ind)
         return e.activation(out, ind, AF.Identity)
 
-    def either(fn, rd, wr, n, note):
+    def scale_on(e, out, in_, s):
+        if e is VEC[0]:
+            return e.tensor_scalar(out, in_, s, None, OP.mult)
+        return e.activation(out, in_, AF.Identity, scale=s)
+
+    def relu_on(e, out, in_):
+        if e is VEC[0]:
+            return e.tensor_scalar(out, in_, 0.0, 2.0, OP.max, OP.mult)
+        return e.activation(out, in_, AF.Relu, scale=2.0)
+
+    def either(fn, rd, wr, n, note=""):
         add("AV", fn, rd, wr, (), n, note=note)
 
-    load("Y", 0, T.bni[:, :, :], T.bn[:, :], ("bni",), 2.2)
-    load("Q", 1, T.xw[:, 0:W], T.xf[:, :], ("xw",), 4.0)
-    load("Y", 2, T.wti[:, :], T.wt[:, :], ("wti",), 2.5)
-    load("Y", 3, T.thi[:, :], T.th[:, :], ("thi",), 2.5)
-    load("Q", 5, T.cni[:, :], T.cn[:, :], ("cni",), 6.0)
+    prev = load("Y", 0, T.bni[:, 0:128], T.bn[:, 0:128], ("bn00",), 2.2)
+    load("Q", 1, T.xw[:, :], T.xf[:, :], ("xw",), 4.0)
+    for k, out, in_, key, c in ((2, T.wti[:, :], T.wt[:, :], "wti", 4.2), (4, T.bni[:, 128:256], T.bn[:, 128:256], "bn01", 4.5),
+                                (3, T.thi[:, :], T.th[:, :], "thi", 4.7), (5, T.cni[:, :], T.cn[:, :], "cw0", 5.2)):
+        o = load("Y", k, out, in_, (key,), c)
+        ops[o]["after"] = prev
+        prev = o
 
+    col = lambda k: T.col[:, k:k + 1]
+    ICOL, SQB, PMC, PM2, WCOL, W16, THC, I16, GOC, INVC = range(10)
     G(lambda e: e.iota(T.pi[:, 0:1], [[0, 1]], 0, 1), (), ("pi",), 0.2)
-    G(lambda e: e.iota(T.tu[:, :], [[16, 128]], 0, 1), (), ("tu",), 0.34)
-    G(lambda e: e.iota(T.bli[:, :], [[0, 2], [1, 8]], 0, 0), (), ("bli",), 0.2)
-    G(lambda e: e.iota(T.prow[:, :], [[0, 8], [1, 16]], 0, 0, allow_small_or_imprecise_dtypes=True), (), ("prow",), 0.4)
-    V(lambda e: e.memset(T.ones[:, :], 1.0), (), ("ones",), 128)
+    G(lambda e: e.iota(T.pf[:, 0:1], [[0, 1]], -592, 1, allow_small_or_imprecise_dtypes=True), (), ("pf",), 0.2)
+    G(lambda e: e.iota(T.pmi[:, :], [[2, 8]], 0, 0), (), ("pmi",), 0.2)
+    G(lambda e: e.iota(T.tu[:, :], [[16, 128]], 0, 1, allow_small_or_imprecise_dtypes=True), (), ("tu",), 0.34)
+    V(lambda e: e.memset(T.ones[:, :], 1.0), (), ("ones",), 64)
     G(lambda e: e.affine_select(T.ident[:, :], T.ones[:, :], [[-1, 128]], OP.is_equal, 0.0, 0, 1), ("ones",), ("ident",), 0.4)
     G(lambda e: e.affine_select(T.m1[:, :], T.ones[:, :], [[-16, 8], [0, 16]], OP.is_ge, 0.0, 0, 1), ("ones",), ("m1",), 0.4)
     G(lambda e: e.affine_select(T.bo[:, :], T.m1[:, :], [[16, 8], [0, 16]], OP.is_ge, 0.0, 15, -1), ("m1",), ("bo",), 0.4)
-    V(lambda e: e.memset(T.zw[:, :], 0.0), (), ("zw",), 144)
-    V(lambda e: e.memset(T.z1[:, :], 0.0), (), ("z1",), 144)
-    V(lambda e: e.memset(T.z16[:, :], 0.0), (), ("z16",), 144)
-    V(lambda e: e.memset(T.zero[:, :], 0.0), (), ("zero",), 8)
-    V(lambda e: e.memset(T.oh[:, 0:1], 0.0), (), ("ohz",), 8)
-
-    def lists_in(h):
-        for ph in range(2):
-            V(lambda e, ph=ph: e.tensor_copy(T["lt0%d" % h][:, 64 * ph:64 * ph + 64], T.bni[:, 8 * h:8 * h + 8, 8 * ph:8 * ph + 8]),
-              ("bni",), ("lt0%d%d" % (h, ph),), 64)
-
-    def charts_in(h):
-        V(lambda e: e.tensor_copy(T["bn0%d" % h][:, :], T.bni[:, 8 * h:8 * h + 8, :]), ("bni",), ("bn0%d" % h,), 128)
-    lists_in(0)
+    G(lambda e: e.iota(T.bli[:, :], [[1, 8]], 0, 0), (), ("bli",), 0.2)
+    G(lambda e: e.iota(T.prow[:, :], [[0, 8], [16, 16]], 4, 0, allow_small_or_imprecise_dtypes=True), (), ("prow",), 0.4)
+    V(lambda e: e.memset(T.zw[:, :], 0.0), (), ("zw",), 72)
+    V(lambda e: e.memset(T.z16[:, :], 0.0), (), ("z16",), 72)
     V(lambda e: e.tensor_scalar(T.pj[:, 0:1], T.pi[:, 0:1], 15, None, OP.bitwise_and), ("pi",), ("pj",), 8)
-    V(lambda e: e.tensor_copy(T.icol[:, 0:1], T.pj[:, 0:1]), ("pj",), ("icol",), 8)
-    V(lambda e: e.tensor_tensor(T.wcol[:, 4:5], T.pi[:, 0:1], T.icol[:, 0:1], OP.subtract), ("pi", "icol"), ("p16",), 8)
-    V(lambda e: e.tensor_scalar(T.tv[:, :], T.tu[:, :], T.wcol[:, 4:5], None, OP.subtract), ("tu", "p16"), ("tv",), 128)
-    V(lambda e: e.tensor_scalar(T.tf[:, :], T.tv[:, :], 1184.0, None, OP.add), ("tv",), ("tf",), 128)
-    V(lambda e: e.tensor_tensor(T.tp[:, :], T.tv[:, :], T.tf[:, :], OP.mult), ("tv", "tf"), ("tp",), 256)
-    V(lambda e: e.tensor_scalar(T.tq[:, :], T.tp[:, :], 5, W - 1, OP.arith_shift_right, OP.bitwise_and), ("tp",), ("tq",), 128)
+    V(lambda e: e.tensor_copy(col(ICOL), T.pj[:, 0:1]), ("pj",), ("icol",), 8)
+    V(lambda e: e.tensor_scalar(col(PM2), col(ICOL), 8.0, -127.0, OP.is_ge, OP.mult), ("icol",), ("pm2",), 8)
+    V(lambda e: e.tensor_scalar(col(PMC), col(ICOL), 16.0, col(PM2), OP.mult, OP.add), ("icol", "pm2"), ("pmc",), 8)
+    V(lambda e: e.tensor_scalar(T.pm[:, :], T.pmi[:, :], col(PMC), None, OP.add), ("pmi", "pmc"), ("pm",), 8)
+    for h in range(2):
+        V(lambda e, h=h: e.tensor_copy(T["lt0%d" % h][:, :], T.bni[:, 128 * h:128 * h + 128].indirect(T.pm[:, :])), ("bn0%d" % h, "pm"), ("lt0%d" % h,), gat(128))
+    V(lambda e: e.tensor_scalar(col(SQB), col(ICOL), T.pf[:, 0:1], None, OP.subtract), ("icol", "pf"), ("sqb",), 8)
+    A(lambda e: e.activation(T.sq[:, :], T.tu[:, :], AF.Square, bias=col(SQB)), ("tu", "sqb"), ("sq",), 128)
     for l in range(4):
-        ls_ = slice(128 * l, 128 * l + 128)
-        V(lambda e, l=l, s=ls_: e.tensor_scalar(T.xa[:, s], T.tq[:, :], float(KAP[l] % W), None, OP.add), ("tq",), ("xa%d" % l,), 128)
-        V(lambda e, l=l, s=ls_: e.tensor_scalar(T.xb[:, s], T.xa[:, s], W - 1, None, OP.bitwise_and), ("xa%d" % l,), ("xb%d" % l,), 128)
-        V(lambda e, l=l, s=ls_: e.tensor_copy(T.xl[:, s], T.xb[:, s]), ("xb%d" % l,), ("xl%d" % l,), 128)
+        V(lambda e, l=l: e.tensor_scalar(T.xa[:, l, :], T.sq[:, :], float((32 * KAP[l] - 592 * 592) % 65536), None, OP.add), ("sq",), ("xa%d" % l,), 128)
+        V(lambda e, l=l: e.tensor_scalar(T.xb[:, l, :], T.xa[:, l, :], 5, W - 1, OP.arith_shift_right, OP.bitwise_and), ("xa%d" % l,), ("xb%d" % l,), 128)
+        V(lambda e, l=l: e.tensor_copy(T.xl[:, 128 * l:128 * l + 128], T.xb[:, l, :]), ("xb%d" % l,), ("xl%d" % l,), 128)
         for c in range(4):
-            either(lambda e, l=l, c=c: gather_on(e, T.xt[:, W * l + 512 * c:W * l + 512 * c + 512], T.xw[:, :].indirect(T.xl[:, 128 * l + 32 * c:128 * l + 32 * c + 32])),
-                   ("xw", "xl%d" % l), ("x%d%d" % (l, c),), gat(512), "table")
-    V(lambda e: e.tensor_scalar(T.nident[:, :], T.ident[:, :], -1.0, None, OP.mult), ("ident",), ("nident",), 64)
-    V(lambda e: e.tensor_copy(T.wcol[:, 0:1], T.wti[:, :]), ("wti",), ("wcol",), 8)
-    V(lambda e: e.tensor_scalar(T.zw[:, 15:128:16], T.bo[:, 0:128:16], T.wcol[:, 0:1], None, OP.mult), ("bo", "wcol"), ("zw",), 8)
-    lists_in(1)
-    V(lambda e: e.tensor_scalar(T.th16[:, 0:1], T.thi[:, :], 0.0625, None, OP.mult), ("thi",), ("th16",), 8)
+            k0, k1 = 32 * c, 32 * c + 32
+            either(lambda e, l=l, k0=k0, k1=k1: gather_on(e, T.xt[:, W * l + 16 * k0:W * l + 16 * k1], T.xw[:, :].indirect(T.xl[:, 128 * l + k0:128 * l + k1])),
+                   ("xw", "xl%d" % l), ("x%d%d" % (l, c),), gat(16 * (k1 - k0)), "table")
+    either(lambda e: scale_on(e, T.nident[:, :], T.ident[:, :], -1.0), ("ident",), ("nident",), 128)
+    V(lambda e: e.tensor_copy(col(WCOL), T.wti[:, :]), ("wti",), ("wcol",), 8)
+    either(lambda e: scale_on(e, T.zw[:, 15:128:16], T.bo[:, 0:128:16], col(WCOL)), ("bo", "wcol"), ("zw",), 8)
+    if RELU:
+        either(lambda e: scale_on(e, T.zn[:, :], T.zw[:, :], -1.0), ("zw",), ("zn",), ("h", 144))
+    V(lambda e: e.tensor_scalar(col(THC), T.thi[:, :], -0.0625, -15.0 / 32, OP.mult, OP.add), ("thi",), ("thc",), 8)
+    either(lambda e: scale_on(e, T.tini[:, 0:8], T.ones[:, 0:8], col(THC)), ("ones", "thc"), ("tini0",), 8)
+    V(lambda e: e.tensor_scalar(T.tini[:, 8:16], T.tini[:, 0:8], -1.0, col(THC), OP.mult, OP.add), ("tini0", "thc"), ("tini1",), 8)
     V(lambda e: e.tensor_copy(T.bl[:, :], T.bli[:, :]), ("bli",), ("bl",), 16)
-    V(lambda e: e.tensor_copy(T.z1[:, 15:128:16], T.bo[:, 0:128:16]), ("bo",), ("z1",), 8)
-    V(lambda e: e.tensor_scalar(T.z16[:, 15:128:16], T.bo[:, 0:128:16], 0.0625, None, OP.mult), ("bo",), ("z16",), 8)
-    V(lambda e: e.tensor_scalar(T.bow[:, :], T.bo[:, :], T.wcol[:, 0:1], None, OP.mult), ("bo", "wcol"), ("bow",), 64)
-    V(lambda e: e.tensor_scalar(T.bo256[:, :], T.bo[:, :], 256.0, None, OP.mult), ("bo",), ("bo256",), 64)
-    V(lambda e: e.tensor_scalar(T.bo16[:, :], T.bo[:, :], T.icol[:, 0:1], 16.0, OP.mult, OP.mult), ("bo", "icol"), ("bo16",), 64)
-    V(lambda e: e.memset(T.cmpc[:, 128:256], -0.25), (), ("cmpc",), 128)
-    V(lambda e: e.tensor_scalar(T.cmpc[:, 0:128], T.prow[:, :], T.icol[:, 0:1], 0.25, OP.not_equal, OP.add), ("prow", "icol"), ("cmpc2",), 128)
-    charts_in(0)
-    charts_in(1)
-    V(lambda e: e.tensor_copy(T.cw[:, 0:256], T.cni[:, :]), ("cni",), ("cw",), 256)
+    either(lambda e: scale_on(e, T.z16[:, 15:128:16], T.bo[:, 0:128:16], 0.0625), ("bo",), ("z16",), 8)
+    V(lambda e: e.tensor_scalar(T.bow[:, :], T.bo[:, :], col(WCOL), 0.0625, OP.mult, OP.mult), ("bo", "wcol"), ("bow",), 64)
+    either(lambda e: scale_on(e, T.bo64[:, :], T.bo[:, :], 64.0), ("bo",), ("bo64",), 128)
+    either(lambda e: scale_on(e, T.nbo64[:, :], T.bo[:, :], -64.0), ("bo",), ("nbo64",), 128)
+    either(lambda e: scale_on(e, col(I16), col(ICOL), 16.0), ("icol",), ("i16",), 8)
+    V(lambda e: e.tensor_scalar(T.cmpc[:, :], T.prow[:, :], col(I16), None, OP.subtract), ("prow", "i16"), ("cmpc",), 128)
+    V(lambda e: e.tensor_scalar(T.diag[:, :], T.cmpc[:, 0:16], 4.0, 4.0, OP.is_equal, OP.mult), ("cmpc",), ("diag",), 16)
+    V(lambda e: e.memset(T.cini[:, 8:24], -15.0 / 32), (), ("cini1",), 8)
+    V(lambda e: e.memset(T.cini[:, 24:32], 1.0 / 32), (), ("cini2",), 8)
+    V(lambda e: e.tensor_scalar(col(W16), col(ICOL), -0.0625, -15.0 / 32, OP.mult, OP.add), ("icol",), ("w16",), 8)
+    either(lambda e: scale_on(e, T.cini[:, 0:8], T.ones[:, 0:8], col(W16)), ("ones", "w16"), ("cini0",), 8)
+    V(lambda e: e.tensor_scalar(col(GOC), col(ICOL), 120.0, None, OP.add), ("icol",), ("goc",), 8)
+    V(lambda e: e.tensor_scalar(col(INVC), col(ICOL), 1920.0, None, OP.add), ("icol",), ("invc",), 8)
+    V(lambda e: e.memset(T.nn[:, 0:1], -13.0 / 32), (), ("nn",), 8)
+    V(lambda e: e.memset(T.ms[:, 256:272], 0.0), (), ("msz",), 16)
+    for h in range(2):
+        V(lambda e, h=h: e.memset(T["qi_%d" % h][:, 24:32], 0), (), ("qiz_%d" % h,), 8)
 
     def half(t, h):
         B = lambda n: T["%s_%d" % (n, h)]
         K = lambda n: "%s_%d" % (n, h)
         S, F, X, Y = B("S"), B("F"), B("X"), B("Y")
-        lt, bn = T["lt%d%d" % (t, h)], T["bn%d%d" % (t, h)]
-        win = T.xw[:, 0:W]
-        fa, dc, ac, ar = B("fa"), B("dc"), B("ac"), B("ar")
+        lt = T["lt%d%d" % (t, h)]
+        bn = T["bn%d%d" % (t, h)][:, :] if t else T.bni[:, 128 * h:128 * h + 128]
+        kbn = "bn%d%d" % (t, h)
+        cw = T["cw%d" % t] if t else T.cni
+        fa, dc, ac, ar, lu = B("fa"), B("dc"), B("ac"), B("ar"), B("lu")
         zs = lambda z, i: z[:, 15 - i:143 - i]
 
-        def of(keys, c, ch):
-            return keys if ch == 1 or len(keys) == 1 else (keys[2 * c // ch],)
+        units = lambda name, x0, m: tuple(K("%s%d" % (name, u)) for u in range(x0 // 128, (x0 + m) // 128))
 
-        def gather_pair(la, lb, ka, kb, n, w, wk, ch):
-            m = n // ch
-            for c in range(ch):
-                either(lambda e, c=c: gather_on(e, fa[:, m * c:m * c + m], w.indirect(la[:, m * c // 16:(m * c + m) // 16])),
-                       of(ka, c, ch) + wk, (K("fa%d" % c),), gat(m), "gA")
-            for c in range(ch):
-                V(lambda e, c=c: e.tensor_tensor(dc[:, m * c:m * c + m], w.indirect(lb[:, m * c // 16:(m * c + m) // 16]), fa[:, m * c:m * c + m], OP.subtract),
-                  of(kb, c, ch) + wk + (K("fa%d" % c),), (K("dc%d" % c),), gat(m), note="gB")
-            for c in range(ch):
-                A(lambda e, c=c: e.activation(ac[:, m * c:m * c + m], dc[:, m * c:m * c + m], AF.Abs), (K("dc%d" % c),), (K("ac%d" % c),), m, note="abs")
-            return tuple(K("fa%d" % c) for c in range(ch)), tuple(K("dc%d" % c) for c in range(ch)), tuple(K("ac%d" % c) for c in range(ch))
+        def gather_pair(l, pieces, w, wk):
+            for la, lb, k, x0, m in pieces:
+                either(lambda e, la=la, x0=x0, m=m: gather_on(e, fa[:, x0:x0 + m], w.indirect(la)), (k,) + wk, units("fa", x0, m), gat(m), "gA")
+            for la, lb, k, x0, m in pieces:
+                V(lambda e, lb=lb, x0=x0, m=m: e.tensor_tensor(dc[:, x0:x0 + m], w.indirect(lb), fa[:, x0:x0 + m], OP.subtract),
+                  (k,) + wk + units("fa", x0, m), units("dc", x0, m), gat(m), note="gB")
+            for la, lb, k, x0, m in pieces:
+                if l in RELU:
+                    either(lambda e, x0=x0, m=m: relu_on(e, ac[:, x0:x0 + m], dc[:, x0:x0 + m]), units("dc", x0, m), units("ac", x0, m), ("h", m), "relu")
+                else:
+                    A(lambda e, x0=x0, m=m: e.activation(ac[:, x0:x0 + m], dc[:, x0:x0 + m], AF.Abs), units("dc", x0, m), units("ac", x0, m), m, note="abs")
 
-        def weigh(l, n, keys):
-            for s, (c0, c1) in parts(l, n):
-                out = psum_of(s, c1 - c0)
+        def pieces(lst, c0, key, x0, n, ch):
+            m, k = n // ch, n // ch // 16
+            return [(lst[:, c0 + k * c:c0 + k * c + k], lst[:, c0 + n // 16 + k * c:c0 + n // 16 + k * c + k], key, x0 + m * c, m) for c in range(ch)]
 
-                def fn(e, out=out, c0=c0, c1=c1):
+        def weigh(l, n):
+            def part(z, src, first, last):
+                def fn(e):
                     for i in range(16):
-                        o = e.matmul(out, zs(T.zw, i), ac[:, 16 * c0 + i:16 * c1:16], i == 0, i == 15)
+                        o = e.matmul(S[:, 0:n // 16], zs(z, i), src[:, i:n:16], first and i == 0, last and i == 15)
                     return o
-                ch = len(keys)
-                ks = keys if ch == 1 or len(parts(l, n)) == 1 else keys[s * ch // 2:(s + 1) * ch // 2]
-                P(fn, ks + ("zw",), (K("S%d" % s),), 16 * max(64, c1 - c0), (K("S"),) if s == 0 else (K("F"),), note="weigh")
+                return fn
+            if l in RELU:
+                P(part(T.zn, dc, True, False), units("dc", 0, n) + ("zn",), (K("S0"),), 1024, (K("S"),), note="weighd")
+            P(part(T.zw, ac, l not in RELU, True), units("ac", 0, n) + ("zw",), (K("S0"),), 1024, (K("S"),), note="weigh")
 
-        def parts(l, n):
-            return ((0, (0, n // 2)), (1, (n // 2, n))) if l in SPLIT else ((0, (0, n)),)
+        def index(src, ks, bank, c0, n, wr):
+            ka, kb = K("ia%d" % (c0 // 64)), K("ib%d" % (c0 // 64))
+            V(lambda e: e.tensor_copy(B("ia")[:, c0:c0 + n], src), (ks,), (ka,), n, bank, note="i1")
+            V(lambda e: e.tensor_scalar(B("ib")[:, c0:c0 + n], B("ia")[:, c0:c0 + n], W - 1, None, OP.bitwise_and), (ka,), (kb,), n, note="i2")
+            V(lambda e: e.tensor_copy(lu[:, c0:c0 + n], B("ib")[:, c0:c0 + n]), (kb,), wr, n, note="i3")
 
-        def psum_of(s, n):
-            return S[:, 0:n] if s == 0 else F[:, 256:256 + n]
+        table = lambda l: (T.xt[:, W * l:W * l + W], tuple("x%d%d" % (l, c) for c in range(4)))
 
-        def index(l, n):
-            i1, j, m = B("i1"), B("j%d" % l), n // 16
-            for s, (c0, c1) in parts(l, n):
-                bank = (K("S"),) if s == 0 else (K("F"),)
-                src = psum_of(s, c1 - c0)
-                ks = (K("S%d" % s),)
-                V(lambda e, src=src, c0=c0, c1=c1: e.tensor_copy(i1[:, c0:c1], src), ks, (K("i1%d" % s),), c1 - c0, bank, note="i1")
-                rows_ = slice(c0 // m, c1 // m) if l < 3 else slice(c0 // 8, c1 // 8)
-                V(lambda e, c0=c0, c1=c1, rows_=rows_: e.tensor_scalar(j[:, rows_, :], i1[:, c0:c1], W - 1, None, OP.bitwise_and),
-                  (K("i1%d" % s),), (K("j%d" % s),), c1 - c0, note="i2")
-                for x, name in enumerate(("la", "lb")):
-                    if l == 3 and len(parts(l, n)) == 2 and x != s:
-                        continue
-                    wr = tuple(K("%s%d" % (name, y)) for y in ((0, 1) if l == 3 or len(parts(l, n)) == 1 else (s,)))
-                    if l < 3:
-                        V(lambda e, c0=c0, c1=c1, x=x, name=name, rows_=rows_: e.tensor_copy(B(name)[:, c0 // 2:c1 // 2], j[:, rows_, x * (m // 2):(x + 1) * (m // 2)]),
-                          (K("j%d" % s),), wr, (c1 - c0) // 2, note="i6")
-                    else:
-                        V(lambda e, x=x, name=name: e.tensor_copy(B(name)[:, 0:8], j[:, x, :]), (K("j%d" % s),), wr, 8, note="i6")
-            return T.xt[:, W * l:W * l + W], tuple("x%d%d" % (l, c) for c in range(4))
+        gather_pair(0, pieces(lt, 0, "lt%d%d" % (t, h), 0, 1024, CH[0]), T.xw[:, :], ("xw",))
 
-        fk, dk, ak = gather_pair(lt[:, 0:64], lt[:, 64:128], ("lt%d%d0" % (t, h),), ("lt%d%d1" % (t, h),), 1024, win, ("xw",), CH[0])
-
-        def rows(bank, srcs):
+        def rows(bank, src, first, last):
             def fn(e):
                 for c in range(8):
-                    lst = [(T.ident, s[:, c:1024:16]) for s in srcs] + [(T.nident, s[:, c + 8:1024:16]) for s in srcs]
-                    for i, (w, r) in enumerate(lst):
-                        o = e.matmul(bank[:, c:512:8], w[:, :], r, i == 0, i == len(lst) - 1)
+                    e.matmul(bank[:, :, 8 * c:8 * c + 8], T.ident[:, :], src[:, c:1024:16], first and c == 0, False)
+                    o = e.matmul(bank[:, :, 8 * c:8 * c + 8], T.nident[:, :], src[:, c + 8:1024:16], False, last and c == 7)
                 return o
             return fn
-        P(rows(X, (fa,)), fk + ("ident", "nident"), (K("X"),), 1024, (K("X"),), note="row0")
-        P(rows(Y, (fa, dc)), fk + dk + ("ident", "nident"), (K("Y"),), 2048, (K("Y"),), note="row1")
+        fk, dk = units("fa", 0, 1024), units("dc", 0, 1024)
+        P(rows(X, fa, True, True), fk + ("ident", "nident"), (K("X"),), 1024, (K("X"),), note="row0")
+        P(rows(Y, fa, True, False), fk + ("ident", "nident"), (K("Y"),), 1024, (K("Y"),), note="row1")
+        P(rows(Y, dc, False, True), dk + ("ident", "nident"), (K("Y"),), 1024, (K("Y"),), note="row2")
         for ph, (bank, kk) in enumerate(((X, K("X")), (Y, K("Y")))):
-            A(lambda e, ph=ph, bank=bank: e.activation(ar[:, ph, :, :], bank[:, :], AF.Abs), (kk,), (K("ar%d" % ph),), 512, (kk,), note="absr")
-        sep = 0 in SPLIT
-        kr, br = (K("S1"), (K("F"),)) if sep else (K("S0"), (K("S"),))
-
-        def wcol(e):
-            for i in range(16):
-                o = e.matmul(S[:, 0:64], zs(T.zw, i), ac[:, i:1024:16], i == 0, i == 15)
-            return o
-        P(wcol, ak + ("zw",), (K("S0"),), 1024, (K("S"),), note="weigh")
-
-        def wrow(e):
-            for ph in range(2):
+            A(lambda e, ph=ph, bank=bank: e.activation(ar[:, ph, :], bank[:, :, :], AF.Abs), (kk,), (K("ar%d" % ph),), 512, (kk,), note="absr")
+        weigh(0, 1024)
+        for ph in range(2):
+            def wrow(e, ph=ph):
                 for pl in range(8):
-                    o = e.matmul(psum_of(1, 64) if sep else S[:, 64:128], zs(T.zw, 8 * ph + pl), ar[:, ph, :, 8 * pl:8 * pl + 8], ph + pl == 0, 8 * ph + pl == 15)
-            return o
-        P(wrow, ("zw", K("ar0"), K("ar1")), (kr,), 1024, br, note="weighr")
-        w, wk = index(0, 128)
-        for l, n in ((1, 1024), (2, 512), (3, 256)):
-            fk, dk, ak = gather_pair(B("la"), B("lb"), (K("la0"), K("la1")), (K("lb0"), K("lb1")), n, w, wk, CH[l])
-            weigh(l, n // 16, ak)
-            w, wk = index(l, n // 16)
-        wc, da, ii, id_ = B("wc"), B("da"), B("ii"), B("id")
-        Fa, FaK = B("Y"), (K("Y"),)
-        A(lambda e: e.activation(wc[:, :], w.indirect(B("la")[:, 0:8]), AF.Identity), wk + (K("la0"),), (K("wc"),), gat(128), note="gWC")
-        V(lambda e: e.tensor_tensor(da[:, 0, :], w.indirect(B("lb")[:, 0:8]), wc[:, :], OP.subtract), wk + (K("lb0"), K("wc")), (K("dw"),), gat(128), note="gWR")
-        A(lambda e: e.activation(da[:, 1, :], da[:, 0, :], AF.Abs), (K("dw"),), (K("aw"),), 128, note="absW")
-        P(lambda e: e.matmul(F[:, 0:8], T.bow[:, :], wc[:, 0:128:16], True, True), (K("wc"), "bow"), (K("Fd"),), 64, (K("F"),), note="donor")
+                    o = e.matmul(F[:, 256:320], zs(T.zw, 8 * ph + pl), ar[:, ph, 64 * pl:64 * pl + 64], ph + pl == 0, 8 * ph + pl == 15)
+                return o
+            P(wrow, ("zw", K("ar%d" % ph)), (K("S1"),), 512, (K("F"),), note="weighr")
+        index(S[:, 0:64], K("S0"), (K("S"),), 0, 64, (K("lu0"),))
+        index(F[:, 256:320], K("S1"), (K("F"),), 64, 64, (K("lu1"),))
+
+        Z, D = F[:, 0:32], Y[:, 7, 0:8]
+        P(lambda e: e.matmul(Z, T.ident[:, :], T.cini[:, :], True, False), ("ident", "cini0", "cini1", "cini2"), (K("Z"),), 64, (K("F"),), note="zini")
+
+        def dini(e):
+            e.matmul(D, T.ident[:, :], T.tini[:, 0:8], True, False)
+            return e.matmul(D, T.ident[:, :], T.tini[:, 8:16], False, False)
+        P(dini, ("ident", "tini0", "tini1"), (K("D"),), 128, (K("Y"),), note="dini")
+
+        for l, n in ((1, 512), (2, 256), (3, 128)):
+            gather_pair(l, [p for s in range(2) for p in pieces(lu, n // 8 * s, K("lu%d" % (s if l == 1 else 0)), n * s, n, CH[l])], *table(l - 1))
+            weigh(l, 2 * n)
+            index(S[:, 0:n // 8], K("S0"), (K("S"),), 0, n // 8, (K("lu0"),))
+
+        w, wk = table(3)
+        wd, qi, fr, nn = B("wd"), B("qi"), B("fr"), T.nn
+        either(lambda e: gather_on(e, wd[:, 0, :], w.indirect(lu[:, 0:8])), wk + (K("lu0"),), (K("wc"),), gat(128), "gWC")
+        V(lambda e: e.tensor_tensor(wd[:, 1, :], w.indirect(lu[:, 8:16]), wd[:, 0, :], OP.subtract), wk + (K("lu0"), K("wc")), (K("dw"),), gat(128), note="gWR")
+        A(lambda e: e.activation(wd[:, 2, :], wd[:, 1, :], AF.Abs), (K("dw"),), (K("aw"),), 128, note="absW")
+
+        def donor(e):
+            e.matmul(F[:, 0:8], T.bow[:, :], wd[:, 0, 0:128:16], False, False)
+            return e.matmul(F[:, 8:16], T.bow[:, :], wd[:, 0, 0:128:16], False, False)
+        P(donor, (K("wc"), "bow", K("Z")), (K("Zd"),), 128, (K("F"),), note="donor")
 
         def asum(e):
             for i in range(16):
-                o = e.matmul(Fa[:, 48:56], zs(T.z1, i), wc[:, i:128:16], i == 0, i == 15)
+                o = e.matmul(F[:, 16:32], zs(T.z16, i), wd[:, 0:2, i:128:16], False, i == 15)
             return o
-        P(asum, (K("wc"), "z1"), (K("Fa"),), 1024, FaK, note="A")
-        V(lambda e: e.tensor_copy(ii[:, 0:8], F[:, 0:8]), (K("Fd"),), (K("ii"),), 8, (K("F"),), note="f1")
-        V(lambda e: e.tensor_scalar(id_[:, 0:8], ii[:, 0:8], 15, None, OP.bitwise_and), (K("ii"),), (K("id"),), 8, note="f2")
-        V(lambda e: e.tensor_copy(ii[:, 8:16], Fa[:, 48:56]), (K("Fa"),), (K("iia"),), 8, FaK, note="f1a")
-        V(lambda e: e.tensor_scalar(id_[:, 8:16], ii[:, 8:16], 15, None, OP.bitwise_and), (K("iia"),), (K("ida"),), 8, note="f2a")
-        V(lambda e: e.tensor_scalar(T.oh[:, 8 * h + 1:8 * h + 9], id_[:, 0:8], T.icol[:, 0:1], None, OP.is_equal), (K("id"), "icol"), ("oh%d" % h,), 8, note="oh")
-        V(lambda e: e.tensor_tensor_scan(T.ex[:, 8 * h:8 * h + 8], T.oh[:, 8 * h:8 * h + 8], T.zero[:, 0:8], T.ex[:, 7:8] if h else 0.0, OP.add, OP.add),
-          ("ohz", "oh0", "zero") + (("oh1", "ex0") if h else ()), ("ex%d" % h,), 8, note="scan")
-        V(lambda e: e.tensor_tensor(B("ce")[:, :], T.oh[:, 8 * h + 1:8 * h + 9], T.ex[:, 8 * h:8 * h + 8], OP.mult), ("oh%d" % h, "ex%d" % h), (K("ce"),), 16, note="ce")
-        P(lambda e: e.matmul(F[:, 32:40], T.bo256[:, :], B("ce")[:, :], True, True), (K("ce"), "bo256"), (K("Fc"),), 64, (K("F"),), note="cnt")
-        V(lambda e: e.tensor_scalar(B("go")[:, :], id_[:, 0:8], 16.0, T.icol[:, 0:1], OP.mult, OP.add), (K("id"), "icol"), (K("go"),), 8, note="go")
-        V(lambda e: e.tensor_scalar(B("t16")[:, :], id_[:, 8:16], 0.0625, T.th16[:, 0:1], OP.mult, OP.add), (K("ida"), "th16"), (K("t16"),), 8, note="t16")
-        V(lambda e: e.tensor_tensor(B("tb")[:, :], T.cw[:, 0:256].indirect(B("go")[:, :]), bn[:, :], OP.subtract), ("cw", K("go"), "bn%d%d" % (t, h)), (K("tb"),), gat(128), note="T")
-        V(lambda e: e.tensor_tensor(B("ta")[:, :], B("t16")[:, :], F[:, 32:40], OP.add), (K("t16"), K("Fc")), (K("ta"),), 8, (K("F"),), note="ta")
+        P(asum, (K("wc"), K("dw"), "z16", K("Z")), (K("Za"),), 1024, (K("F"),), note="A")
 
         def dsum(e):
             for i in range(16):
-                o = e.matmul(S[:, 384:400], zs(T.z16, i), da[:, :, i:128:16], i == 0, i == 15)
+                o = e.matmul(D, zs(T.z16, i), wd[:, 2, i:128:16], False, i == 15)
             return o
-        P(dsum, (K("dw"), K("aw"), "z16"), (K("Sd"),), 1024, (K("S"),), note="D")
-        V(lambda e: e.tensor_scalar(B("sg")[:, :], S[:, 384:392], 0.0, 0.5, OP.is_lt, OP.subtract), (K("Sd"),), (K("sg"),), 8, (K("S"),), note="sg")
-        V(lambda e: e.tensor_tensor(B("qa")[:, :], S[:, 392:400], B("ta")[:, :], OP.is_gt), (K("Sd"), K("ta")), (K("qa"),), 8, (K("S"),), note="qa")
-        V(lambda e: e.tensor_tensor(B("zz")[:, :], B("sg")[:, :], B("qa")[:, :], OP.mult), (K("sg"), K("qa")), (K("zz"),), 16, note="zz")
-        V(lambda e: e.tensor_tensor(B("ee")[:, :], B("zz")[:, 0:8].indirect(T.bl[:, :]), T.cmpc[:, :], OP.is_ge), (K("zz"), "bl", "cmpc", "cmpc2"), (K("ee"),), gat(256), note="ee")
+        P(dsum, (K("aw"), "z16"), (K("D"),), 1024, (K("Y"),), note="D")
+        V(lambda e: e.tensor_copy(qi[:, 0:24], F[:, 0:24]), (K("Zd"), K("Za")), (K("qi"),), 24, (K("F"),), note="q")
+        V(lambda e: e.tensor_tensor(fr[:, :], Z, qi[:, :], OP.subtract), (K("Zd"), K("Za"), K("Z"), K("qi"), K("qiz")), (K("fr"),), 32, (K("F"),), note="frac")
+        V(lambda e: e.tensor_tensor_scan(nn[:, 8 * h + 1:8 * h + 9], fr[:, 0:8], fr[:, 0:8], nn[:, 8 * h:8 * h + 1], OP.min, OP.min),
+          (K("fr"), "nn0" if h else "nn"), ("nn%d" % h,), 16, note="scan")
+        A(lambda e: e.activation(B("sn")[:, :], fr[:, 24:32], AF.Sign), (K("fr"),), (K("sn"),), 8, note="sign")
+        V(lambda e: e.tensor_scalar(B("go")[:, :], fr[:, 8:16], 256.0, col(GOC), OP.mult, OP.add), (K("fr"), "goc"), (K("go"),), 8, note="go")
+
+        def act(e):
+            e.matmul(F[:, 32:40], T.bo64[:, :], nn[:, 8 * h:8 * h + 8], True, False)
+            e.matmul(F[:, 32:40], T.nbo64[:, :], nn[:, 8 * h + 1:8 * h + 9], False, False)
+            return e.matmul(F[:, 32:40], T.ident[:, :], B("sn")[:, :], False, True)
+        P(act, ("nn", "nn0", "nn%d" % h, K("sn"), "bo64", "nbo64", "ident"), (K("Fa"),), 192, (K("F"),), note="act")
+        qa = T["qr%d" % t][:, 8 * h:8 * h + 8]
+        V(lambda e: e.tensor_tensor(qa, D, fr[:, 16:24], OP.is_gt), (K("D"), K("fr")), ("qr%d%d" % (t, h),), 8, (K("Y"),), note="qa")
+        neg = t == 2
+        V(lambda e: e.tensor_tensor(B("tb")[:, :], cw[:, :].indirect(B("go")[:, :]), bn, OP.add if neg else OP.subtract), ("cw%d" % t, K("go"), kbn), (K("tb"),), gat(128), note="T")
+        V(lambda e: e.tensor_tensor(B("zz")[:, :], F[:, 32:40], qa, OP.add), (K("Fa"), "qr%d%d" % (t, h)), (K("zz"),), 8, (K("F"),), note="zz")
+        spread = B("zz")[:, 0:8].indirect(T.bl[:, :])
+        V(lambda e: e.tensor_tensor(B("ee")[:, 0:128], spread, T.cmpc[:, :], OP.is_equal), (K("zz"), "bl", "cmpc"), (K("er"),), gat(128), note="er")
+
+        def colmask(e):
+            if e is VEC[0]:
+                return e.tensor_scalar(B("ee")[:, 128:256], spread, 6.0, None, OP.is_equal)
+            return e.activation(B("ee")[:, 128:256], spread, AF.Relu, bias=-5.0)
+        either(colmask, (K("zz"), "bl"), (K("ec"),), gat(128), "ec")
+        Xm, M = X[:, 0:2, :], Y[:, 0:2, :]
 
         def xm(e):
-            e.matmul(X[:, 0:128], T.bo[:, :], B("ee")[:, 0:128], True, False)
-            return e.matmul(X[:, 0:128], T.ident[:, :], B("ee")[:, 128:256], False, True)
-        P(xm, (K("ee"), "bo", "ident"), (K("X"),), 256, (K("X"),), note="X")
-        A(lambda e: e.activation(Y[:, 0:128], X[:, 0:128], AF.Square, bias=-1.0), (K("X"),), (K("Y"),), 128, (K("X"), K("Y")), note="M")
-        last = t == R - 1
-        b3 = T["b3%d%d" % (t, h)]
-        kb3 = "b3%d%d" % (t, h)
-        mt = B("ms")[:, :] if last else Y[:, 128:256]
-        V(lambda e: e.tensor_tensor(mt, B("tb")[:, :], Y[:, 0:128], OP.mult), (K("tb"), K("Y")), (K("ms") if last else K("MT"),), 128, (K("Y"),), note="MT")
-        V(lambda e: e.tensor_tensor(b3[:, :, :], bn[:, :], mt, OP.add), ("bn%d%d" % (t, h), K("ms") if last else K("MT")), (kb3,), 256 if last else 128, () if last else (K("Y"),), note="B")
+            e.matmul(Xm, T.bo[:, :], B("ee")[:, 0:128], True, False)
+            return e.matmul(Xm, T.nident[:, :], B("ee")[:, 128:256], False, True)
+        P(xm, (K("er"), K("ec"), "bo", "nident"), (K("X"),), 256, (K("X"),), note="X")
+        if t == 0:
+            V(lambda e: e.tensor_scalar(M, Xm, 0.0, -1.0, OP.not_equal, OP.mult), (K("X"),), (K("Y"),), 128, (K("X"), K("Y")), note="M")
+        else:
+            A(lambda e: e.activation(M, Xm, AF.Abs), (K("X"),), (K("Y"),), 128, (K("X"), K("Y")), note="M")
+        b3, kb3 = T["b3%d%d" % (t, h)], "b3%d%d" % (t, h)
+        ms = T.ms[:, 128 * h:128 * h + 128]
+        if BPS and t < R - 1:
+            mp = Y[:, 2:4, :]
+            V(lambda e: e.tensor_tensor(mp, B("tb")[:, :], M, OP.mult), (K("tb"), K("Y")), (K("mp"),), 128, (K("Y"),), note="MT")
+            V(lambda e: e.tensor_tensor(b3[:, :], bn, mp, OP.add if t == 1 else OP.subtract), (kbn, K("mp")), (kb3,), 128, (K("Y"),), note="B")
+            A(lambda e: e.activation(ms, mp, AF.Identity), (K("mp"),), (K("ms"),), 128, (K("Y"),), note="MS")
+        else:
+            V(lambda e: e.tensor_tensor(ms, B("tb")[:, :], M, OP.mult), (K("tb"), K("Y")), (K("ms"),), 128, (K("Y"),), note="MT")
+            V(lambda e: e.tensor_tensor(b3[:, :], bn, ms, OP.add if t == 1 else OP.subtract), (kbn, K("ms")), (kb3,), 256, note="B")
         if t < R - 1:
             ls = T["ls%d%d" % (t, h)]
-            for ph in range(2):
-                V(lambda e, ph=ph: e.tensor_copy(ls[:, 64 * ph:64 * ph + 64], b3[:, :, 8 * ph:8 * ph + 8]), (kb3,), ("ls%d%d%d" % (t, h, ph),), 64, note="ls")
+            V(lambda e: e.tensor_copy(ls[:, :], b3[:, :].indirect(T.pm[:, :])), (kb3, "pm"), ("ls%d%d" % (t, h),), gat(128), note="ls")
             dst = T.cores[(T.rank_of(core) + HOP) % len(T.cores)]
             rid, pid, _ = topo.addr(dst)
             mask = 0
@@ -366,27 +396,23 @@ def build(core, T, topo, VEC):
                 mask |= 1 << en
             ne = len(topo.engines(core, dst)[::2])
             o = add("G", lambda e: e.remote_dma(T["lt%d%d" % (t + 1, h)][:, :], ls[:, :], T.sem["al%d%d" % (t + 1, h)], T.sem["sent"], pid, rid, mask),
-                    ("ls%d%d0" % (t, h), "ls%d%d1" % (t, h)), (), (), 0.3, sem="-sent", n=ne, note="send")
-            arr = add(None, None, (), ("lt%d%d0" % (t + 1, h), "lt%d%d1" % (t + 1, h)), (), 2.0, sem="al%d%d" % (t + 1, h), n=ne)
+                    ("ls%d%d" % (t, h),), (), (), 0.3, sem="-sent", n=ne, note="send")
+            arr = add(None, None, (), ("lt%d%d" % (t + 1, h),), (), 2.0, sem="al%d%d" % (t + 1, h), n=ne)
             ops[arr]["order"].add(o)
-            o = add("G", lambda e: e.remote_dma(T["bn%d%d" % (t + 1, h)][:, :], b3[:, :, :], T.sem["ab%d%d" % (t + 1, h)], T.sem["sent"], pid, rid, mask),
+            o = add("G", lambda e: e.remote_dma(T["bn%d%d" % (t + 1, h)][:, :], b3[:, :], T.sem["ab%d%d" % (t + 1, h)], T.sem["sent"], pid, rid, mask),
                     (kb3,), (), (), 0.3, sem="-sent", n=ne, note="send2")
             ops[o]["order"].add(arr - 1)
             arr = add(None, None, (), ("bn%d%d" % (t + 1, h),), (), 2.5, sem="ab%d%d" % (t + 1, h), n=ne)
             ops[arr]["order"].add(o)
         else:
-            add("Y", lambda e: e.dma_start(T.yb[:, 128 * h:128 * h + 128], b3[:, :, :]), (kb3,), (), (), 2.0, sem="st%d" % h, n=16)
-        A(lambda e: e.activation(B("cp")[:, :], T.cw[:, 0:256].indirect(B("go")[:, :]), AF.Identity), ("cw", K("go")), (K("cp"),), gat(128), note="CP")
-        if not last:
-            A(lambda e: e.activation(B("ms")[:, :], Y[:, 128:256], AF.Identity), (K("MT"),), (K("ms"),), 128, (K("Y"),), note="MS")
-
-        def smat(e):
-            e.matmul(F[:, 40:48], T.bo16[:, :], T.oh[:, 8 * h + 1:8 * h + 9], True, False)
-            return e.matmul(F[:, 40:48], T.bo256[:, :], B("ce")[:, :], False, True)
-        P(smat, (K("ce"), "oh%d" % h, "bo16", "bo256"), (K("Fs"),), 128, (K("F"),), note="so_p")
-        V(lambda e: e.tensor_scalar(B("so")[:, :], F[:, 40:48], T.icol[:, 0:1], None, OP.add), (K("Fs"), "icol"), (K("so"),), 8, (K("F"),), note="so")
-        V(lambda e: e.tensor_tensor(T.cw[:, :].indirect(B("so")[:, :]), B("cp")[:, :], B("ms")[:, :], OP.subtract), (K("cp"), K("ms"), K("so")), ("cw",), ("s", 128), note="scatter")
-        V(lambda e: e.tensor_tensor(T["qr%d" % t][:, 8 * h:8 * h + 8], S[:, 392:400], B("t16")[:, :], OP.is_gt), (K("Sd"), K("t16")), ("qr%d%d" % (t, h),), 8, (K("S"),), note="qr")
+            add("Y", lambda e: e.dma_start(T.yb[:, 128 * h:128 * h + 128], b3[:, :]), (kb3,), (), (), 2.0, sem="st%d" % h, n=16)
+        if h == 1:
+            A(lambda e: e.activation(T.nd[:, :], nn[:, 1:17], AF.Identity, accum_out=T.ns[:, 0:1]), ("nn0", "nn1"), ("ns",), 90, note="nsum")
+            either(lambda e: scale_on(e, T.sp[:, :], T.diag[:, :], T.ns[:, 0:1]), ("diag", "ns"), ("sp",), 16, "spread")
+            P(lambda e: e.matmul(S[:, 0:16], T.bo64[:, :], T.sp[:, :], True, True), ("sp", "bo64"), (K("S0"),), 64, (K("S"),), note="inv_p")
+            V(lambda e: e.tensor_scalar(T.inv[:, :], S[:, 0:16], col(INVC), None, OP.add), (K("S0"), "invc"), ("inv",), 16, (K("S"),), note="inv")
+            V(lambda e: e.tensor_tensor(T["cw%d" % (t + 1)][:, :], T.ms[:, :].indirect(T.inv[:, :]), cw[:, :], OP.add if t == 0 else OP.subtract),
+              ("ms_0", "ms_1", "msz", "inv", "cw%d" % t), ("cw%d" % (t + 1),), gat(256), note="C")
 
     for t in range(R):
         for h in range(2):
@@ -398,7 +424,7 @@ def build(core, T, topo, VEC):
             V(lambda e: e.tensor_tensor(T.qs[:, :], T.qr0[:, :], T.qr1[:, :], OP.add), ("qr00", "qr01", "qr10", "qr11"), ("qs",), 32)
     V(lambda e: e.tensor_tensor(T.qf[:, :], T.qs[:, :], T.qr2[:, :], OP.add), ("qs", "qr20", "qr21"), ("qf",), 32)
     add("Y", lambda e: e.dma_start(T.yq[:, :], T.qf[:, :]), ("qf",), (), (), 2.0, sem="st2", n=16)
-    add("Q", lambda e: e.dma_start(T.yc[:, :], T.cw[:, 0:256]), ("cw",), (), (), 2.0, sem="st3", n=16)
+    add("Q", lambda e: e.dma_start(T.yc[:, :], T["cw%d" % R][:, :]), ("cw%d" % R,), (), (), 2.0, sem="st3", n=16)
     return ops
 
 
@@ -409,46 +435,73 @@ def schedule(ops, tries):
     succ, needs = [[] for _ in range(n)], [len(a) + len(b) for a, b in deps]
     for i, (a, b) in enumerate(deps):
         for d in a:
-            succ[d].append((i, COSTS[0]["hop"]))
+            succ[d].append((i, COSTS[0]["hop"], 1))
         for d in b:
-            succ[d].append((i, 0.0))
-    way = [0.0] * n
+            succ[d].append((i, 0.0, 1))
+        if "after" in ops[i]:
+            succ[ops[i]["after"]].append((i, 0.0, 0))
+            needs[i] += 1
+    c0, cls, way, rank = c[0], [o.get("cls", -1) for o in ops], [0.0] * n, [0.0] * n
     for i in range(n - 1, -1, -1):
-        way[i] = min(c[0][i].values()) + max([way[s] + h for s, h in succ[i]] or [0.0])
+        way[i] = min(c0[i].values()) + max([way[s] + h for s, h, _ in succ[i] if cls[s] == cls[i]] or [0.0])
+    top = {k: max(way[i] for i in range(n) if cls[i] == k) for k in set(cls)}
+    for i in range(n - 1, -1, -1):
+        if cls[i] < 0:
+            rank[i] = min([rank[s] for s, _, _ in succ[i]] or [100.0]) - min(c0[i].values()) - 0.5
+        elif succ[i] and all(cls[s] != cls[i] for s, _, _ in succ[i]):
+            rank[i] = min(rank[s] for s, _, _ in succ[i]) - 2
+        else:
+            rank[i] = STRETCH * (top[cls[i]] - way[i]) + PERIOD * (cls[i] // 2) + LAG * (cls[i] % 2)
     first = [i for i in range(n) if needs[i] == 0]
     free_to_choose = [i for i in range(n) if ops[i]["q"] == "AV"]
+    queue = {"Q": "A"}
 
-    def listed(shift, pick):
-        rank = [s - w for s, w in zip(shift, way)]
-        est, free, order, need, ready, c0 = [0.0] * n, dict.fromkeys("AVPGYQ", 0.0), [], needs[:], first[:], c[0]
-        while ready:
-            b0, b1, bi = 1e9, 0.0, -1
-            for i in ready:
-                q = pick[i]
-                r = est[i]
-                if q is not None and free[q] > r:
-                    r = free[q]
-                if r < b0 - 0.005 or (r < b0 + 0.005 and rank[i] < b1):
-                    b0, b1, bi = r, rank[i], i
-            q = pick[bi]
-            r = est[bi] if q is None else max(est[bi], free[q])
-            ready.remove(bi)
-            order.append(bi)
-            x = c0[bi][q]
-            if q is not None:
-                free[q] = r + (0.06 if q in "YQ" else x)
-            for s, h in succ[bi]:
-                if r + x + h > est[s]:
-                    est[s] = r + x + h
+    def listed(rank, pick):
+        est, order, need = [0.0] * n, [], needs[:]
+        free, low = dict.fromkeys("AVPGY", 0.0), dict.fromkeys("AVPGY", 1e9)
+        ready = {q: [] for q in "AVPGY"}
+        on = [queue.get(q, q) for q in pick]
+
+        def done(i, r, x):
+            order.append(i)
+            for s, h, k in succ[i]:
+                if r + k * x + h > est[s]:
+                    est[s] = r + k * x + h
                 need[s] -= 1
                 if need[s] == 0:
-                    ready.append(s)
-        return order
+                    q = on[s]
+                    if q is None:
+                        done(s, est[s], c0[s][None])
+                    else:
+                        ready[q].append(s)
+                        if est[s] < low[q]:
+                            low[q] = est[s]
+        for i in first:
+            ready[on[i]].append(i)
+            low[on[i]] = 0.0
+        while True:
+            q, t = None, 1e8
+            for e in "AVPGY":
+                r = low[e] if low[e] > free[e] else free[e]
+                if r < t:
+                    q, t = e, r
+            if q is None:
+                return order
+            lst, b, bi = ready[q], 1e9, -1
+            for i in lst:
+                if est[i] - t <= 0.005 and rank[i] < b:
+                    b, bi = rank[i], i
+            lst.remove(bi)
+            low[q] = min([est[i] for i in lst]) if lst else 1e9
+            r = est[bi] if est[bi] > t else t
+            x = c0[bi][pick[bi]]
+            free[q] = r + (0.06 if pick[bi] in "YQ" else x)
+            done(bi, r, x)
 
     def spans(order, pick):
         out = []
         for C, cc in zip(COSTS, c):
-            hop, done, free = C["hop"], [0.0] * n, dict.fromkeys("AVPGYQ", 0.0)
+            hop, done, free = C["hop"], [0.0] * n, dict.fromkeys("AVPGY", 0.0)
             for i in order:
                 r = 0.0
                 a, b = deps[i]
@@ -462,30 +515,36 @@ def schedule(ops, tries):
                 q = pick[i]
                 x = cc[i][q]
                 if q is not None:
-                    if free[q] > r:
-                        r = free[q]
-                    free[q] = r + (0.06 if q in "YQ" else x)
+                    e = queue.get(q, q)
+                    if free[e] > r:
+                        r = free[e]
+                    free[e] = r + (0.06 if q in "YQ" else x)
                 done[i] = r + x
             out.append(max(done))
         return out, done
 
     rng = np.random.default_rng(SEED)
-    shift, pick = [0.0] * n, ["A" if o["q"] == "AV" else o["q"] for o in ops]
-    order = listed(shift, pick)
+    pick = ["A" if o["q"] == "AV" else o["q"] for o in ops]
+    order = listed(rank, pick)
     base = spans(order, pick)[0]
     cur, best = 1.0, (1.0, order, list(pick), base)
     for k in range(tries):
-        s2, p2 = list(shift), list(pick)
-        for i in rng.integers(0, n, int(rng.choice([1, 2, 4, 10, 25]))):
-            s2[i] = float(4 * rng.normal())
-        if rng.random() < 0.3:
+        s2, p2, u = list(rank), list(pick), rng.random()
+        if u < 0.55:
+            for i in rng.integers(0, n, int(rng.choice([1, 2, 4, 10]))):
+                s2[i] += float(0.5 * rng.normal())
+        elif u < 0.7:
+            a, d = int(rng.integers(0, n)), float(0.5 * rng.normal())
+            for i in range(a, min(n, a + int(rng.integers(5, 60)))):
+                s2[i] += d
+        else:
             for i in rng.choice(free_to_choose, int(rng.integers(1, 3))):
                 p2[i] = "V" if p2[i] == "A" else "A"
         order = listed(s2, p2)
         sp = spans(order, p2)[0]
         f = sum(a / b for a, b in zip(sp, base)) / len(sp)
-        if f < cur + 0.0004 * (1 - k / tries) * rng.random():
-            cur, shift, pick = f, s2, p2
+        if f < cur + 0.0006 * (1 - k / tries) * rng.random():
+            cur, rank, pick = f, s2, p2
             if f < best[0]:
                 best = (f, order, p2, sp)
     _, order, pick, sp = best

@@ -33,15 +33,15 @@ SCRATCH = {
     "ident": ("sbuf", [128, 128], "bfloat16"),
     "nident": ("sbuf", [128, 128], "bfloat16"),
     "zw": ("sbuf", [128, 144], "bfloat16"),
-    "zn": ("sbuf", [128, 144], "bfloat16"),
+    "z2": ("sbuf", [128, 144], "bfloat16"),
+    "far": ("sbuf", [128, 32, 2], "bfloat16"),
     "z16": ("sbuf", [128, 144], "bfloat16"),
     "prow": ("sbuf", [128, 128], "float32"),
-    "cmpc": ("sbuf", [128, 128], "float32"),
+    "cmpc": ("sbuf", [128, 256], "float32"),
     "diag": ("sbuf", [128, 16], "bfloat16"),
-    "cini": ("sbuf", [128, 32], "bfloat16"),
-    "tini": ("sbuf", [128, 16], "bfloat16"),
-    "bli": ("sbuf", [128, 8], "int32"),
-    "bl": ("sbuf", [128, 8], "uint16"),
+    "cini": ("sbuf", [128, 56], "bfloat16"),
+    "bli": ("sbuf", [128, 16], "int32"),
+    "bl": ("sbuf", [128, 16], "uint16"),
     "pmi": ("sbuf", [128, 8], "int32"),
     "pm": ("sbuf", [128, 8], "uint16"),
     "nn": ("sbuf", [128, 24], "bfloat16"),
@@ -64,9 +64,9 @@ for _t in range(R):
         if _t < R - 1:
             SCRATCH["ls%d%d" % (_t, _h)] = ("sbuf", [128, 128], "uint16")
 for _h in range(2):
-    for _n, _s, _d in (("fa", [128, 1024], "bfloat16"), ("dc", [128, 1024], "bfloat16"), ("ac", [128, 1024], "bfloat16"),
+    for _n, _s, _d in (("fa", [128, 1024], "bfloat16"), ("dc", [128, 1024], "bfloat16"), ("ac", [128, 8, 128], "bfloat16"),
                        ("ar", [128, 2, 512], "bfloat16"), ("ia", [128, 128], "int32"), ("ib", [128, 128], "int32"), ("lu", [128, 128], "uint16"),
-                       ("wd", [128, 3, 128], "bfloat16"), ("qi", [128, 32], "int32"), ("fr", [128, 32], "float32"),
+                       ("wd", [128, 3, 128], "bfloat16"), ("qi", [128, 32], "int32"), ("fr", [128, 40], "float32"),
                        ("go", [128, 8], "uint16"), ("sn", [128, 8], "bfloat16"), ("tb", [128, 128], "float32"),
                        ("zz", [128, 8], "float32"), ("ee", [128, 256], "bfloat16")):
         SCRATCH["%s_%d" % (_n, _h)] = ("sbuf", _s, _d)
@@ -78,15 +78,21 @@ for _h in range(2):
 DMAS = ["ld%d" % _k for _k in range(8)] + ["st%d" % _k for _k in range(4)]
 SEMAPHORES = ["V", "A", "P", "G", "sent"] + DMAS + ["%s%d%d" % (_a, _t, _h) for _a in ("al", "ab") for _t in (1, 2) for _h in (0, 1)]
 
-COSTS = ({"cy": 0.00083, "V": 0.03, "A": 0.05, "P": 0.0005, "g": 1.5, "hop": 0.09},
-         {"cy": 0.00083, "V": 0.05, "A": 0.065, "P": 0.00075, "g": 1.5, "hop": 0.07},
-         {"cy": 0.00083, "V": 0.02, "A": 0.03, "P": 0.00042, "g": 1.3, "hop": 0.12},
-         {"cy": 0.00083, "V": 0.03, "A": 0.04, "P": 0.0005, "g": 1.9, "hop": 0.07})
+COSTS = ({"cy": 0.00083, "V": 0.0, "A": 0.02, "P": 0.00042, "g": 1.56, "hop": (0.21, 0.21, 0.10, 0.07), "dma": 0.7},
+         {"cy": 0.00104, "V": 0.0, "A": 0.03, "P": 0.00055, "g": 1.3, "hop": (0.22, 0.10, 0.10, 0.10), "dma": 0.9},
+         {"cy": 0.00100, "V": 0.0, "A": 0.02, "P": 0.00050, "g": 1.9, "hop": (0.22, 0.15, 0.15, 0.15), "dma": 0.7},
+         {"cy": 0.00116, "V": 0.0, "A": 0.03, "P": 0.00065, "g": 1.6, "hop": (0.25, 0.22, 0.10, 0.07), "dma": 0.9})
+
+
+def hop(a, b, c):
+    return c["hop"][(0 if b == "V" else 1) if a == "V" else 2 if a == "A" else 3]
 
 
 def cost(q, n, c):
-    if q not in ("A", "V", "P"):
+    if q == "G":
         return n
+    if q not in ("A", "V", "P"):
+        return n * c["dma"]
     if q == "P":
         return n * c["P"]
     if isinstance(n, tuple):
@@ -96,11 +102,11 @@ def cost(q, n, c):
     return c[q] + max(64, n) * c["cy"]
 
 
-CH = (2, 2, 1, 1)
-RELU = ()
-BPS = True
-PERIOD, LAG, STRETCH = 20.0, 6.0, 1.15
-SEED, TRIES = 1, 12000
+CH = (2, 2, 2, 2)
+JOIN, HALF, FIRST = 4, (), 0.5
+BPS, SP, TCH = True, False, 4
+PERIOD, LAG, STRETCH, TIED, HEAT = 23.0, 5.0, 1.15, 0.1, 0.0006
+SEED, TRIES = 1, 20000
 
 
 def build(core, T, topo, VEC):
@@ -128,7 +134,9 @@ def build(core, T, topo, VEC):
             readers.setdefault(k, []).append(me)
         for b in bk:
             banks.setdefault(b, {})[q] = me
-        deps.discard(me)
+        if note in ("row2", "weighr", "weighe", "D"):
+            order |= {d for d in deps if ops[d]["q"] == "P"}
+            deps -= order
         ops.append({"q": q, "fn": fn, "deps": deps, "order": order - deps, "c": c, "sem": sem, "n": n, "note": note})
         return me
 
@@ -159,11 +167,6 @@ def build(core, T, topo, VEC):
             return e.tensor_scalar(out, in_, s, None, OP.mult)
         return e.activation(out, in_, AF.Identity, scale=s)
 
-    def relu_on(e, out, in_):
-        if e is VEC[0]:
-            return e.tensor_scalar(out, in_, 0.0, 2.0, OP.max, OP.mult)
-        return e.activation(out, in_, AF.Relu, scale=2.0)
-
     def either(fn, rd, wr, n, note=""):
         add("AV", fn, rd, wr, (), n, note=note)
 
@@ -176,18 +179,17 @@ def build(core, T, topo, VEC):
         prev = o
 
     col = lambda k: T.col[:, k:k + 1]
-    ICOL, SQB, PMC, PM2, WCOL, W16, THC, I16, GOC, INVC = range(10)
+    ICOL, SQB, PMC, PM2, WCOL, W16, THC, I16, GOC, FAR = range(10)
     G(lambda e: e.iota(T.pi[:, 0:1], [[0, 1]], 0, 1), (), ("pi",), 0.2)
-    G(lambda e: e.iota(T.pf[:, 0:1], [[0, 1]], -592, 1, allow_small_or_imprecise_dtypes=True), (), ("pf",), 0.2)
+    G(lambda e: e.iota(T.pf[:, 0:1], [[0, 1]], 592, -1, allow_small_or_imprecise_dtypes=True), (), ("pf",), 0.2)
     G(lambda e: e.iota(T.pmi[:, :], [[2, 8]], 0, 0), (), ("pmi",), 0.2)
     G(lambda e: e.iota(T.tu[:, :], [[16, 128]], 0, 1, allow_small_or_imprecise_dtypes=True), (), ("tu",), 0.34)
     V(lambda e: e.memset(T.ones[:, :], 1.0), (), ("ones",), 64)
     G(lambda e: e.affine_select(T.ident[:, :], T.ones[:, :], [[-1, 128]], OP.is_equal, 0.0, 0, 1), ("ones",), ("ident",), 0.4)
     G(lambda e: e.affine_select(T.m1[:, :], T.ones[:, :], [[-16, 8], [0, 16]], OP.is_ge, 0.0, 0, 1), ("ones",), ("m1",), 0.4)
     G(lambda e: e.affine_select(T.bo[:, :], T.m1[:, :], [[16, 8], [0, 16]], OP.is_ge, 0.0, 15, -1), ("m1",), ("bo",), 0.4)
-    G(lambda e: e.iota(T.bli[:, :], [[1, 8]], 0, 0), (), ("bli",), 0.2)
-    G(lambda e: e.iota(T.prow[:, :], [[0, 8], [16, 16]], 4, 0, allow_small_or_imprecise_dtypes=True), (), ("prow",), 0.4)
-    V(lambda e: e.memset(T.zw[:, :], 0.0), (), ("zw",), 72)
+    G(lambda e: e.iota(T.bli[:, :], [[0, 2], [1, 8]], 0, 0), (), ("bli",), 0.2)
+    G(lambda e: e.iota(T.prow[:, :], [[0, 8], [1 if SP else 16, 16]], 0 if SP else 4, 0, allow_small_or_imprecise_dtypes=True), (), ("prow",), 0.4)
     V(lambda e: e.memset(T.z16[:, :], 0.0), (), ("z16",), 72)
     V(lambda e: e.tensor_scalar(T.pj[:, 0:1], T.pi[:, 0:1], 15, None, OP.bitwise_and), ("pi",), ("pj",), 8)
     V(lambda e: e.tensor_copy(col(ICOL), T.pj[:, 0:1]), ("pj",), ("icol",), 8)
@@ -196,41 +198,49 @@ def build(core, T, topo, VEC):
     V(lambda e: e.tensor_scalar(T.pm[:, :], T.pmi[:, :], col(PMC), None, OP.add), ("pmi", "pmc"), ("pm",), 8)
     for h in range(2):
         V(lambda e, h=h: e.tensor_copy(T["lt0%d" % h][:, :], T.bni[:, 128 * h:128 * h + 128].indirect(T.pm[:, :])), ("bn0%d" % h, "pm"), ("lt0%d" % h,), gat(128))
-    V(lambda e: e.tensor_scalar(col(SQB), col(ICOL), T.pf[:, 0:1], None, OP.subtract), ("icol", "pf"), ("sqb",), 8)
+    A(lambda e: e.activation(col(SQB), col(ICOL), AF.Identity, bias=T.pf[:, 0:1]), ("icol", "pf"), ("sqb",), 8)
     A(lambda e: e.activation(T.sq[:, :], T.tu[:, :], AF.Square, bias=col(SQB)), ("tu", "sqb"), ("sq",), 128)
     for l in range(4):
         V(lambda e, l=l: e.tensor_scalar(T.xa[:, l, :], T.sq[:, :], float((32 * KAP[l] - 592 * 592) % 65536), None, OP.add), ("sq",), ("xa%d" % l,), 128)
         V(lambda e, l=l: e.tensor_scalar(T.xb[:, l, :], T.xa[:, l, :], 5, W - 1, OP.arith_shift_right, OP.bitwise_and), ("xa%d" % l,), ("xb%d" % l,), 128)
         V(lambda e, l=l: e.tensor_copy(T.xl[:, 128 * l:128 * l + 128], T.xb[:, l, :]), ("xb%d" % l,), ("xl%d" % l,), 128)
-        for c in range(4):
-            k0, k1 = 32 * c, 32 * c + 32
+        for c in range(TCH):
+            k0, k1 = 128 // TCH * c, 128 // TCH * (c + 1)
             either(lambda e, l=l, k0=k0, k1=k1: gather_on(e, T.xt[:, W * l + 16 * k0:W * l + 16 * k1], T.xw[:, :].indirect(T.xl[:, 128 * l + k0:128 * l + k1])),
                    ("xw", "xl%d" % l), ("x%d%d" % (l, c),), gat(16 * (k1 - k0)), "table")
-    either(lambda e: scale_on(e, T.nident[:, :], T.ident[:, :], -1.0), ("ident",), ("nident",), 128)
-    V(lambda e: e.tensor_copy(col(WCOL), T.wti[:, :]), ("wti",), ("wcol",), 8)
-    either(lambda e: scale_on(e, T.zw[:, 15:128:16], T.bo[:, 0:128:16], col(WCOL)), ("bo", "wcol"), ("zw",), 8)
-    if RELU:
-        either(lambda e: scale_on(e, T.zn[:, :], T.zw[:, :], -1.0), ("zw",), ("zn",), ("h", 144))
-    V(lambda e: e.tensor_scalar(col(THC), T.thi[:, :], -0.0625, -15.0 / 32, OP.mult, OP.add), ("thi",), ("thc",), 8)
-    either(lambda e: scale_on(e, T.tini[:, 0:8], T.ones[:, 0:8], col(THC)), ("ones", "thc"), ("tini0",), 8)
-    V(lambda e: e.tensor_scalar(T.tini[:, 8:16], T.tini[:, 0:8], -1.0, col(THC), OP.mult, OP.add), ("tini0", "thc"), ("tini1",), 8)
-    V(lambda e: e.tensor_copy(T.bl[:, :], T.bli[:, :]), ("bli",), ("bl",), 16)
+    either(lambda e: scale_on(e, T.nident[:, :], T.ident[:, :], -1.0), ("ident",), ("nident",), ("h", 128))
     either(lambda e: scale_on(e, T.z16[:, 15:128:16], T.bo[:, 0:128:16], 0.0625), ("bo",), ("z16",), 8)
-    V(lambda e: e.tensor_scalar(T.bow[:, :], T.bo[:, :], col(WCOL), 0.0625, OP.mult, OP.mult), ("bo", "wcol"), ("bow",), 64)
-    either(lambda e: scale_on(e, T.bo64[:, :], T.bo[:, :], 64.0), ("bo",), ("bo64",), 128)
-    either(lambda e: scale_on(e, T.nbo64[:, :], T.bo[:, :], -64.0), ("bo",), ("nbo64",), 128)
-    either(lambda e: scale_on(e, col(I16), col(ICOL), 16.0), ("icol",), ("i16",), 8)
-    V(lambda e: e.tensor_scalar(T.cmpc[:, :], T.prow[:, :], col(I16), None, OP.subtract), ("prow", "i16"), ("cmpc",), 128)
-    V(lambda e: e.tensor_scalar(T.diag[:, :], T.cmpc[:, 0:16], 4.0, 4.0, OP.is_equal, OP.mult), ("cmpc",), ("diag",), 16)
+    V(lambda e: e.tensor_scalar(col(WCOL), T.wti[:, :], 16.0, None, OP.mult), ("wti",), ("wcol",), 8)
+    either(lambda e: scale_on(e, T.zw[:, :], T.z16[:, :], col(WCOL)), ("z16", "wcol"), ("zw",), ("h", 144))
+    if HALF:
+        V(lambda e: e.tensor_tensor(T.z2[:, 8:144], T.zw[:, 8:144], T.zw[:, 0:136], OP.add), ("zw",), ("z2",), 272)
+        for s in range(2):
+            V(lambda e, s=s: e.tensor_scalar(col(FAR + s), col(ICOL), 8.0, 2.0 ** 21, OP.is_lt if s else OP.is_ge, OP.mult), ("icol",), ("farc%d" % s,), 8)
+            either(lambda e, s=s: scale_on(e, T.far[:, :, s], T.ones[:, 0:32], col(FAR + s)), ("ones", "farc%d" % s), ("far%d" % s,), 32)
+    V(lambda e: e.tensor_scalar(col(THC), T.thi[:, :], -0.0625, -15.0 / 32, OP.mult, OP.add), ("thi",), ("thc",), 8)
+    either(lambda e: scale_on(e, T.cini[:, 32:40], T.ones[:, 0:8], col(THC)), ("ones", "thc"), ("tini0",), 8)
+    A(lambda e: e.activation(T.cini[:, 40:48], T.cini[:, 32:40], AF.Identity, bias=col(THC), scale=-1.0), ("tini0", "thc"), ("tini1",), 8)
+    V(lambda e: e.tensor_copy(T.bl[:, :], T.bli[:, :]), ("bli",), ("bl",), 16)
+    V(lambda e: e.tensor_scalar(T.bow[:, :], T.bo[:, :], col(WCOL), 1.0 / 256, OP.mult, OP.mult), ("bo", "wcol"), ("bow",), 64)
+    KB = 16384.0 if SP else 64.0
+    either(lambda e: scale_on(e, T.bo64[:, :], T.bo[:, :], KB), ("bo",), ("bo64",), ("h", 128))
+    either(lambda e: scale_on(e, T.nbo64[:, :], T.bo[:, :], -KB), ("bo",), ("nbo64",), ("h", 128))
+    if SP:
+        V(lambda e: e.memset(T.cmpc[:, 128:256], 1.0 / 64), (), ("cmpd",), 128)
+        V(lambda e: e.memset(T.cini[:, 48:56], 1.0 / 256), (), ("cini3",), 8)
+        V(lambda e: e.tensor_scalar(T.cmpc[:, 0:128], T.prow[:, :], col(ICOL), -1000.0, OP.not_equal, OP.mult), ("prow", "icol"), ("cmpc",), 128)
+    else:
+        either(lambda e: scale_on(e, col(I16), col(ICOL), -16.0), ("icol",), ("i16",), 8)
+        A(lambda e: e.activation(T.cmpc[:, 0:128], T.prow[:, :], AF.Identity, bias=col(I16)), ("prow", "i16"), ("cmpc",), 128)
+    V(lambda e: e.tensor_scalar(T.diag[:, :], T.cmpc[:, 0:16], 0.0 if SP else 4.0, 256 / KB, OP.is_equal, OP.mult), ("cmpc",), ("diag",), 16)
     V(lambda e: e.memset(T.cini[:, 8:24], -15.0 / 32), (), ("cini1",), 8)
     V(lambda e: e.memset(T.cini[:, 24:32], 1.0 / 32), (), ("cini2",), 8)
-    V(lambda e: e.tensor_scalar(col(W16), col(ICOL), -0.0625, -15.0 / 32, OP.mult, OP.add), ("icol",), ("w16",), 8)
+    A(lambda e: e.activation(col(W16), col(ICOL), AF.Identity, bias=-15.0 / 32, scale=-0.0625), ("icol",), ("w16",), 8)
     either(lambda e: scale_on(e, T.cini[:, 0:8], T.ones[:, 0:8], col(W16)), ("ones", "w16"), ("cini0",), 8)
-    V(lambda e: e.tensor_scalar(col(GOC), col(ICOL), 120.0, None, OP.add), ("icol",), ("goc",), 8)
-    V(lambda e: e.tensor_scalar(col(INVC), col(ICOL), 1920.0, None, OP.add), ("icol",), ("invc",), 8)
+    A(lambda e: e.activation(col(GOC), col(ICOL), AF.Identity, bias=120.0), ("icol",), ("goc",), 8)
     V(lambda e: e.memset(T.nn[:, 0:1], -13.0 / 32), (), ("nn",), 8)
     V(lambda e: e.memset(T.ms[:, 256:272], 0.0), (), ("msz",), 16)
-    for h in range(2):
+    for h in range(0 if SP else 2):
         V(lambda e, h=h: e.memset(T["qi_%d" % h][:, 24:32], 0), (), ("qiz_%d" % h,), 8)
 
     def half(t, h):
@@ -253,33 +263,41 @@ def build(core, T, topo, VEC):
                 V(lambda e, lb=lb, x0=x0, m=m: e.tensor_tensor(dc[:, x0:x0 + m], w.indirect(lb), fa[:, x0:x0 + m], OP.subtract),
                   (k,) + wk + units("fa", x0, m), units("dc", x0, m), gat(m), note="gB")
             for la, lb, k, x0, m in pieces:
-                if l in RELU:
-                    either(lambda e, x0=x0, m=m: relu_on(e, ac[:, x0:x0 + m], dc[:, x0:x0 + m]), units("dc", x0, m), units("ac", x0, m), ("h", m), "relu")
-                else:
-                    A(lambda e, x0=x0, m=m: e.activation(ac[:, x0:x0 + m], dc[:, x0:x0 + m], AF.Abs), units("dc", x0, m), units("ac", x0, m), m, note="abs")
+                r = range(x0 % 512 // 128 * 2 + x0 // 512, (x0 % 512 + m) // 64, 2) if l == JOIN else range(x0 // 128, (x0 + m) // 128)
+                A(lambda e, x0=x0, m=m, r=r: e.activation(ac[:, r.start:r.stop:r.step, :], dc[:, x0:x0 + m], AF.Abs),
+                  units("dc", x0, m), tuple(K("ac%d" % u) for u in r), m, note="abs")
 
         def pieces(lst, c0, key, x0, n, ch):
             m, k = n // ch, n // ch // 16
             return [(lst[:, c0 + k * c:c0 + k * c + k], lst[:, c0 + n // 16 + k * c:c0 + n // 16 + k * c + k], key, x0 + m * c, m) for c in range(ch)]
 
-        def weigh(l, n):
-            def part(z, src, first, last):
+        def weigh(l, n, s=0):
+            if l in HALF:
                 def fn(e):
-                    for i in range(16):
-                        o = e.matmul(S[:, 0:n // 16], zs(z, i), src[:, i:n:16], first and i == 0, last and i == 15)
+                    for i in range(8):
+                        o = e.matmul(S[:, 0:n // 8], zs(T.z2, i), ac[:, 0:n // 128, i:128:8], False, i == 7)
                     return o
-                return fn
-            if l in RELU:
-                P(part(T.zn, dc, True, False), units("dc", 0, n) + ("zn",), (K("S0"),), 1024, (K("S"),), note="weighd")
-            P(part(T.zw, ac, l not in RELU, True), units("ac", 0, n) + ("zw",), (K("S0"),), 1024, (K("S"),), note="weigh")
+                P(lambda e: e.matmul(S[:, 0:n // 8], T.ident[:, :], T.far[:, 0:n // 16, :], True, False), ("ident", "far0", "far1"), (K("S0"),), 64, (K("S"),), note="far")
+                P(fn, units("ac", 0, n) + ("z2",), (K("S0"),), 512, (K("S"),), note="weighe")
+                V(lambda e: e.tensor_copy(B("ib")[:, 0:n // 16], S[:, 0:n // 8:2]), (K("S0"),), (K("ib0"),), n // 16, (K("S"),), note="i0")
+                return
 
-        def index(src, ks, bank, c0, n, wr):
+            def fn(e):
+                for i in range(16):
+                    o = e.matmul(F[:, 256:256 + n // 16] if s else S[:, 0:n // 16], zs(T.zw, i), ac[:, 4 * s:4 * s + n // 128, i:128:16], i == 0, i == 15)
+                return o
+            P(fn, units("ac", 512 * s, n) + ("zw",), (K("S%d" % s),), 1024, (K("SF"[s]),), note="weigh")
+
+        def index(src, ks, bank, c0, n, wr, two=False):
             ka, kb = K("ia%d" % (c0 // 64)), K("ib%d" % (c0 // 64))
-            V(lambda e: e.tensor_copy(B("ia")[:, c0:c0 + n], src), (ks,), (ka,), n, bank, note="i1")
+            if two:
+                V(lambda e: e.tensor_tensor(B("ia")[:, 0:n], S[:, 1:2 * n:2], B("ib")[:, 0:n], OP.min), (ks, kb), (ka,), n, bank, note="i1")
+            else:
+                V(lambda e: e.tensor_copy(B("ia")[:, c0:c0 + n], src), (ks,), (ka,), n, bank, note="i1")
             V(lambda e: e.tensor_scalar(B("ib")[:, c0:c0 + n], B("ia")[:, c0:c0 + n], W - 1, None, OP.bitwise_and), (ka,), (kb,), n, note="i2")
             V(lambda e: e.tensor_copy(lu[:, c0:c0 + n], B("ib")[:, c0:c0 + n]), (kb,), wr, n, note="i3")
 
-        table = lambda l: (T.xt[:, W * l:W * l + W], tuple("x%d%d" % (l, c) for c in range(4)))
+        table = lambda l: (T.xt[:, W * l:W * l + W], tuple("x%d%d" % (l, c) for c in range(TCH)))
 
         gather_pair(0, pieces(lt, 0, "lt%d%d" % (t, h), 0, 1024, CH[0]), T.xw[:, :], ("xw",))
 
@@ -306,76 +324,97 @@ def build(core, T, topo, VEC):
         index(S[:, 0:64], K("S0"), (K("S"),), 0, 64, (K("lu0"),))
         index(F[:, 256:320], K("S1"), (K("F"),), 64, 64, (K("lu1"),))
 
-        Z, D = F[:, 0:32], Y[:, 7, 0:8]
-        P(lambda e: e.matmul(Z, T.ident[:, :], T.cini[:, :], True, False), ("ident", "cini0", "cini1", "cini2"), (K("Z"),), 64, (K("F"),), note="zini")
+        Z, GD, D, kZ, kD, nz = X[:, 7, :], Y[:, 7, 0:16], Y[:, 7, 8:16], K("X"), K("Y"), 24 if SP else 32
+        P(lambda e: e.matmul(Z[:, 0:nz], T.ident[:, :], T.cini[:, 0:nz], True, False), ("ident", "cini0", "cini1", "cini2"), (K("Z"),), 64, (kZ,), note="zini")
 
         def dini(e):
-            e.matmul(D, T.ident[:, :], T.tini[:, 0:8], True, False)
-            return e.matmul(D, T.ident[:, :], T.tini[:, 8:16], False, False)
-        P(dini, ("ident", "tini0", "tini1"), (K("D"),), 128, (K("Y"),), note="dini")
+            e.matmul(GD, T.ident[:, :], T.cini[:, 24:40], True, False)
+            return e.matmul(D, T.ident[:, :], T.cini[:, 40:48], False, False)
+        P(dini, ("ident", "cini2", "tini0", "tini1"), (K("D"),), 128, (kD,), note="dini")
 
         for l, n in ((1, 512), (2, 256), (3, 128)):
-            gather_pair(l, [p for s in range(2) for p in pieces(lu, n // 8 * s, K("lu%d" % (s if l == 1 else 0)), n * s, n, CH[l])], *table(l - 1))
+            if l < JOIN:
+                for s in range(2):
+                    gather_pair(l, pieces(lu, 64 * s, K("lu%d" % s), 512 * s, n, CH[l] // 2), *table(l - 1))
+                    weigh(l, n, s)
+                    index(F[:, 256:256 + n // 16] if s else S[:, 0:n // 16], K("S%d" % s), (K("SF"[s]),), 64 * s, n // 16, (K("lu%d" % s),))
+                continue
+            if l > JOIN:
+                gather_pair(l, pieces(lu, 0, K("lu0"), 0, 2 * n, CH[l]), *table(l - 1))
+            else:
+                gather_pair(l, [p for s in range(2) for p in pieces(lu, 64 * s, K("lu%d" % s), 512 * s, n, CH[l] // 2)], *table(l - 1))
             weigh(l, 2 * n)
-            index(S[:, 0:n // 8], K("S0"), (K("S"),), 0, n // 8, (K("lu0"),))
+            index(S[:, 0:n // 8], K("S0"), (K("S"),), 0, n // 8, (K("lu0"),), l in HALF)
 
         w, wk = table(3)
         wd, qi, fr, nn = B("wd"), B("qi"), B("fr"), T.nn
         either(lambda e: gather_on(e, wd[:, 0, :], w.indirect(lu[:, 0:8])), wk + (K("lu0"),), (K("wc"),), gat(128), "gWC")
-        V(lambda e: e.tensor_tensor(wd[:, 1, :], w.indirect(lu[:, 8:16]), wd[:, 0, :], OP.subtract), wk + (K("lu0"), K("wc")), (K("dw"),), gat(128), note="gWR")
+        V(lambda e: e.tensor_tensor(wd[:, 1, :], w.indirect(lu[:, 8:16] if JOIN < 4 else lu[:, 64:72]), wd[:, 0, :], OP.subtract), wk + (K("lu%d" % (JOIN // 4)), K("wc")), (K("dw"),), gat(128), note="gWR")
         A(lambda e: e.activation(wd[:, 2, :], wd[:, 1, :], AF.Abs), (K("dw"),), (K("aw"),), 128, note="absW")
 
         def donor(e):
-            e.matmul(F[:, 0:8], T.bow[:, :], wd[:, 0, 0:128:16], False, False)
-            return e.matmul(F[:, 8:16], T.bow[:, :], wd[:, 0, 0:128:16], False, False)
-        P(donor, (K("wc"), "bow", K("Z")), (K("Zd"),), 128, (K("F"),), note="donor")
+            e.matmul(Z[:, 0:8], T.bow[:, :], wd[:, 0, 0:128:16], False, False)
+            return e.matmul(Z[:, 8:16], T.bow[:, :], wd[:, 0, 0:128:16], False, False)
+        P(donor, (K("wc"), "bow", K("Z")), (K("Zd"),), 128, (kZ,), note="donor")
 
         def asum(e):
             for i in range(16):
-                o = e.matmul(F[:, 16:32], zs(T.z16, i), wd[:, 0:2, i:128:16], False, i == 15)
+                o = e.matmul(Z[:, 16:nz], zs(T.z16, i), wd[:, 0:nz // 8 - 2, i:128:16], False, i == 15)
             return o
-        P(asum, (K("wc"), K("dw"), "z16", K("Z")), (K("Za"),), 1024, (K("F"),), note="A")
+        P(asum, (K("wc"), "z16", K("Z")) + (() if SP else (K("dw"),)), (K("Za"),), 1024, (kZ,), note="A")
 
         def dsum(e):
             for i in range(16):
-                o = e.matmul(D, zs(T.z16, i), wd[:, 2, i:128:16], False, i == 15)
+                o = e.matmul(GD if SP else D, zs(T.z16, i), wd[:, 1 if SP else 2:3, i:128:16], False, i == 15)
             return o
-        P(dsum, (K("aw"), "z16"), (K("D"),), 1024, (K("Y"),), note="D")
-        V(lambda e: e.tensor_copy(qi[:, 0:24], F[:, 0:24]), (K("Zd"), K("Za")), (K("qi"),), 24, (K("F"),), note="q")
-        V(lambda e: e.tensor_tensor(fr[:, :], Z, qi[:, :], OP.subtract), (K("Zd"), K("Za"), K("Z"), K("qi"), K("qiz")), (K("fr"),), 32, (K("F"),), note="frac")
+        P(dsum, (K("dw"), K("aw"), "z16"), (K("D"),), 1024, (kD,), note="D")
+        V(lambda e: e.tensor_copy(qi[:, 0:24], Z[:, 0:24]), (K("Zd"), K("Za")), (K("qi"),), 24, (kZ,), note="q")
+        V(lambda e: e.tensor_tensor(fr[:, 0:nz], Z[:, 0:nz], qi[:, 0:nz], OP.subtract), (K("Zd"), K("Za"), K("Z"), K("qi"), K("qiz")), (K("fr"),), 32, (kZ,), note="frac")
         V(lambda e: e.tensor_tensor_scan(nn[:, 8 * h + 1:8 * h + 9], fr[:, 0:8], fr[:, 0:8], nn[:, 8 * h:8 * h + 1], OP.min, OP.min),
           (K("fr"), "nn0" if h else "nn"), ("nn%d" % h,), 16, note="scan")
-        A(lambda e: e.activation(B("sn")[:, :], fr[:, 24:32], AF.Sign), (K("fr"),), (K("sn"),), 8, note="sign")
+        if not SP:
+            A(lambda e: e.activation(B("sn")[:, :], fr[:, 24:32], AF.Sign), (K("fr"),), (K("sn"),), 8, note="sign")
         V(lambda e: e.tensor_scalar(B("go")[:, :], fr[:, 8:16], 256.0, col(GOC), OP.mult, OP.add), (K("fr"), "goc"), (K("go"),), 8, note="go")
 
         def act(e):
-            e.matmul(F[:, 32:40], T.bo64[:, :], nn[:, 8 * h:8 * h + 8], True, False)
-            e.matmul(F[:, 32:40], T.nbo64[:, :], nn[:, 8 * h + 1:8 * h + 9], False, False)
-            return e.matmul(F[:, 32:40], T.ident[:, :], B("sn")[:, :], False, True)
-        P(act, ("nn", "nn0", "nn%d" % h, K("sn"), "bo64", "nbo64", "ident"), (K("Fa"),), 192, (K("F"),), note="act")
+            e.matmul(Act, T.bo64[:, :], nn[:, 8 * h:8 * h + 8], True, False)
+            e.matmul(Act, T.nbo64[:, :], nn[:, 8 * h + 1:8 * h + 9], False, False)
+            if SP:
+                return e.matmul(Act, T.nbo64[:, :], T.cini[:, 48:56], False, True)
+            return e.matmul(Act, T.ident[:, :], B("sn")[:, :], False, True)
+        Act, kA = (X[:, 6, 0:8], K("X")) if SP else (F[:, 0:8], K("F"))
+        P(act, ("nn", "nn0", "nn%d" % h, K("sn"), "bo64", "nbo64", "ident", "cini3"), (K("Fa"),), 192, (kA,), note="act")
         qa = T["qr%d" % t][:, 8 * h:8 * h + 8]
-        V(lambda e: e.tensor_tensor(qa, D, fr[:, 16:24], OP.is_gt), (K("D"), K("fr")), ("qr%d%d" % (t, h),), 8, (K("Y"),), note="qa")
+        if SP:
+            V(lambda e: e.tensor_tensor(fr[:, 24:32], fr[:, 16:24], Act, OP.subtract), (K("Fa"), K("fr")), (K("fra"),), 8, (kA,), note="fra")
+            V(lambda e: e.tensor_tensor(fr[:, 32:40], D, fr[:, 24:32], OP.is_gt), (K("D"), K("fra")), (K("qa"),), 8, (kD,), note="qa")
+            V(lambda e: e.tensor_tensor(B("zz")[:, :], GD[:, 0:8], fr[:, 32:40], OP.mult), (K("D"), K("qa")), (K("zz"),), 8, (kD,), note="zz")
+        V(lambda e: e.tensor_tensor(qa, D, fr[:, 16:24], OP.is_gt), (K("D"), K("fr")), ("qr%d%d" % (t, h),), 8, (kD,), note="qr" if SP else "qa")
         neg = t == 2
         V(lambda e: e.tensor_tensor(B("tb")[:, :], cw[:, :].indirect(B("go")[:, :]), bn, OP.add if neg else OP.subtract), ("cw%d" % t, K("go"), kbn), (K("tb"),), gat(128), note="T")
-        V(lambda e: e.tensor_tensor(B("zz")[:, :], F[:, 32:40], qa, OP.add), (K("Fa"), "qr%d%d" % (t, h)), (K("zz"),), 8, (K("F"),), note="zz")
-        spread = B("zz")[:, 0:8].indirect(T.bl[:, :])
-        V(lambda e: e.tensor_tensor(B("ee")[:, 0:128], spread, T.cmpc[:, :], OP.is_equal), (K("zz"), "bl", "cmpc"), (K("er"),), gat(128), note="er")
+        if not SP:
+            V(lambda e: e.tensor_tensor(B("zz")[:, :], Act, qa, OP.add), (K("Fa"), "qr%d%d" % (t, h)), (K("zz"),), 8, (K("F"),), note="zz")
+        spread = B("zz")[:, 0:8].indirect(T.bl[:, 0:8])
 
         def colmask(e):
             if e is VEC[0]:
                 return e.tensor_scalar(B("ee")[:, 128:256], spread, 6.0, None, OP.is_equal)
             return e.activation(B("ee")[:, 128:256], spread, AF.Relu, bias=-5.0)
-        either(colmask, (K("zz"), "bl"), (K("ec"),), gat(128), "ec")
+        if SP:
+            V(lambda e: e.tensor_tensor(B("ee")[:, :], B("zz")[:, 0:8].indirect(T.bl[:, :]), T.cmpc[:, :], OP.is_lt), (K("zz"), "bl", "cmpc", "cmpd"), (K("er"), K("ec")), gat(256), note="er")
+        else:
+            V(lambda e: e.tensor_tensor(B("ee")[:, 0:128], spread, T.cmpc[:, 0:128], OP.is_equal), (K("zz"), "bl", "cmpc"), (K("er"),), gat(128), note="er")
+            either(colmask, (K("zz"), "bl"), (K("ec"),), gat(128), "ec")
         Xm, M = X[:, 0:2, :], Y[:, 0:2, :]
 
         def xm(e):
             e.matmul(Xm, T.bo[:, :], B("ee")[:, 0:128], True, False)
-            return e.matmul(Xm, T.nident[:, :], B("ee")[:, 128:256], False, True)
+            return e.matmul(Xm, (T.ident if SP else T.nident)[:, :], B("ee")[:, 128:256], False, True)
         P(xm, (K("er"), K("ec"), "bo", "nident"), (K("X"),), 256, (K("X"),), note="X")
         if t == 0:
-            V(lambda e: e.tensor_scalar(M, Xm, 0.0, -1.0, OP.not_equal, OP.mult), (K("X"),), (K("Y"),), 128, (K("X"), K("Y")), note="M")
+            V(lambda e: e.tensor_scalar(M, Xm, float(SP), -1.0, OP.not_equal, OP.mult), (K("X"),), (K("Y"),), 128, (K("X"), K("Y")), note="M")
         else:
-            A(lambda e: e.activation(M, Xm, AF.Abs), (K("X"),), (K("Y"),), 128, (K("X"), K("Y")), note="M")
+            A(lambda e: e.activation(M, Xm, AF.Abs, bias=-float(SP)), (K("X"),), (K("Y"),), 128, (K("X"), K("Y")), note="M")
         b3, kb3 = T["b3%d%d" % (t, h)], "b3%d%d" % (t, h)
         ms = T.ms[:, 128 * h:128 * h + 128]
         if BPS and t < R - 1:
@@ -391,26 +430,25 @@ def build(core, T, topo, VEC):
             V(lambda e: e.tensor_copy(ls[:, :], b3[:, :].indirect(T.pm[:, :])), (kb3, "pm"), ("ls%d%d" % (t, h),), gat(128), note="ls")
             dst = T.cores[(T.rank_of(core) + HOP) % len(T.cores)]
             rid, pid, _ = topo.addr(dst)
-            mask = 0
-            for en in topo.engines(core, dst)[::2]:
-                mask |= 1 << en
-            ne = len(topo.engines(core, dst)[::2])
-            o = add("G", lambda e: e.remote_dma(T["lt%d%d" % (t + 1, h)][:, :], ls[:, :], T.sem["al%d%d" % (t + 1, h)], T.sem["sent"], pid, rid, mask),
-                    ("ls%d%d" % (t, h),), (), (), 0.3, sem="-sent", n=ne, note="send")
-            arr = add(None, None, (), ("lt%d%d" % (t + 1, h),), (), 2.0, sem="al%d%d" % (t + 1, h), n=ne)
+            engines = topo.engines(core, dst)
+            el, eb = engines[::2] if t == 0 else engines, engines[1::2]
+            mask = lambda es: sum(1 << en for en in es)
+            o = add("G", lambda e: e.remote_dma(T["lt%d%d" % (t + 1, h)][:, :], ls[:, :], T.sem["al%d%d" % (t + 1, h)], T.sem["sent"], pid, rid, mask(el)),
+                    ("ls%d%d" % (t, h),), (), (), 0.3, sem="-sent", n=len(el), note="send")
+            arr = add(None, None, (), ("lt%d%d" % (t + 1, h),), (), 2.0 + (FIRST if t + h == 0 else 0.0), sem="al%d%d" % (t + 1, h), n=len(el))
             ops[arr]["order"].add(o)
-            o = add("G", lambda e: e.remote_dma(T["bn%d%d" % (t + 1, h)][:, :], b3[:, :], T.sem["ab%d%d" % (t + 1, h)], T.sem["sent"], pid, rid, mask),
-                    (kb3,), (), (), 0.3, sem="-sent", n=ne, note="send2")
+            o = add("G", lambda e: e.remote_dma(T["bn%d%d" % (t + 1, h)][:, :], b3[:, :], T.sem["ab%d%d" % (t + 1, h)], T.sem["sent"], pid, rid, mask(eb)),
+                    (kb3,), (), (), 0.3, sem="-sent", n=len(eb), note="send2")
             ops[o]["order"].add(arr - 1)
-            arr = add(None, None, (), ("bn%d%d" % (t + 1, h),), (), 2.5, sem="ab%d%d" % (t + 1, h), n=ne)
+            arr = add(None, None, (), ("bn%d%d" % (t + 1, h),), (), 2.5, sem="ab%d%d" % (t + 1, h), n=len(eb))
             ops[arr]["order"].add(o)
         else:
             add("Y", lambda e: e.dma_start(T.yb[:, 128 * h:128 * h + 128], b3[:, :]), (kb3,), (), (), 2.0, sem="st%d" % h, n=16)
         if h == 1:
-            A(lambda e: e.activation(T.nd[:, :], nn[:, 1:17], AF.Identity, accum_out=T.ns[:, 0:1]), ("nn0", "nn1"), ("ns",), 90, note="nsum")
+            A(lambda e: e.activation(T.nd[:, :], nn[:, 1:17], AF.Identity, bias=15.0 / 32, accum_out=T.ns[:, 0:1]), ("nn0", "nn1"), ("ns",), 90, note="nsum")
             either(lambda e: scale_on(e, T.sp[:, :], T.diag[:, :], T.ns[:, 0:1]), ("diag", "ns"), ("sp",), 16, "spread")
             P(lambda e: e.matmul(S[:, 0:16], T.bo64[:, :], T.sp[:, :], True, True), ("sp", "bo64"), (K("S0"),), 64, (K("S"),), note="inv_p")
-            V(lambda e: e.tensor_scalar(T.inv[:, :], S[:, 0:16], col(INVC), None, OP.add), (K("S0"), "invc"), ("inv",), 16, (K("S"),), note="inv")
+            V(lambda e: e.tensor_scalar(T.inv[:, :], S[:, 0:16], col(ICOL), None, OP.add), (K("S0"), "icol"), ("inv",), 16, (K("S"),), note="inv")
             V(lambda e: e.tensor_tensor(T["cw%d" % (t + 1)][:, :], T.ms[:, :].indirect(T.inv[:, :]), cw[:, :], OP.add if t == 0 else OP.subtract),
               ("ms_0", "ms_1", "msz", "inv", "cw%d" % t), ("cw%d" % (t + 1),), gat(256), note="C")
 
@@ -435,7 +473,7 @@ def schedule(ops, tries):
     succ, needs = [[] for _ in range(n)], [len(a) + len(b) for a, b in deps]
     for i, (a, b) in enumerate(deps):
         for d in a:
-            succ[d].append((i, COSTS[0]["hop"], 1))
+            succ[d].append((i, 0.15, 2))
         for d in b:
             succ[d].append((i, 0.0, 1))
         if "after" in ops[i]:
@@ -454,7 +492,9 @@ def schedule(ops, tries):
             rank[i] = STRETCH * (top[cls[i]] - way[i]) + PERIOD * (cls[i] // 2) + LAG * (cls[i] % 2)
     first = [i for i in range(n) if needs[i] == 0]
     free_to_choose = [i for i in range(n) if ops[i]["q"] == "AV"]
-    queue = {"Q": "A"}
+    queue, end = {"Q": "A"}, [0.0]
+    names = ("A", "V", "P", "G", "Y", "Q", None)
+    hops = [{a: {b: hop(a, b, C) for b in names} for a in names} for C in COSTS]
 
     def listed(rank, pick):
         est, order, need = [0.0] * n, [], needs[:]
@@ -464,9 +504,11 @@ def schedule(ops, tries):
 
         def done(i, r, x):
             order.append(i)
+            wake = hops[0][on[i]]
             for s, h, k in succ[i]:
-                if r + k * x + h > est[s]:
-                    est[s] = r + k * x + h
+                h = r + x + wake[on[s]] if k == 2 else r + k * x
+                if h > est[s]:
+                    est[s] = h
                 need[s] -= 1
                 if need[s] == 0:
                     q = on[s]
@@ -496,23 +538,24 @@ def schedule(ops, tries):
             r = est[bi] if est[bi] > t else t
             x = c0[bi][pick[bi]]
             free[q] = r + (0.06 if pick[bi] in "YQ" else x)
+            end[0] = r + x
             done(bi, r, x)
 
     def spans(order, pick):
         out = []
-        for C, cc in zip(COSTS, c):
-            hop, done, free = C["hop"], [0.0] * n, dict.fromkeys("AVPGY", 0.0)
+        for wake, cc in zip(hops, c):
+            done, free = [0.0] * n, dict.fromkeys("AVPGY", 0.0)
             for i in order:
                 r = 0.0
                 a, b = deps[i]
+                q = pick[i]
                 for d in a:
-                    if done[d] > r:
-                        r = done[d]
-                r = r + hop if a else r
+                    x = done[d] + wake[pick[d]][q]
+                    if x > r:
+                        r = x
                 for d in b:
                     if done[d] > r:
                         r = done[d]
-                q = pick[i]
                 x = cc[i][q]
                 if q is not None:
                     e = queue.get(q, q)
@@ -525,29 +568,46 @@ def schedule(ops, tries):
 
     rng = np.random.default_rng(SEED)
     pick = ["A" if o["q"] == "AV" else o["q"] for o in ops]
-    order = listed(rank, pick)
-    base = spans(order, pick)[0]
-    cur, best = 1.0, (1.0, order, list(pick), base)
-    for k in range(tries):
-        s2, p2, u = list(rank), list(pick), rng.random()
-        if u < 0.55:
-            for i in rng.integers(0, n, int(rng.choice([1, 2, 4, 10]))):
-                s2[i] += float(0.5 * rng.normal())
-        elif u < 0.7:
-            a, d = int(rng.integers(0, n)), float(0.5 * rng.normal())
-            for i in range(a, min(n, a + int(rng.integers(5, 60)))):
-                s2[i] += d
-        else:
-            for i in rng.choice(free_to_choose, int(rng.integers(1, 3))):
-                p2[i] = "V" if p2[i] == "A" else "A"
-        order = listed(s2, p2)
-        sp = spans(order, p2)[0]
-        f = sum(a / b for a, b in zip(sp, base)) / len(sp)
-        if f < cur + 0.0006 * (1 - k / tries) * rng.random():
-            cur, rank, pick = f, s2, p2
-            if f < best[0]:
-                best = (f, order, p2, sp)
-    _, order, pick, sp = best
+    base = spans(listed(rank, pick), pick)[0]
+    seen, like = {}, {}
+    for i, o in enumerate(ops):
+        seen[cls[i], o["note"]] = seen.get((cls[i], o["note"]), 0) + 1
+        like.setdefault((cls[i] % 2 if cls[i] >= 0 else -1, o["note"], seen[cls[i], o["note"]]), []).append(i)
+    like = {i: v for v in like.values() for i in v}
+
+    def improved(rank, pick, tries):
+        order = listed(rank, pick)
+        sp = spans(order, pick)[0]
+        cur = sum(a / b for a, b in zip(sp, base)) / len(sp)
+        best, now = (cur, rank, pick, order, sp), end[0]
+        for k in range(tries):
+            s2, p2, u, tied = list(rank), list(pick), rng.random(), rng.random() < TIED
+            if u < 0.55:
+                for i in rng.integers(0, n, int(rng.choice([1, 2, 4, 10]))):
+                    d = float(0.5 * rng.normal())
+                    for j in like[i] if tied else (i,):
+                        s2[j] += d
+            elif u < 0.7:
+                a, d = int(rng.integers(0, n)), float(0.5 * rng.normal())
+                for i in range(a, min(n, a + int(rng.integers(5, 60)))):
+                    s2[i] += d
+            else:
+                for i in rng.choice(free_to_choose, int(rng.integers(1, 3))):
+                    q = "V" if p2[i] == "A" else "A"
+                    for j in like[i] if tied else (i,):
+                        p2[j] = q
+            order = listed(s2, p2)
+            if end[0] > 1.006 * now:
+                continue
+            sp = spans(order, p2)[0]
+            f = sum(a / b for a, b in zip(sp, base)) / len(sp)
+            if f < cur + HEAT * (1 - k / tries) * rng.random():
+                cur, rank, pick, now = f, s2, p2, end[0]
+                if f < best[0]:
+                    best = (f, rank, pick, order, sp)
+        return best
+    starts = [improved([r + d * (c % 2 if c >= 0 else 0) for r, c in zip(rank, cls)], pick, tries // 8) for d in (-2, -1, 0, 1)]
+    _, rank, pick, order, sp = improved(*min(starts, key=lambda s: s[0])[1:3], tries // 2)
     return order, spans(order, pick)[1], pick, (base, sp)
 
 

@@ -7,15 +7,16 @@ AF = ActivationFunctionType
 R, NB, HOP = 3, 16, 3
 KAP = (101, 1303, 2717, 3911)
 W = 2048
+TW = W + 16
+BIG = 1.5 * 2.0 ** 34
 
 SCRATCH = {
-    "xw": ("sbuf", [128, W], "bfloat16"),
-    "xt": ("sbuf", [128, 4 * W], "bfloat16"),
-    "tu": ("sbuf", [128, 128], "float32"),
-    "sq": ("sbuf", [128, 128], "float32"),
-    "xa": ("sbuf", [128, 4, 128], "int32"),
-    "xb": ("sbuf", [128, 4, 128], "int32"),
-    "xl": ("sbuf", [128, 4 * 128], "uint16"),
+    "xw": ("sbuf", [128, 2 * W + 4 * TW], "bfloat16"),
+    "tu": ("sbuf", [128, 130], "float32"),
+    "sq": ("sbuf", [128, 130], "float32"),
+    "xa": ("sbuf", [128, 130], "int32"),
+    "xb": ("sbuf", [128, 130], "int32"),
+    "xl": ("sbuf", [128, 4 * 130], "uint16"),
     "bni": ("sbuf", [128, 256], "int32"),
     "cni": ("sbuf", [128, 256], "int32"),
     "wti": ("sbuf", [128, 1], "int32"),
@@ -33,6 +34,8 @@ SCRATCH = {
     "ident": ("sbuf", [128, 128], "bfloat16"),
     "nident": ("sbuf", [128, 128], "bfloat16"),
     "zw": ("sbuf", [128, 144], "bfloat16"),
+    "i32": ("sbuf", [128, 2, 128], "float32"),
+    "hident": ("sbuf", [128, 128], "bfloat16"),
     "z2": ("sbuf", [128, 144], "bfloat16"),
     "far": ("sbuf", [128, 32, 2], "bfloat16"),
     "z16": ("sbuf", [128, 144], "bfloat16"),
@@ -54,7 +57,7 @@ SCRATCH = {
     "qf": ("sbuf", [128, 16], "float32"),
 }
 for _t in range(R):
-    SCRATCH["qr%d" % _t] = ("sbuf", [128, 16], "float32")
+    SCRATCH["qr%d" % _t] = ("sbuf", [128, 16], "bfloat16")
     SCRATCH["cw%d" % (_t + 1)] = ("sbuf", [128, 256], "float32")
     for _h in range(2):
         SCRATCH["lt%d%d" % (_t, _h)] = ("sbuf", [128, 128], "uint16")
@@ -65,10 +68,10 @@ for _t in range(R):
             SCRATCH["ls%d%d" % (_t, _h)] = ("sbuf", [128, 128], "uint16")
 for _h in range(2):
     for _n, _s, _d in (("fa", [128, 1024], "bfloat16"), ("dc", [128, 1024], "bfloat16"), ("ac", [128, 8, 128], "bfloat16"),
-                       ("ar", [128, 2, 512], "bfloat16"), ("ia", [128, 128], "int32"), ("ib", [128, 128], "int32"), ("lu", [128, 128], "uint16"),
+                       ("ar", [128, 2, 512], "bfloat16"), ("ia", [128, 128], "float32"), ("lu", [128, 128], "uint16"),
                        ("wd", [128, 3, 128], "bfloat16"), ("qi", [128, 32], "int32"), ("fr", [128, 40], "float32"),
                        ("go", [128, 8], "uint16"), ("sn", [128, 8], "bfloat16"), ("tb", [128, 128], "float32"),
-                       ("zz", [128, 8], "float32"), ("ee", [128, 256], "bfloat16")):
+                       ("zz", [128, 8], "float32"), ("mk", [128, 128], "float32"), ("ee", [128, 256], "bfloat16")):
         SCRATCH["%s_%d" % (_n, _h)] = ("sbuf", _s, _d)
     for _n in ("S", "F"):
         SCRATCH["%s_%d" % (_n, _h)] = ("psum", [128, 512], "float32")
@@ -78,14 +81,14 @@ for _h in range(2):
 DMAS = ["ld%d" % _k for _k in range(8)] + ["st%d" % _k for _k in range(4)]
 SEMAPHORES = ["V", "A", "P", "G", "sent"] + DMAS + ["%s%d%d" % (_a, _t, _h) for _a in ("al", "ab") for _t in (1, 2) for _h in (0, 1)]
 
-COSTS = ({"cy": 0.00083, "V": 0.0, "A": 0.02, "P": 0.00042, "g": 1.56, "hop": (0.21, 0.21, 0.10, 0.07), "dma": 0.7},
-         {"cy": 0.00104, "V": 0.0, "A": 0.03, "P": 0.00055, "g": 1.3, "hop": (0.22, 0.10, 0.10, 0.10), "dma": 0.9},
-         {"cy": 0.00100, "V": 0.0, "A": 0.02, "P": 0.00050, "g": 1.9, "hop": (0.22, 0.15, 0.15, 0.15), "dma": 0.7},
-         {"cy": 0.00116, "V": 0.0, "A": 0.03, "P": 0.00065, "g": 1.6, "hop": (0.25, 0.22, 0.10, 0.07), "dma": 0.9})
+COSTS = ({"cy": 0.00083, "V": 0.04, "A": 0.06, "P": 0.00048, "g": 1.56, "hop": (0.19, 0.15, 0.14), "dma": 0.8},
+         {"cy": 0.00104, "V": 0.04, "A": 0.07, "P": 0.00056, "g": 1.3, "hop": (0.20, 0.17, 0.17), "dma": 0.8},
+         {"cy": 0.00100, "V": 0.05, "A": 0.07, "P": 0.00058, "g": 1.9, "hop": (0.18, 0.14, 0.11), "dma": 0.7},
+         {"cy": 0.00116, "V": 0.05, "A": 0.08, "P": 0.00066, "g": 1.6, "hop": (0.22, 0.16, 0.16), "dma": 1.0})
 
 
 def hop(a, b, c):
-    return c["hop"][(0 if b == "V" else 1) if a == "V" else 2 if a == "A" else 3]
+    return c["hop"][0 if a == b else 1 if a == "V" else 2]
 
 
 def cost(q, n, c):
@@ -102,11 +105,12 @@ def cost(q, n, c):
     return c[q] + max(64, n) * c["cy"]
 
 
-CH = (2, 2, 2, 2)
-JOIN, HALF, FIRST = 4, (), 0.5
-BPS, SP, TCH = True, False, 4
-PERIOD, LAG, STRETCH, TIED, HEAT = 23.0, 5.0, 1.15, 0.1, 0.0006
-SEED, TRIES = 1, 20000
+CH = (2, 4, 2, 2)
+JOIN, HALF, FIRST = 4, (), 0.6
+RCUT, ICUT, LS = ((0, 8), (8, 16)), (), True
+TPE, SP, TCH, PL, ZA, BPE = False, False, 4, (), False, ()
+PERIOD, LAG, STRETCH, HEAT, PART = 23.0, 5.0, 1.15, 0.006, 8
+SEED, TRIES = 7, 12000
 
 
 def build(core, T, topo, VEC):
@@ -134,7 +138,7 @@ def build(core, T, topo, VEC):
             readers.setdefault(k, []).append(me)
         for b in bk:
             banks.setdefault(b, {})[q] = me
-        if note in ("row2", "weighr", "weighe", "D"):
+        if note in ("row2", "weighr", "weighe", "D", "act2", "Bp"):
             order |= {d for d in deps if ops[d]["q"] == "P"}
             deps -= order
         ops.append({"q": q, "fn": fn, "deps": deps, "order": order - deps, "c": c, "sem": sem, "n": n, "note": note})
@@ -171,9 +175,10 @@ def build(core, T, topo, VEC):
         add("AV", fn, rd, wr, (), n, note=note)
 
     prev = load("Y", 0, T.bni[:, 0:128], T.bn[:, 0:128], ("bn00",), 2.2)
-    load("Q", 1, T.xw[:, :], T.xf[:, :], ("xw",), 4.0)
+    load("Q", 1, T.xw[:, 0:W], T.xf[:, :], ("xw",), 4.0)
     for k, out, in_, key, c in ((2, T.wti[:, :], T.wt[:, :], "wti", 4.2), (4, T.bni[:, 128:256], T.bn[:, 128:256], "bn01", 4.5),
-                                (3, T.thi[:, :], T.th[:, :], "thi", 4.7), (5, T.cni[:, :], T.cn[:, :], "cw0", 5.2)):
+                                (6, T.xw[:, W:2 * W], T.xf[:, :], "xw2", 7.0),
+                                (3, T.thi[:, :], T.th[:, :], "thi", 7.2), (5, T.cni[:, :], T.cn[:, :], "cw0", 7.7)):
         o = load("Y", k, out, in_, (key,), c)
         ops[o]["after"] = prev
         prev = o
@@ -183,7 +188,8 @@ def build(core, T, topo, VEC):
     G(lambda e: e.iota(T.pi[:, 0:1], [[0, 1]], 0, 1), (), ("pi",), 0.2)
     G(lambda e: e.iota(T.pf[:, 0:1], [[0, 1]], 592, -1, allow_small_or_imprecise_dtypes=True), (), ("pf",), 0.2)
     G(lambda e: e.iota(T.pmi[:, :], [[2, 8]], 0, 0), (), ("pmi",), 0.2)
-    G(lambda e: e.iota(T.tu[:, :], [[16, 128]], 0, 1, allow_small_or_imprecise_dtypes=True), (), ("tu",), 0.34)
+    G(lambda e: e.iota(T.tu[:, 0:128], [[-1024, 2], [16, 64]], 1024, 1, allow_small_or_imprecise_dtypes=True), (), ("tu",), 0.34)
+    G(lambda e: e.iota(T.tu[:, 128:130], [[0, 2]], 1024, 1, allow_small_or_imprecise_dtypes=True), (), ("tu2",), 0.2)
     V(lambda e: e.memset(T.ones[:, :], 1.0), (), ("ones",), 64)
     G(lambda e: e.affine_select(T.ident[:, :], T.ones[:, :], [[-1, 128]], OP.is_equal, 0.0, 0, 1), ("ones",), ("ident",), 0.4)
     G(lambda e: e.affine_select(T.m1[:, :], T.ones[:, :], [[-16, 8], [0, 16]], OP.is_ge, 0.0, 0, 1), ("ones",), ("m1",), 0.4)
@@ -191,6 +197,7 @@ def build(core, T, topo, VEC):
     G(lambda e: e.iota(T.bli[:, :], [[0, 2], [1, 8]], 0, 0), (), ("bli",), 0.2)
     G(lambda e: e.iota(T.prow[:, :], [[0, 8], [1 if SP else 16, 16]], 0 if SP else 4, 0, allow_small_or_imprecise_dtypes=True), (), ("prow",), 0.4)
     V(lambda e: e.memset(T.z16[:, :], 0.0), (), ("z16",), 72)
+    fill = lambda out, n, v, key: G(lambda e: e.affine_select(out, T.ones[:, 0:n], [[0, n]], OP.is_ge, v, -1, 0), ("ones",), (key,), 0.2)
     V(lambda e: e.tensor_scalar(T.pj[:, 0:1], T.pi[:, 0:1], 15, None, OP.bitwise_and), ("pi",), ("pj",), 8)
     V(lambda e: e.tensor_copy(col(ICOL), T.pj[:, 0:1]), ("pj",), ("icol",), 8)
     V(lambda e: e.tensor_scalar(col(PM2), col(ICOL), 8.0, -127.0, OP.is_ge, OP.mult), ("icol",), ("pm2",), 8)
@@ -199,15 +206,15 @@ def build(core, T, topo, VEC):
     for h in range(2):
         V(lambda e, h=h: e.tensor_copy(T["lt0%d" % h][:, :], T.bni[:, 128 * h:128 * h + 128].indirect(T.pm[:, :])), ("bn0%d" % h, "pm"), ("lt0%d" % h,), gat(128))
     A(lambda e: e.activation(col(SQB), col(ICOL), AF.Identity, bias=T.pf[:, 0:1]), ("icol", "pf"), ("sqb",), 8)
-    A(lambda e: e.activation(T.sq[:, :], T.tu[:, :], AF.Square, bias=col(SQB)), ("tu", "sqb"), ("sq",), 128)
+    A(lambda e: e.activation(T.sq[:, :], T.tu[:, :], AF.Square, bias=col(SQB)), ("tu", "tu2", "sqb"), ("sq",), 128)
+    V(lambda e: e.tensor_scalar(T.xa[:, :], T.sq[:, :], float((32 * KAP[0] - 592 * 592) % 65536), None, OP.add), ("sq",), ("xa",), 128)
+    V(lambda e: e.tensor_scalar(T.xb[:, :], T.xa[:, :], 5, W - 1, OP.arith_shift_right, OP.bitwise_and), ("xa",), ("xb",), 128)
     for l in range(4):
-        V(lambda e, l=l: e.tensor_scalar(T.xa[:, l, :], T.sq[:, :], float((32 * KAP[l] - 592 * 592) % 65536), None, OP.add), ("sq",), ("xa%d" % l,), 128)
-        V(lambda e, l=l: e.tensor_scalar(T.xb[:, l, :], T.xa[:, l, :], 5, W - 1, OP.arith_shift_right, OP.bitwise_and), ("xa%d" % l,), ("xb%d" % l,), 128)
-        V(lambda e, l=l: e.tensor_copy(T.xl[:, 128 * l:128 * l + 128], T.xb[:, l, :]), ("xb%d" % l,), ("xl%d" % l,), 128)
+        V(lambda e, l=l: e.tensor_scalar(T.xl[:, 130 * l:130 * l + 130], T.xb[:, :], float((KAP[l] - KAP[0]) % W), None, OP.add), ("xb",), ("xl%d" % l,), 128)
         for c in range(TCH):
-            k0, k1 = 128 // TCH * c, 128 // TCH * (c + 1)
-            either(lambda e, l=l, k0=k0, k1=k1: gather_on(e, T.xt[:, W * l + 16 * k0:W * l + 16 * k1], T.xw[:, :].indirect(T.xl[:, 128 * l + k0:128 * l + k1])),
-                   ("xw", "xl%d" % l), ("x%d%d" % (l, c),), gat(16 * (k1 - k0)), "table")
+            k0, k1, x0 = 128 // TCH * c, 128 // TCH * (c + 1) + (c == TCH - 1), 2 * W + TW * l
+            either(lambda e, l=l, k0=k0, k1=k1, x0=x0: gather_on(e, T.xw[:, x0 + 16 * k0:x0 + 16 * k1], T.xw[:, 0:2 * W if l else W].indirect(T.xl[:, 130 * l + k0:130 * l + k1])),
+                   ("xw", "xl%d" % l) + (("xw2",) if l else ()), ("x%d%d" % (l, c),), gat(16 * (k1 - k0)), "table")
     either(lambda e: scale_on(e, T.nident[:, :], T.ident[:, :], -1.0), ("ident",), ("nident",), ("h", 128))
     either(lambda e: scale_on(e, T.z16[:, 15:128:16], T.bo[:, 0:128:16], 0.0625), ("bo",), ("z16",), 8)
     V(lambda e: e.tensor_scalar(col(WCOL), T.wti[:, :], 16.0, None, OP.mult), ("wti",), ("wcol",), 8)
@@ -222,26 +229,28 @@ def build(core, T, topo, VEC):
     A(lambda e: e.activation(T.cini[:, 40:48], T.cini[:, 32:40], AF.Identity, bias=col(THC), scale=-1.0), ("tini0", "thc"), ("tini1",), 8)
     V(lambda e: e.tensor_copy(T.bl[:, :], T.bli[:, :]), ("bli",), ("bl",), 16)
     V(lambda e: e.tensor_scalar(T.bow[:, :], T.bo[:, :], col(WCOL), 1.0 / 256, OP.mult, OP.mult), ("bo", "wcol"), ("bow",), 64)
+    for s in range(2 if TPE or BPE else 0):
+        either(lambda e, s=s: scale_on(e, T.i32[:, s, :], T.ident[:, :], 1.0 - 2 * s), ("ident",), ("i32%d" % s,), 128)
     KB = 16384.0 if SP else 64.0
     either(lambda e: scale_on(e, T.bo64[:, :], T.bo[:, :], KB), ("bo",), ("bo64",), ("h", 128))
     either(lambda e: scale_on(e, T.nbo64[:, :], T.bo[:, :], -KB), ("bo",), ("nbo64",), ("h", 128))
     if SP:
-        V(lambda e: e.memset(T.cmpc[:, 128:256], 1.0 / 64), (), ("cmpd",), 128)
-        V(lambda e: e.memset(T.cini[:, 48:56], 1.0 / 256), (), ("cini3",), 8)
+        either(lambda e: scale_on(e, T.hident[:, :], T.ident[:, :], -0.5), ("ident",), ("hident",), ("h", 128))
+        fill(T.cini[:, 48:56], 8, 1.0 / 256, "cini3")
         V(lambda e: e.tensor_scalar(T.cmpc[:, 0:128], T.prow[:, :], col(ICOL), -1000.0, OP.not_equal, OP.mult), ("prow", "icol"), ("cmpc",), 128)
     else:
         either(lambda e: scale_on(e, col(I16), col(ICOL), -16.0), ("icol",), ("i16",), 8)
         A(lambda e: e.activation(T.cmpc[:, 0:128], T.prow[:, :], AF.Identity, bias=col(I16)), ("prow", "i16"), ("cmpc",), 128)
     V(lambda e: e.tensor_scalar(T.diag[:, :], T.cmpc[:, 0:16], 0.0 if SP else 4.0, 256 / KB, OP.is_equal, OP.mult), ("cmpc",), ("diag",), 16)
-    V(lambda e: e.memset(T.cini[:, 8:24], -15.0 / 32), (), ("cini1",), 8)
-    V(lambda e: e.memset(T.cini[:, 24:32], 1.0 / 32), (), ("cini2",), 8)
+    fill(T.cini[:, 8:24], 16, -15.0 / 32, "cini1")
+    fill(T.cini[:, 24:32], 8, 1.0 / 32, "cini2")
     A(lambda e: e.activation(col(W16), col(ICOL), AF.Identity, bias=-15.0 / 32, scale=-0.0625), ("icol",), ("w16",), 8)
     either(lambda e: scale_on(e, T.cini[:, 0:8], T.ones[:, 0:8], col(W16)), ("ones", "w16"), ("cini0",), 8)
     A(lambda e: e.activation(col(GOC), col(ICOL), AF.Identity, bias=120.0), ("icol",), ("goc",), 8)
-    V(lambda e: e.memset(T.nn[:, 0:1], -13.0 / 32), (), ("nn",), 8)
-    V(lambda e: e.memset(T.ms[:, 256:272], 0.0), (), ("msz",), 16)
+    fill(T.nn[:, 0:1], 1, -13.0 / 32, "nn")
+    G(lambda e: e.iota(T.ms[:, 256:272], [[0, 16]], 0, 0, allow_small_or_imprecise_dtypes=True), (), ("msz",), 0.2)
     for h in range(0 if SP else 2):
-        V(lambda e, h=h: e.memset(T["qi_%d" % h][:, 24:32], 0), (), ("qiz_%d" % h,), 8)
+        G(lambda e, h=h: e.iota(T["qi_%d" % h][:, 24:32], [[0, 8]], 0, 0), (), ("qiz_%d" % h,), 0.2)
 
     def half(t, h):
         B = lambda n: T["%s_%d" % (n, h)]
@@ -264,8 +273,23 @@ def build(core, T, topo, VEC):
                   (k,) + wk + units("fa", x0, m), units("dc", x0, m), gat(m), note="gB")
             for la, lb, k, x0, m in pieces:
                 r = range(x0 % 512 // 128 * 2 + x0 // 512, (x0 % 512 + m) // 64, 2) if l == JOIN else range(x0 // 128, (x0 + m) // 128)
+                if (l, x0 // 512 if l else 0) in ICUT and x0 == pieces[-1][3]:
+                    for i0, name in ((0, "ac"), (1, "ad")):
+                        A(lambda e, x0=x0, m=m, r=r, i0=i0: e.activation(ac[:, r.start:r.stop:r.step, i0:128:2], dc[:, x0 + i0:x0 + m:2], AF.Abs),
+                          units("dc", x0, m), tuple(K("%s%d" % (name, u)) for u in r), m // 2, note="abs")
+                    continue
                 A(lambda e, x0=x0, m=m, r=r: e.activation(ac[:, r.start:r.stop:r.step, :], dc[:, x0:x0 + m], AF.Abs),
-                  units("dc", x0, m), tuple(K("ac%d" % u) for u in r), m, note="abs")
+                  units("dc", x0, m), tuple(K("%s%d" % (name, u)) for u in r for name in ("ac", "ad")), m, note="abs")
+
+        def gather_both(s, n, w, wk):
+            x0, out, kb = 512 * s, (F[:, 0:n] if s else S[:, 256:256 + n]), K("SF"[s])
+            either(lambda e: gather_on(e, fa[:, x0:x0 + 2 * n], w.indirect(lu[:, 64 * s:64 * s + n // 8])), (K("lu%d" % s),) + wk, units("fa", x0, 2 * n), gat(2 * n), "gAB")
+
+            def diff(e):
+                e.matmul(out, T.ident[:, :], fa[:, x0:x0 + n], True, False)
+                return e.matmul(out, T.nident[:, :], fa[:, x0 + n:x0 + 2 * n], False, True)
+            P(diff, units("fa", x0, 2 * n) + ("ident", "nident"), (K("S%d" % s),), 2 * n, (kb,), note="diff")
+            A(lambda e: e.activation(ac[:, 4 * s:4 * s + n // 128, :], out, AF.Abs), (K("S%d" % s),), units("ac", x0, n), n, (kb,), note="abs")
 
         def pieces(lst, c0, key, x0, n, ch):
             m, k = n // ch, n // ch // 16
@@ -282,24 +306,23 @@ def build(core, T, topo, VEC):
                 V(lambda e: e.tensor_copy(B("ib")[:, 0:n // 16], S[:, 0:n // 8:2]), (K("S0"),), (K("ib0"),), n // 16, (K("S"),), note="i0")
                 return
 
-            def fn(e):
-                for i in range(16):
-                    o = e.matmul(F[:, 256:256 + n // 16] if s else S[:, 0:n // 16], zs(T.zw, i), ac[:, 4 * s:4 * s + n // 128, i:128:16], i == 0, i == 15)
-                return o
-            P(fn, units("ac", 512 * s, n) + ("zw",), (K("S%d" % s),), 1024, (K("SF"[s]),), note="weigh")
+            for r in (range(0, 16, 2), range(1, 16, 2)) if (l, s) in ICUT else (range(16),):
+                def fn(e, r=r):
+                    for i in r:
+                        o = e.matmul(F[:, 256:256 + n // 16] if s else S[:, 0:n // 16], zs(T.zw, i), ac[:, 4 * s:4 * s + n // 128, i:128:16], i == 0, i == 15)
+                    return o
+                P(fn, units("ac", 512 * s, n) + units("ad", 512 * s, n) * (15 in r) + ("zw",), (K("S%d" % s),), 64 * len(r), (K("SF"[s]),), note="weighe" if r.start else "weigh")
 
-        def index(src, ks, bank, c0, n, wr, two=False):
+        def index(l, src, ks, bank, c0, n, wr, two=False):
             ka, kb = K("ia%d" % (c0 // 64)), K("ib%d" % (c0 // 64))
-            if two:
-                V(lambda e: e.tensor_tensor(B("ia")[:, 0:n], S[:, 1:2 * n:2], B("ib")[:, 0:n], OP.min), (ks, kb), (ka,), n, bank, note="i1")
-            else:
-                V(lambda e: e.tensor_copy(B("ia")[:, c0:c0 + n], src), (ks,), (ka,), n, bank, note="i1")
-            V(lambda e: e.tensor_scalar(B("ib")[:, c0:c0 + n], B("ia")[:, c0:c0 + n], W - 1, None, OP.bitwise_and), (ka,), (kb,), n, note="i2")
-            V(lambda e: e.tensor_copy(lu[:, c0:c0 + n], B("ib")[:, c0:c0 + n]), (kb,), wr, n, note="i3")
+            V(lambda e: e.tensor_scalar(B("ia")[:, c0:c0 + n], src, BIG, BIG + W, OP.add, OP.subtract), (ks,), (ka,), n, bank, note="i1")
+            V(lambda e: e.tensor_tensor(lu[:, c0:c0 + n], src, B("ia")[:, c0:c0 + n], OP.subtract), (ka, ks), wr, n, bank, note="i2")
 
-        table = lambda l: (T.xt[:, W * l:W * l + W], tuple("x%d%d" % (l, c) for c in range(TCH)))
+        def table(l):
+            keys = tuple("x%d%d" % (k, c) for k in (l - 1, l) for c in range(TCH) if k >= 0)
+            return T.xw[:, 2 * W + TW * l - W // 2:2 * W + TW * (l + 1)], keys + ("xw2",)
 
-        gather_pair(0, pieces(lt, 0, "lt%d%d" % (t, h), 0, 1024, CH[0]), T.xw[:, :], ("xw",))
+        gather_pair(0, pieces(lt, 0, "lt%d%d" % (t, h), 0, 1024, CH[0]), T.xw[:, 0:W], ("xw",))
 
         def rows(bank, src, first, last):
             def fn(e):
@@ -312,17 +335,19 @@ def build(core, T, topo, VEC):
         P(rows(X, fa, True, True), fk + ("ident", "nident"), (K("X"),), 1024, (K("X"),), note="row0")
         P(rows(Y, fa, True, False), fk + ("ident", "nident"), (K("Y"),), 1024, (K("Y"),), note="row1")
         P(rows(Y, dc, False, True), dk + ("ident", "nident"), (K("Y"),), 1024, (K("Y"),), note="row2")
-        for ph, (bank, kk) in enumerate(((X, K("X")), (Y, K("Y")))):
-            A(lambda e, ph=ph, bank=bank: e.activation(ar[:, ph, :], bank[:, :, :], AF.Abs), (kk,), (K("ar%d" % ph),), 512, (kk,), note="absr")
+        for p0, p1 in RCUT:
+            bank, kk = (X, Y)[p0 // 8], K("XY"[p0 // 8])
+            A(lambda e, p0=p0, p1=p1, bank=bank: e.activation(ar[:, p0 // 8, p0 % 8 * 64:(p1 - p0 + p0 % 8) * 64], bank[:, p0 % 8:p1 - p0 + p0 % 8, :], AF.Abs),
+              (kk,), (K("ar%d" % p0),), 64 * (p1 - p0), (kk,), note="absr")
         weigh(0, 1024)
-        for ph in range(2):
-            def wrow(e, ph=ph):
-                for pl in range(8):
-                    o = e.matmul(F[:, 256:320], zs(T.zw, 8 * ph + pl), ar[:, ph, 64 * pl:64 * pl + 64], ph + pl == 0, 8 * ph + pl == 15)
+        for p0, p1 in RCUT:
+            def wrow(e, p0=p0, p1=p1):
+                for p in range(p0, p1):
+                    o = e.matmul(F[:, 256:320], zs(T.zw, p), ar[:, p // 8, p % 8 * 64:p % 8 * 64 + 64], p == 0, p == 15)
                 return o
-            P(wrow, ("zw", K("ar%d" % ph)), (K("S1"),), 512, (K("F"),), note="weighr")
-        index(S[:, 0:64], K("S0"), (K("S"),), 0, 64, (K("lu0"),))
-        index(F[:, 256:320], K("S1"), (K("F"),), 64, 64, (K("lu1"),))
+            P(wrow, ("zw", K("ar%d" % p0)), (K("S1"),), 64 * (p1 - p0), (K("F"),), note="weighr")
+        index(0, S[:, 0:64], K("S0"), (K("S"),), 0, 64, (K("lu0"),))
+        index(0, F[:, 256:320], K("S1"), (K("F"),), 64, 64, (K("lu1"),))
 
         Z, GD, D, kZ, kD, nz = X[:, 7, :], Y[:, 7, 0:16], Y[:, 7, 8:16], K("X"), K("Y"), 24 if SP else 32
         P(lambda e: e.matmul(Z[:, 0:nz], T.ident[:, :], T.cini[:, 0:nz], True, False), ("ident", "cini0", "cini1", "cini2"), (K("Z"),), 64, (kZ,), note="zini")
@@ -335,16 +360,19 @@ def build(core, T, topo, VEC):
         for l, n in ((1, 512), (2, 256), (3, 128)):
             if l < JOIN:
                 for s in range(2):
-                    gather_pair(l, pieces(lu, 64 * s, K("lu%d" % s), 512 * s, n, CH[l] // 2), *table(l - 1))
+                    if (l, s) in PL:
+                        gather_both(s, n, *table(l - 1))
+                    else:
+                        gather_pair(l, pieces(lu, 64 * s, K("lu%d" % s), 512 * s, n, CH[l] // 2), *table(l - 1))
                     weigh(l, n, s)
-                    index(F[:, 256:256 + n // 16] if s else S[:, 0:n // 16], K("S%d" % s), (K("SF"[s]),), 64 * s, n // 16, (K("lu%d" % s),))
+                    index(l, F[:, 256:256 + n // 16] if s else S[:, 0:n // 16], K("S%d" % s), (K("SF"[s]),), 64 * s, n // 16, (K("lu%d" % s),))
                 continue
             if l > JOIN:
                 gather_pair(l, pieces(lu, 0, K("lu0"), 0, 2 * n, CH[l]), *table(l - 1))
             else:
                 gather_pair(l, [p for s in range(2) for p in pieces(lu, 64 * s, K("lu%d" % s), 512 * s, n, CH[l] // 2)], *table(l - 1))
             weigh(l, 2 * n)
-            index(S[:, 0:n // 8], K("S0"), (K("S"),), 0, n // 8, (K("lu0"),), l in HALF)
+            index(l, S[:, 0:n // 8], K("S0"), (K("S"),), 0, n // 8, (K("lu0"),), l in HALF)
 
         w, wk = table(3)
         wd, qi, fr, nn = B("wd"), B("qi"), B("fr"), T.nn
@@ -381,7 +409,7 @@ def build(core, T, topo, VEC):
             e.matmul(Act, T.nbo64[:, :], nn[:, 8 * h + 1:8 * h + 9], False, False)
             if SP:
                 return e.matmul(Act, T.nbo64[:, :], T.cini[:, 48:56], False, True)
-            return e.matmul(Act, T.ident[:, :], B("sn")[:, :], False, True)
+            return e.matmul(Act, T.ident[:, :], B("sn")[:, :], False, not ZA)
         Act, kA = (X[:, 6, 0:8], K("X")) if SP else (F[:, 0:8], K("F"))
         P(act, ("nn", "nn0", "nn%d" % h, K("sn"), "bo64", "nbo64", "ident", "cini3"), (K("Fa"),), 192, (kA,), note="act")
         qa = T["qr%d" % t][:, 8 * h:8 * h + 8]
@@ -391,8 +419,23 @@ def build(core, T, topo, VEC):
             V(lambda e: e.tensor_tensor(B("zz")[:, :], GD[:, 0:8], fr[:, 32:40], OP.mult), (K("D"), K("qa")), (K("zz"),), 8, (kD,), note="zz")
         V(lambda e: e.tensor_tensor(qa, D, fr[:, 16:24], OP.is_gt), (K("D"), K("fr")), ("qr%d%d" % (t, h),), 8, (kD,), note="qr" if SP else "qa")
         neg = t == 2
-        V(lambda e: e.tensor_tensor(B("tb")[:, :], cw[:, :].indirect(B("go")[:, :]), bn, OP.add if neg else OP.subtract), ("cw%d" % t, K("go"), kbn), (K("tb"),), gat(128), note="T")
-        if not SP:
+        onpe = TPE and t > 0
+        if onpe:
+            either(lambda e: gather_on(e, B("tb")[:, :], cw[:, :].indirect(B("go")[:, :])), ("cw%d" % t, K("go")), (K("tb"),), gat(128), "T")
+
+            def less(e):
+                e.matmul(Y[:, 0:2, :], T.i32[:, 0 if neg else 1, :], bn, True, False)
+                return e.matmul(Y[:, 0:2, :], T.i32[:, 0, :], B("tb")[:, :], False, True)
+            P(less, (K("tb"), kbn, "i320", "i321"), (K("Y"),), 1024, (K("Y"),), note="Tp")
+        else:
+            V(lambda e: e.tensor_tensor(B("tb")[:, :], cw[:, :].indirect(B("go")[:, :]), bn, OP.add if neg else OP.subtract), ("cw%d" % t, K("go"), kbn), (K("tb"),), gat(128), note="T")
+        if ZA:
+            P(lambda e: e.matmul(Act, T.ident[:, :], qa, False, True), (K("Fa"), "qr%d%d" % (t, h)), (K("Fb"),), 64, (kA,), note="act2")
+
+            def zcopy(e):
+                return e.tensor_copy(B("zz")[:, :], Act) if e is VEC[0] else e.activation(B("zz")[:, :], Act, AF.Identity)
+            A(zcopy, (K("Fb"),), (K("zz"),), 8, (K("F"),), note="zz")
+        elif not SP:
             V(lambda e: e.tensor_tensor(B("zz")[:, :], Act, qa, OP.add), (K("Fa"), "qr%d%d" % (t, h)), (K("zz"),), 8, (K("F"),), note="zz")
         spread = B("zz")[:, 0:8].indirect(T.bl[:, 0:8])
 
@@ -401,7 +444,8 @@ def build(core, T, topo, VEC):
                 return e.tensor_scalar(B("ee")[:, 128:256], spread, 6.0, None, OP.is_equal)
             return e.activation(B("ee")[:, 128:256], spread, AF.Relu, bias=-5.0)
         if SP:
-            V(lambda e: e.tensor_tensor(B("ee")[:, :], B("zz")[:, 0:8].indirect(T.bl[:, :]), T.cmpc[:, :], OP.is_lt), (K("zz"), "bl", "cmpc", "cmpd"), (K("er"), K("ec")), gat(256), note="er")
+            V(lambda e: e.tensor_tensor(B("ee")[:, 0:128], spread, T.cmpc[:, 0:128], OP.is_lt), (K("zz"), "bl", "cmpc"), (K("er"),), gat(128), note="er")
+            A(lambda e: e.activation(B("ee")[:, 128:256], spread, AF.Sign, bias=-1.0 / 64), (K("zz"), "bl"), (K("ec"),), gat(128), note="ec")
         else:
             V(lambda e: e.tensor_tensor(B("ee")[:, 0:128], spread, T.cmpc[:, 0:128], OP.is_equal), (K("zz"), "bl", "cmpc"), (K("er"),), gat(128), note="er")
             either(colmask, (K("zz"), "bl"), (K("ec"),), gat(128), "ec")
@@ -409,25 +453,40 @@ def build(core, T, topo, VEC):
 
         def xm(e):
             e.matmul(Xm, T.bo[:, :], B("ee")[:, 0:128], True, False)
-            return e.matmul(Xm, (T.ident if SP else T.nident)[:, :], B("ee")[:, 128:256], False, True)
-        P(xm, (K("er"), K("ec"), "bo", "nident"), (K("X"),), 256, (K("X"),), note="X")
-        if t == 0:
-            V(lambda e: e.tensor_scalar(M, Xm, float(SP), -1.0, OP.not_equal, OP.mult), (K("X"),), (K("Y"),), 128, (K("X"), K("Y")), note="M")
-        else:
-            A(lambda e: e.activation(M, Xm, AF.Abs, bias=-float(SP)), (K("X"),), (K("Y"),), 128, (K("X"), K("Y")), note="M")
+            return e.matmul(Xm, (T.hident if SP else T.nident)[:, :], B("ee")[:, 128:256], False, True)
+        P(xm, (K("er"), K("ec"), "bo", "nident", "hident"), (K("X"),), 256, (K("X"),), note="X")
         b3, kb3 = T["b3%d%d" % (t, h)], "b3%d%d" % (t, h)
         ms = T.ms[:, 128 * h:128 * h + 128]
-        if BPS and t < R - 1:
-            mp = Y[:, 2:4, :]
-            V(lambda e: e.tensor_tensor(mp, B("tb")[:, :], M, OP.mult), (K("tb"), K("Y")), (K("mp"),), 128, (K("Y"),), note="MT")
-            V(lambda e: e.tensor_tensor(b3[:, :], bn, mp, OP.add if t == 1 else OP.subtract), (kbn, K("mp")), (kb3,), 128, (K("Y"),), note="B")
-            A(lambda e: e.activation(ms, mp, AF.Identity), (K("mp"),), (K("ms"),), 128, (K("Y"),), note="MS")
+        if onpe:
+            A(lambda e: e.activation(B("mk")[:, :], Xm, AF.Abs, bias=-0.5 * SP), (K("X"),), (K("mk"),), 128, (K("X"),), note="M")
+            a, b, ks = M, B("mk")[:, :], (K("mk"), K("Y"))
         else:
-            V(lambda e: e.tensor_tensor(ms, B("tb")[:, :], M, OP.mult), (K("tb"), K("Y")), (K("ms"),), 128, (K("Y"),), note="MT")
-            V(lambda e: e.tensor_tensor(b3[:, :], bn, ms, OP.add if t == 1 else OP.subtract), (kbn, K("ms")), (kb3,), 256, note="B")
+            A(lambda e: e.activation(M, Xm, AF.Abs, bias=-0.5 * SP), (K("X"),), (K("Y"),), 128, (K("X"), K("Y")), note="M")
+            a, b, ks = B("tb")[:, :], M, (K("tb"), K("Y"))
+        if t in BPE:
+            V(lambda e: e.tensor_tensor(ms, a, b, OP.mult), ks, (K("ms"),), 128, (K("Y"),), note="MT")
+            P(lambda e: e.matmul(S[:, 128:256], T.i32[:, 0, :], bn, True, False), (kbn, "i320"), (K("S0"),), 512, (K("S"),), note="B0")
+            P(lambda e: e.matmul(S[:, 128:256], T.i32[:, t - 1, :], ms, False, True), (K("ms"), "i320", "i321"), (K("S0"),), 512, (K("S"),), note="Bp")
+            A(lambda e: e.activation(b3[:, :], S[:, 128:256], AF.Identity), (K("S0"),), (kb3,), 128, (K("S"),), note="B")
+        elif t < R - 1 and LS:
+            mb, kmb = (ms, K("ms")) if t else (B("mk")[:, :], K("mk"))
+            V(lambda e: e.tensor_tensor(mb, a, b, OP.mult), ks, (kmb,), 128, (K("Y"),), note="MT")
+            V(lambda e: e.tensor_tensor(T["ls%d%d" % (t, h)][:, :], mb.indirect(T.pm[:, :]), lt[:, :], OP.add), (kmb, "pm", "lt%d%d" % (t, h)), ("ls%d%d" % (t, h),), gat(128), note="ls")
+            V(lambda e: e.tensor_tensor(b3[:, :], bn, mb, OP.add), (kbn, kmb), (kb3,), 256, note="B")
+            if t == 0:
+                A(lambda e: e.activation(ms, mb, AF.Identity, scale=-1.0), (kmb,), (K("ms"),), 128, note="MS")
+        elif t < R - 1:
+            mp = Y[:, 2:4, :]
+            V(lambda e: e.tensor_tensor(mp, a, b, OP.mult), ks, (K("mp"),), 128, (K("Y"),), note="MT")
+            V(lambda e: e.tensor_tensor(b3[:, :], bn, mp, OP.add), (kbn, K("mp")), (kb3,), 128, (K("Y"),), note="B")
+            A(lambda e: e.activation(ms, mp, AF.Identity, scale=1.0 if t else -1.0), (K("mp"),), (K("ms"),), 128, (K("Y"),), note="MS")
+        else:
+            V(lambda e: e.tensor_tensor(ms, a, b, OP.mult), ks, (K("ms"),), 128, (K("Y"),), note="MT")
+            V(lambda e: e.tensor_tensor(b3[:, :], bn, ms, OP.subtract), (kbn, K("ms")), (kb3,), 256, note="B")
         if t < R - 1:
             ls = T["ls%d%d" % (t, h)]
-            V(lambda e: e.tensor_copy(ls[:, :], b3[:, :].indirect(T.pm[:, :])), (kb3, "pm"), ("ls%d%d" % (t, h),), gat(128), note="ls")
+            if not LS:
+                V(lambda e: e.tensor_copy(ls[:, :], b3[:, :].indirect(T.pm[:, :])), (kb3, "pm"), ("ls%d%d" % (t, h),), gat(128), note="ls")
             dst = T.cores[(T.rank_of(core) + HOP) % len(T.cores)]
             rid, pid, _ = topo.addr(dst)
             engines = topo.engines(core, dst)
@@ -609,6 +668,170 @@ def schedule(ops, tries):
     starts = [improved([r + d * (c % 2 if c >= 0 else 0) for r, c in zip(rank, cls)], pick, tries // 8) for d in (-2, -1, 0, 1)]
     _, rank, pick, order, sp = improved(*min(starts, key=lambda s: s[0])[1:3], tries // 2)
     return order, spans(order, pick)[1], pick, (base, sp)
+
+
+def schedule(ops, tries):
+    n, names = len(ops), ("A", "V", "P", "G", "Y", None)
+    home = [names.index({"Q": "A", "AV": "A"}.get(o["q"], o["q"])) for o in ops]
+    took = [[[cost(q, o["c"], C) for q in "AV"] if o["q"] == "AV" else [cost(o["q"], o["c"], C)] * 6 for o in ops] for C in COSTS]
+    dma = [o["q"] in ("Y", "Q") for o in ops]
+    hops = [[[hop(a, b, C) for b in names] for a in names] for C in COSTS]
+    waits, after = [sorted(o["deps"]) for o in ops], [sorted(o["order"]) for o in ops]
+    succ, needs = [[] for _ in range(n)], [len(a) + len(b) for a, b in zip(waits, after)]
+    for i in range(n):
+        for d in waits[i]:
+            succ[d].append((i, 2))
+        for d in after[i]:
+            succ[d].append((i, 1))
+        if "after" in ops[i]:
+            succ[ops[i]["after"]].append((i, 0))
+            needs[i] += 1
+    c0, cls, way, plan = took[0], [o.get("cls", -1) for o in ops], [0.0] * n, [0.0] * n
+    for i in range(n - 1, -1, -1):
+        way[i] = min(c0[i]) + max([way[s] + 0.15 * (k == 2) for s, k in succ[i] if cls[s] == cls[i]] or [0.0])
+    top = {k: max(way[i] for i in range(n) if cls[i] == k) for k in set(cls)}
+    for i in range(n - 1, -1, -1):
+        if cls[i] < 0:
+            plan[i] = min([plan[s] for s, _ in succ[i]] or [100.0]) - min(c0[i]) - 0.5
+        elif succ[i] and all(cls[s] != cls[i] for s, _ in succ[i]):
+            plan[i] = min(plan[s] for s, _ in succ[i]) - 2
+        else:
+            plan[i] = STRETCH * (top[cls[i]] - way[i]) + PERIOD * (cls[i] // 2) + LAG * (cls[i] % 2)
+    first = [i for i in range(n) if needs[i] == 0]
+    free_to_choose = [i for i in range(n) if ops[i]["q"] == "AV"]
+
+    def listed(rank, on, hold):
+        est, order, need, last = hold[:], [], needs[:], 0.0
+        free, low, ready, h0 = [0.0] * 5, [1e9] * 5, [[] for _ in range(5)], hops[0]
+        for i in first:
+            ready[on[i]].append(i)
+            low[on[i]] = min(low[on[i]], est[i])
+        while True:
+            q, t = -1, 1e8
+            for e in range(5):
+                r = low[e]
+                if r < free[e]:
+                    r = free[e]
+                if r < t:
+                    q, t = e, r
+            if q < 0:
+                return order, last
+            lst = ready[q]
+            if len(lst) == 1:
+                i = lst.pop()
+                low[q] = 1e9
+            else:
+                b, i, lim = 1e9, -1, t + 0.005
+                for j in lst:
+                    if rank[j] < b and est[j] <= lim:
+                        b, i = rank[j], j
+                lst.remove(i)
+                low[q] = min([est[j] for j in lst])
+            r = est[i] if est[i] > t else t
+            free[q] = r + (0.06 if dma[i] else c0[i][q])
+            todo = [(i, r)]
+            while todo:
+                i, r = todo.pop()
+                order.append(i)
+                q = on[i]
+                x, wake = r + c0[i][q], h0[q]
+                if x > last:
+                    last = x
+                for s, k in succ[i]:
+                    h = x + wake[on[s]] if k == 2 else x if k else r
+                    if h > est[s]:
+                        est[s] = h
+                    need[s] -= 1
+                    if not need[s]:
+                        e = on[s]
+                        if e == 5:
+                            todo.append((s, est[s]))
+                        else:
+                            ready[e].append(s)
+                            if est[s] < low[e]:
+                                low[e] = est[s]
+
+    def span(order, on, k):
+        wake, cc, done, free = hops[k], took[k], [0.0] * n, [0.0] * 6
+        for i in order:
+            q = on[i]
+            r = free[q]
+            for d in waits[i]:
+                x = done[d] + wake[on[d]][q]
+                if x > r:
+                    r = x
+            for d in after[i]:
+                if done[d] > r:
+                    r = done[d]
+            done[i] = x = r + cc[i][q]
+            if q < 5:
+                free[q] = r + 0.06 if dma[i] else x
+        return done
+
+    base = [max(span(listed(plan, home, [0.0] * n)[0], home, k)) for k in range(len(COSTS))]
+
+    def held_up(order, on):
+        done, before, last, out = span(order, on, 0), {}, [-1] * 6, []
+        for i in order:
+            before[i], last[on[i]] = last[on[i]], i
+        j = done.index(max(done))
+        while j >= 0:
+            q = on[j]
+            t, i = max([(done[d] + hops[0][on[d]][q], d) for d in waits[j]] + [(done[d], d) for d in after[j]] + [(0.0, -1)])
+            if t < done[j] - c0[j][q] - 0.01 and q < 5:
+                i = before[j]
+                out.append((i, j, t))
+            j = i
+        return [x for x in out if x[0] >= 0]
+
+    def improved(rank, on, hold, tries, seed, guide=0.0):
+        rng = np.random.default_rng(seed)
+        order, now = listed(rank, on, hold)
+        cur = sum(max(span(order, on, k)) / b for k, b in enumerate(base))
+        best, jam = (cur, rank, on, hold, order), held_up(order, on)
+        for k in range(tries):
+            s2, p2, h2, u = rank[:], on, hold, rng.random()
+            if rng.random() < guide and jam:
+                i, j, t = jam[int(rng.integers(len(jam)))]
+                s2[j] = min(s2[j], s2[i] - 0.01)
+                if u < 0.6:
+                    h2 = hold[:]
+                    h2[i] = t + 0.01
+                elif u < 0.8 and ops[i]["q"] == "AV":
+                    p2 = on[:]
+                    p2[i] ^= 1
+            elif u < 0.05:
+                h2 = hold[:]
+                for i in rng.integers(0, n, 40).tolist():
+                    h2[i] = 0.0
+            elif u < 0.55:
+                for i, d in zip(rng.integers(0, n, (1, 2, 4, 10)[k % 4]).tolist(), rng.normal(0.0, 0.5, 10).tolist()):
+                    s2[i] += d
+            elif u < 0.7:
+                a, d = int(rng.integers(0, n)), float(rng.normal(0.0, 0.5))
+                for i in range(a, min(n, a + int(rng.integers(5, 60)))):
+                    s2[i] += d
+            else:
+                p2 = on[:]
+                for i in rng.integers(0, len(free_to_choose), 1 + k % 2).tolist():
+                    p2[free_to_choose[i]] ^= 1
+            order, end = listed(s2, p2, h2)
+            if guide:
+                end = max(span(order, p2, 0))
+            if end > 1.006 * now:
+                continue
+            f, lim = end / base[0], cur + HEAT * (1 - k / tries) * rng.random()
+            for j in range(1, len(base)):
+                f += max(span(order, p2, j)) / base[j]
+            if f < lim:
+                cur, rank, on, hold, now, jam = f, s2, p2, h2, end, held_up(order, p2) if guide else []
+                if f < best[0]:
+                    best = (f, rank, on, hold, order)
+        return best
+    starts = [improved([r + d * (c % 2 if c >= 0 else 0) for r, c in zip(plan, cls)], home, [0.0] * n, tries // PART, SEED + d + 2) for d in (-2, -1, 0, 1)]
+    _, rank, on, hold, order = improved(*min(starts, key=lambda s: s[0])[1:4], tries - 4 * (tries // PART), SEED + 9)
+    pick = ["AV"[q] if o["q"] == "AV" else o["q"] for o, q in zip(ops, on)]
+    return order, span(order, on, 0), pick, (base, [max(span(order, on, k)) for k in range(len(COSTS))])
 
 
 _CACHE = {}

@@ -1,6 +1,5 @@
 import numpy as np
-from concourse.mybir import dt, AluOpType, AxisListType, ActivationFunctionType
-import comms_topo
+from concourse.mybir import AluOpType, ActivationFunctionType
 
 OP = AluOpType
 AF = ActivationFunctionType
@@ -28,25 +27,16 @@ SCRATCH = {
     "ones": ("sbuf", [128, 128], "bfloat16"),
     "m1": ("sbuf", [128, 128], "bfloat16"),
     "bo": ("sbuf", [128, 128], "bfloat16"),
-    "bo64": ("sbuf", [128, 128], "bfloat16"),
-    "nbo64": ("sbuf", [128, 128], "bfloat16"),
+    "bok": ("sbuf", [128, 128], "bfloat16"),
+    "nbok": ("sbuf", [128, 128], "bfloat16"),
     "bow": ("sbuf", [128, 128], "bfloat16"),
     "ident": ("sbuf", [128, 128], "bfloat16"),
     "nident": ("sbuf", [128, 128], "bfloat16"),
     "zw": ("sbuf", [128, 144], "bfloat16"),
-    "i32": ("sbuf", [128, 2, 128], "float32"),
-    "hident": ("sbuf", [128, 128], "bfloat16"),
-    "z2": ("sbuf", [128, 144], "bfloat16"),
-    "far": ("sbuf", [128, 32, 2], "bfloat16"),
     "z16": ("sbuf", [128, 144], "bfloat16"),
-    "prow": ("sbuf", [128, 128], "float32"),
-    "cmpc": ("sbuf", [128, 256], "float32"),
+    "prow": ("sbuf", [128, 16], "float32"),
     "diag": ("sbuf", [128, 16], "bfloat16"),
     "cini": ("sbuf", [128, 56], "bfloat16"),
-    "bli": ("sbuf", [128, 16], "int32"),
-    "bl": ("sbuf", [128, 16], "uint16"),
-    "pmi": ("sbuf", [128, 8], "int32"),
-    "pm": ("sbuf", [128, 8], "uint16"),
     "nn": ("sbuf", [128, 24], "bfloat16"),
     "nd": ("sbuf", [128, 16], "bfloat16"),
     "ns": ("sbuf", [128, 8], "float32"),
@@ -56,30 +46,27 @@ SCRATCH = {
     "qs": ("sbuf", [128, 16], "float32"),
     "qf": ("sbuf", [128, 16], "float32"),
 }
+for _t in range(R + 1):
+    SCRATCH["cw%d" % _t] = ("sbuf", [128, 256], "float32")
 for _t in range(R):
-    SCRATCH["qr%d" % _t] = ("sbuf", [128, 16], "bfloat16")
-    SCRATCH["cw%d" % (_t + 1)] = ("sbuf", [128, 256], "float32")
+    SCRATCH["qr%d" % _t] = ("sbuf", [128, 2, 16], "bfloat16")
     for _h in range(2):
         SCRATCH["lt%d%d" % (_t, _h)] = ("sbuf", [128, 128], "uint16")
-        SCRATCH["b3%d%d" % (_t, _h)] = ("sbuf", [128, 128], "float32")
-        if _t > 0:
-            SCRATCH["bn%d%d" % (_t, _h)] = ("sbuf", [128, 128], "float32")
-        if _t < R - 1:
-            SCRATCH["ls%d%d" % (_t, _h)] = ("sbuf", [128, 128], "uint16")
+        SCRATCH["ls%d%d" % (_t, _h)] = ("sbuf", [128, 128], "uint16" if _t < R - 1 else "float32")
 for _h in range(2):
-    for _n, _s, _d in (("fa", [128, 1024], "bfloat16"), ("dc", [128, 1024], "bfloat16"), ("ac", [128, 8, 128], "bfloat16"),
-                       ("ar", [128, 2, 512], "bfloat16"), ("ia", [128, 128], "float32"), ("lu", [128, 128], "uint16"),
-                       ("wd", [128, 3, 128], "bfloat16"), ("qi", [128, 32], "int32"), ("fr", [128, 40], "float32"),
-                       ("go", [128, 8], "uint16"), ("sn", [128, 8], "bfloat16"), ("tb", [128, 128], "float32"),
-                       ("zz", [128, 8], "float32"), ("mk", [128, 128], "float32"), ("ee", [128, 256], "bfloat16")):
+    for _n, _s, _d in (("fa", [128, 2048], "bfloat16"), ("dc", [128, 1024], "bfloat16"), ("ac", [128, 16, 128], "bfloat16"),
+                       ("ia", [128, 128], "float32"), ("lu", [128, 128], "uint16"),
+                       ("wd", [128, 3, 128], "bfloat16"), ("qi", [128, 24], "int32"), ("fr", [128, 32], "float32"),
+                       ("go", [128, 8], "uint16"), ("rr", [128, 8], "float32"), ("tb", [128, 128], "float32"),
+                       ("lo", [128, 8], "uint16"), ("wm", [128, 32], "float32")):
         SCRATCH["%s_%d" % (_n, _h)] = ("sbuf", _s, _d)
     for _n in ("S", "F"):
-        SCRATCH["%s_%d" % (_n, _h)] = ("psum", [128, 512], "float32")
-    for _n in ("X", "Y"):
-        SCRATCH["%s_%d" % (_n, _h)] = ("psum", [128, 8, 64], "float32")
+        SCRATCH["%s_%d" % (_n, _h)] = ("psum", [128, 64, 8], "float32")
+for _k in range(4):
+    SCRATCH["X%d" % _k] = ("psum", [128, 8, 64], "float32")
 
-DMAS = ["ld%d" % _k for _k in range(8)] + ["st%d" % _k for _k in range(4)]
-SEMAPHORES = ["V", "A", "P", "G", "sent"] + DMAS + ["%s%d%d" % (_a, _t, _h) for _a in ("al", "ab") for _t in (1, 2) for _h in (0, 1)]
+DMAS = ["ld%d" % _k for _k in range(7)] + ["st%d" % _k for _k in range(4)]
+SEMAPHORES = ["V", "A", "P", "G", "sent"] + DMAS + ["al%d%d" % (_t, _h) for _t in (1, 2) for _h in (0, 1)]
 
 COSTS = ({"cy": 0.00083, "V": 0.04, "A": 0.06, "P": 0.00048, "g": 1.56, "hop": (0.19, 0.15, 0.14), "dma": 0.8},
          {"cy": 0.00104, "V": 0.04, "A": 0.07, "P": 0.00056, "g": 1.3, "hop": (0.20, 0.17, 0.17), "dma": 0.8},
@@ -105,18 +92,17 @@ def cost(q, n, c):
     return c[q] + max(64, n) * c["cy"]
 
 
-CH = (2, 4, 2, 2)
-JOIN, HALF, FIRST = 4, (), 0.6
-RCUT, ICUT, LS = ((0, 8), (8, 16)), (), True
-TPE, SP, TCH, PL, ZA, BPE = False, False, 4, (), False, ()
-PERIOD, LAG, STRETCH, HEAT, PART = 23.0, 5.0, 1.15, 0.006, 8
-SEED, TRIES = 7, 12000
+OPT = {"CH": (4, 2, 1, 1),
+       "J0": False, "TCH": 4, "FIRST": 0.6,
+       "PERIOD": 22.0, "LAG": 3.0, "LAGS": (-1, 0, 1), "STRETCH": 1.15, "HEAT": 0.006, "PART": 8, "SEED": 7, "TRIES": 1200,
+       "MOVES": 120000, "WARM": 0.002}
 
 
 def build(core, T, topo, VEC):
     ops, lastw, readers, banks = [], {}, {}, {}
+    CH, TCH = OPT["CH"], OPT["TCH"]
 
-    def add(q, fn, rd=(), wr=(), bk=(), c=0.1, sem=None, n=1, note=""):
+    def add(q, fn, rd=(), wr=(), bk=(), c=0.1, sem=None, n=1, note="", acc=False):
         deps, order = set(), set()
         for k in rd:
             if k in lastw:
@@ -138,7 +124,7 @@ def build(core, T, topo, VEC):
             readers.setdefault(k, []).append(me)
         for b in bk:
             banks.setdefault(b, {})[q] = me
-        if note in ("row2", "weighr", "weighe", "D", "act2", "Bp"):
+        if acc:
             order |= {d for d in deps if ops[d]["q"] == "P"}
             deps -= order
         ops.append({"q": q, "fn": fn, "deps": deps, "order": order - deps, "c": c, "sem": sem, "n": n, "note": note})
@@ -150,8 +136,8 @@ def build(core, T, topo, VEC):
     def A(fn, rd, wr, n, bk=(), note=""):
         return add("A", fn, rd, wr, bk, n, note=note)
 
-    def P(fn, rd, wr, n, bk=(), note=""):
-        return add("P", fn, rd, wr, bk, n, note=note)
+    def P(fn, rd, wr, n, bk=(), note="", acc=False):
+        return add("P", fn, rd, wr, bk, n, note=note, acc=acc)
 
     def G(fn, rd, wr, c, note=""):
         return add("G", fn, rd, wr, (), c, note=note)
@@ -166,45 +152,41 @@ def build(core, T, topo, VEC):
             return e.tensor_copy(out, ind)
         return e.activation(out, ind, AF.Identity)
 
-    def scale_on(e, out, in_, s):
+    def scale_on(e, out, in_, s, b=None):
         if e is VEC[0]:
-            return e.tensor_scalar(out, in_, s, None, OP.mult)
-        return e.activation(out, in_, AF.Identity, scale=s)
+            return e.tensor_scalar(out, in_, s, None, OP.mult) if b is None else e.tensor_scalar(out, in_, s, b, OP.mult, OP.add)
+        return e.activation(out, in_, AF.Identity, scale=s) if b is None else e.activation(out, in_, AF.Identity, bias=b, scale=s)
 
     def either(fn, rd, wr, n, note=""):
         add("AV", fn, rd, wr, (), n, note=note)
 
-    prev = load("Y", 0, T.bni[:, 0:128], T.bn[:, 0:128], ("bn00",), 2.2)
+    prev = load("Y", 0, T.bni[:, 0:128], T.bn[:, 0:128], ("bn0",), 2.2)
     load("Q", 1, T.xw[:, 0:W], T.xf[:, :], ("xw",), 4.0)
-    for k, out, in_, key, c in ((2, T.wti[:, :], T.wt[:, :], "wti", 4.2), (4, T.bni[:, 128:256], T.bn[:, 128:256], "bn01", 4.5),
+    for k, out, in_, key, c in ((2, T.wti[:, :], T.wt[:, :], "wti", 4.2), (4, T.bni[:, 128:256], T.bn[:, 128:256], "bn1", 4.5),
                                 (6, T.xw[:, W:2 * W], T.xf[:, :], "xw2", 7.0),
-                                (3, T.thi[:, :], T.th[:, :], "thi", 7.2), (5, T.cni[:, :], T.cn[:, :], "cw0", 7.7)):
+                                (3, T.thi[:, :], T.th[:, :], "thi", 7.2), (5, T.cni[:, :], T.cn[:, :], "cni", 7.7)):
         o = load("Y", k, out, in_, (key,), c)
         ops[o]["after"] = prev
         prev = o
 
     col = lambda k: T.col[:, k:k + 1]
-    ICOL, SQB, PMC, PM2, WCOL, W16, THC, I16, GOC, FAR = range(10)
+    ICOL, SQB, WCOL, W16, THC, GOC = range(6)
+    whole = lambda out, pattern, base, cm, key, c=0.2: G(lambda e: e.iota(out, pattern, base, cm, allow_small_or_imprecise_dtypes=True), (), (key,), c)
+    fill = lambda out, n, v, key: G(lambda e: e.affine_select(out, T.ones[:, 0:n], [[0, n]], OP.is_ge, v, -1, 0), ("ones",), (key,), 0.2)
     G(lambda e: e.iota(T.pi[:, 0:1], [[0, 1]], 0, 1), (), ("pi",), 0.2)
-    G(lambda e: e.iota(T.pf[:, 0:1], [[0, 1]], 592, -1, allow_small_or_imprecise_dtypes=True), (), ("pf",), 0.2)
-    G(lambda e: e.iota(T.pmi[:, :], [[2, 8]], 0, 0), (), ("pmi",), 0.2)
-    G(lambda e: e.iota(T.tu[:, 0:128], [[-1024, 2], [16, 64]], 1024, 1, allow_small_or_imprecise_dtypes=True), (), ("tu",), 0.34)
-    G(lambda e: e.iota(T.tu[:, 128:130], [[0, 2]], 1024, 1, allow_small_or_imprecise_dtypes=True), (), ("tu2",), 0.2)
+    whole(T.pf[:, 0:1], [[0, 1]], 592, -1, "pf")
+    whole(T.tu[:, 0:128], [[-1024, 2], [16, 64]], 1024, 1, "tu", 0.34)
+    whole(T.tu[:, 128:130], [[0, 2]], 1024, 1, "tu2")
     V(lambda e: e.memset(T.ones[:, :], 1.0), (), ("ones",), 64)
     G(lambda e: e.affine_select(T.ident[:, :], T.ones[:, :], [[-1, 128]], OP.is_equal, 0.0, 0, 1), ("ones",), ("ident",), 0.4)
     G(lambda e: e.affine_select(T.m1[:, :], T.ones[:, :], [[-16, 8], [0, 16]], OP.is_ge, 0.0, 0, 1), ("ones",), ("m1",), 0.4)
     G(lambda e: e.affine_select(T.bo[:, :], T.m1[:, :], [[16, 8], [0, 16]], OP.is_ge, 0.0, 15, -1), ("m1",), ("bo",), 0.4)
-    G(lambda e: e.iota(T.bli[:, :], [[0, 2], [1, 8]], 0, 0), (), ("bli",), 0.2)
-    G(lambda e: e.iota(T.prow[:, :], [[0, 8], [1 if SP else 16, 16]], 0 if SP else 4, 0, allow_small_or_imprecise_dtypes=True), (), ("prow",), 0.4)
+    whole(T.prow[:, :], [[1, 16]], 0, 0, "prow")
     V(lambda e: e.memset(T.z16[:, :], 0.0), (), ("z16",), 72)
-    fill = lambda out, n, v, key: G(lambda e: e.affine_select(out, T.ones[:, 0:n], [[0, n]], OP.is_ge, v, -1, 0), ("ones",), (key,), 0.2)
     V(lambda e: e.tensor_scalar(T.pj[:, 0:1], T.pi[:, 0:1], 15, None, OP.bitwise_and), ("pi",), ("pj",), 8)
     V(lambda e: e.tensor_copy(col(ICOL), T.pj[:, 0:1]), ("pj",), ("icol",), 8)
-    V(lambda e: e.tensor_scalar(col(PM2), col(ICOL), 8.0, -127.0, OP.is_ge, OP.mult), ("icol",), ("pm2",), 8)
-    V(lambda e: e.tensor_scalar(col(PMC), col(ICOL), 16.0, col(PM2), OP.mult, OP.add), ("icol", "pm2"), ("pmc",), 8)
-    V(lambda e: e.tensor_scalar(T.pm[:, :], T.pmi[:, :], col(PMC), None, OP.add), ("pmi", "pmc"), ("pm",), 8)
     for h in range(2):
-        V(lambda e, h=h: e.tensor_copy(T["lt0%d" % h][:, :], T.bni[:, 128 * h:128 * h + 128].indirect(T.pm[:, :])), ("bn0%d" % h, "pm"), ("lt0%d" % h,), gat(128))
+        V(lambda e, h=h: e.tensor_copy(T["lt0%d" % h][:, :], T.bni[:, 128 * h:128 * h + 128]), ("bn%d" % h,), ("lt0%d" % h,), 128)
     A(lambda e: e.activation(col(SQB), col(ICOL), AF.Identity, bias=T.pf[:, 0:1]), ("icol", "pf"), ("sqb",), 8)
     A(lambda e: e.activation(T.sq[:, :], T.tu[:, :], AF.Square, bias=col(SQB)), ("tu", "tu2", "sqb"), ("sq",), 128)
     V(lambda e: e.tensor_scalar(T.xa[:, :], T.sq[:, :], float((32 * KAP[0] - 592 * 592) % 65536), None, OP.add), ("sq",), ("xa",), 128)
@@ -219,296 +201,172 @@ def build(core, T, topo, VEC):
     either(lambda e: scale_on(e, T.z16[:, 15:128:16], T.bo[:, 0:128:16], 0.0625), ("bo",), ("z16",), 8)
     V(lambda e: e.tensor_scalar(col(WCOL), T.wti[:, :], 16.0, None, OP.mult), ("wti",), ("wcol",), 8)
     either(lambda e: scale_on(e, T.zw[:, :], T.z16[:, :], col(WCOL)), ("z16", "wcol"), ("zw",), ("h", 144))
-    if HALF:
-        V(lambda e: e.tensor_tensor(T.z2[:, 8:144], T.zw[:, 8:144], T.zw[:, 0:136], OP.add), ("zw",), ("z2",), 272)
-        for s in range(2):
-            V(lambda e, s=s: e.tensor_scalar(col(FAR + s), col(ICOL), 8.0, 2.0 ** 21, OP.is_lt if s else OP.is_ge, OP.mult), ("icol",), ("farc%d" % s,), 8)
-            either(lambda e, s=s: scale_on(e, T.far[:, :, s], T.ones[:, 0:32], col(FAR + s)), ("ones", "farc%d" % s), ("far%d" % s,), 32)
     V(lambda e: e.tensor_scalar(col(THC), T.thi[:, :], -0.0625, -15.0 / 32, OP.mult, OP.add), ("thi",), ("thc",), 8)
-    either(lambda e: scale_on(e, T.cini[:, 32:40], T.ones[:, 0:8], col(THC)), ("ones", "thc"), ("tini0",), 8)
-    A(lambda e: e.activation(T.cini[:, 40:48], T.cini[:, 32:40], AF.Identity, bias=col(THC), scale=-1.0), ("tini0", "thc"), ("tini1",), 8)
-    V(lambda e: e.tensor_copy(T.bl[:, :], T.bli[:, :]), ("bli",), ("bl",), 16)
+    either(lambda e: scale_on(e, T.cini[:, 24:32], T.ones[:, 0:8], col(THC)), ("ones", "thc"), ("tini0",), 8)
+    A(lambda e: e.activation(T.cini[:, 40:48], T.cini[:, 24:32], AF.Identity, bias=col(THC), scale=-1.0), ("tini0", "thc"), ("tini1",), 8)
     V(lambda e: e.tensor_scalar(T.bow[:, :], T.bo[:, :], col(WCOL), 1.0 / 256, OP.mult, OP.mult), ("bo", "wcol"), ("bow",), 64)
-    for s in range(2 if TPE or BPE else 0):
-        either(lambda e, s=s: scale_on(e, T.i32[:, s, :], T.ident[:, :], 1.0 - 2 * s), ("ident",), ("i32%d" % s,), 128)
-    KB = 16384.0 if SP else 64.0
-    either(lambda e: scale_on(e, T.bo64[:, :], T.bo[:, :], KB), ("bo",), ("bo64",), ("h", 128))
-    either(lambda e: scale_on(e, T.nbo64[:, :], T.bo[:, :], -KB), ("bo",), ("nbo64",), ("h", 128))
-    if SP:
-        either(lambda e: scale_on(e, T.hident[:, :], T.ident[:, :], -0.5), ("ident",), ("hident",), ("h", 128))
-        fill(T.cini[:, 48:56], 8, 1.0 / 256, "cini3")
-        V(lambda e: e.tensor_scalar(T.cmpc[:, 0:128], T.prow[:, :], col(ICOL), -1000.0, OP.not_equal, OP.mult), ("prow", "icol"), ("cmpc",), 128)
-    else:
-        either(lambda e: scale_on(e, col(I16), col(ICOL), -16.0), ("icol",), ("i16",), 8)
-        A(lambda e: e.activation(T.cmpc[:, 0:128], T.prow[:, :], AF.Identity, bias=col(I16)), ("prow", "i16"), ("cmpc",), 128)
-    V(lambda e: e.tensor_scalar(T.diag[:, :], T.cmpc[:, 0:16], 0.0 if SP else 4.0, 256 / KB, OP.is_equal, OP.mult), ("cmpc",), ("diag",), 16)
+    either(lambda e: scale_on(e, T.bok[:, :], T.bo[:, :], 256.0), ("bo",), ("bok",), ("h", 128))
+    either(lambda e: scale_on(e, T.nbok[:, :], T.bo[:, :], -256.0), ("bo",), ("nbok",), ("h", 128))
+    V(lambda e: e.tensor_scalar(T.diag[:, :], T.prow[:, :], col(ICOL), None, OP.is_equal), ("prow", "icol"), ("diag",), 16)
     fill(T.cini[:, 8:24], 16, -15.0 / 32, "cini1")
-    fill(T.cini[:, 24:32], 8, 1.0 / 32, "cini2")
+    fill(T.cini[:, 32:40], 8, 1.0 / 32, "cini2")
+    whole(T.cini[:, 48:56], [[2, 8]], 0, 0, "cini3")
     A(lambda e: e.activation(col(W16), col(ICOL), AF.Identity, bias=-15.0 / 32, scale=-0.0625), ("icol",), ("w16",), 8)
     either(lambda e: scale_on(e, T.cini[:, 0:8], T.ones[:, 0:8], col(W16)), ("ones", "w16"), ("cini0",), 8)
     A(lambda e: e.activation(col(GOC), col(ICOL), AF.Identity, bias=120.0), ("icol",), ("goc",), 8)
     fill(T.nn[:, 0:1], 1, -13.0 / 32, "nn")
-    G(lambda e: e.iota(T.ms[:, 256:272], [[0, 16]], 0, 0, allow_small_or_imprecise_dtypes=True), (), ("msz",), 0.2)
-    for h in range(0 if SP else 2):
-        G(lambda e, h=h: e.iota(T["qi_%d" % h][:, 24:32], [[0, 8]], 0, 0), (), ("qiz_%d" % h,), 0.2)
+    whole(T.ms[:, 256:272], [[0, 16]], 0, 0, "msz")
+    for h in range(2):
+        whole(T["fr_%d" % h][:, 24:32], [[0, 8]], 0, 0, "frz_%d" % h)
+        whole(T["wm_%d" % h][:, 0:16], [[0, 16]], 0, 0, "wmz_%d" % h)
+    V(lambda e: e.tensor_scalar(T.cw0[:, :], T.cni[:, :], -1.0, None, OP.mult), ("cni",), ("cw0",), 256)
 
     def half(t, h):
         B = lambda n: T["%s_%d" % (n, h)]
         K = lambda n: "%s_%d" % (n, h)
-        S, F, X, Y = B("S"), B("F"), B("X"), B("Y")
-        lt = T["lt%d%d" % (t, h)]
-        bn = T["bn%d%d" % (t, h)][:, :] if t else T.bni[:, 128 * h:128 * h + 128]
-        kbn = "bn%d%d" % (t, h)
-        cw = T["cw%d" % t] if t else T.cni
-        fa, dc, ac, ar, lu = B("fa"), B("dc"), B("ac"), B("ar"), B("lu")
+        SF = (B("S"), B("F"))
+        S, F = SF
+        lt, klt = T["lt%d%d" % (t, h)], "lt%d%d" % (t, h)
+        cw = T["cw%d" % t]
+        fa, dc, ac, lu = B("fa"), B("dc"), B("ac"), B("lu")
         zs = lambda z, i: z[:, 15 - i:143 - i]
-
         units = lambda name, x0, m: tuple(K("%s%d" % (name, u)) for u in range(x0 // 128, (x0 + m) // 128))
+        both = lambda x0, m: units("ac", x0, m) + units("ad", x0, m)
 
-        def gather_pair(l, pieces, w, wk):
-            for la, lb, k, x0, m in pieces:
-                either(lambda e, la=la, x0=x0, m=m: gather_on(e, fa[:, x0:x0 + m], w.indirect(la)), (k,) + wk, units("fa", x0, m), gat(m), "gA")
-            for la, lb, k, x0, m in pieces:
-                V(lambda e, lb=lb, x0=x0, m=m: e.tensor_tensor(dc[:, x0:x0 + m], w.indirect(lb), fa[:, x0:x0 + m], OP.subtract),
-                  (k,) + wk + units("fa", x0, m), units("dc", x0, m), gat(m), note="gB")
-            for la, lb, k, x0, m in pieces:
-                r = range(x0 % 512 // 128 * 2 + x0 // 512, (x0 % 512 + m) // 64, 2) if l == JOIN else range(x0 // 128, (x0 + m) // 128)
-                if (l, x0 // 512 if l else 0) in ICUT and x0 == pieces[-1][3]:
-                    for i0, name in ((0, "ac"), (1, "ad")):
-                        A(lambda e, x0=x0, m=m, r=r, i0=i0: e.activation(ac[:, r.start:r.stop:r.step, i0:128:2], dc[:, x0 + i0:x0 + m:2], AF.Abs),
-                          units("dc", x0, m), tuple(K("%s%d" % (name, u)) for u in r), m // 2, note="abs")
-                    continue
-                A(lambda e, x0=x0, m=m, r=r: e.activation(ac[:, r.start:r.stop:r.step, :], dc[:, x0:x0 + m], AF.Abs),
-                  units("dc", x0, m), tuple(K("%s%d" % (name, u)) for u in r for name in ("ac", "ad")), m, note="abs")
-
-        def gather_both(s, n, w, wk):
-            x0, out, kb = 512 * s, (F[:, 0:n] if s else S[:, 256:256 + n]), K("SF"[s])
-            either(lambda e: gather_on(e, fa[:, x0:x0 + 2 * n], w.indirect(lu[:, 64 * s:64 * s + n // 8])), (K("lu%d" % s),) + wk, units("fa", x0, 2 * n), gat(2 * n), "gAB")
-
-            def diff(e):
-                e.matmul(out, T.ident[:, :], fa[:, x0:x0 + n], True, False)
-                return e.matmul(out, T.nident[:, :], fa[:, x0 + n:x0 + 2 * n], False, True)
-            P(diff, units("fa", x0, 2 * n) + ("ident", "nident"), (K("S%d" % s),), 2 * n, (kb,), note="diff")
-            A(lambda e: e.activation(ac[:, 4 * s:4 * s + n // 128, :], out, AF.Abs), (K("S%d" % s),), units("ac", x0, n), n, (kb,), note="abs")
-
-        def pieces(lst, c0, key, x0, n, ch):
-            m, k = n // ch, n // ch // 16
-            return [(lst[:, c0 + k * c:c0 + k * c + k], lst[:, c0 + n // 16 + k * c:c0 + n // 16 + k * c + k], key, x0 + m * c, m) for c in range(ch)]
-
-        def weigh(l, n, s=0):
-            if l in HALF:
-                def fn(e):
-                    for i in range(8):
-                        o = e.matmul(S[:, 0:n // 8], zs(T.z2, i), ac[:, 0:n // 128, i:128:8], False, i == 7)
-                    return o
-                P(lambda e: e.matmul(S[:, 0:n // 8], T.ident[:, :], T.far[:, 0:n // 16, :], True, False), ("ident", "far0", "far1"), (K("S0"),), 64, (K("S"),), note="far")
-                P(fn, units("ac", 0, n) + ("z2",), (K("S0"),), 512, (K("S"),), note="weighe")
-                V(lambda e: e.tensor_copy(B("ib")[:, 0:n // 16], S[:, 0:n // 8:2]), (K("S0"),), (K("ib0"),), n // 16, (K("S"),), note="i0")
-                return
-
-            for r in (range(0, 16, 2), range(1, 16, 2)) if (l, s) in ICUT else (range(16),):
-                def fn(e, r=r):
-                    for i in r:
-                        o = e.matmul(F[:, 256:256 + n // 16] if s else S[:, 0:n // 16], zs(T.zw, i), ac[:, 4 * s:4 * s + n // 128, i:128:16], i == 0, i == 15)
-                    return o
-                P(fn, units("ac", 512 * s, n) + units("ad", 512 * s, n) * (15 in r) + ("zw",), (K("S%d" % s),), 64 * len(r), (K("SF"[s]),), note="weighe" if r.start else "weigh")
-
-        def index(l, src, ks, bank, c0, n, wr, two=False):
-            ka, kb = K("ia%d" % (c0 // 64)), K("ib%d" % (c0 // 64))
-            V(lambda e: e.tensor_scalar(B("ia")[:, c0:c0 + n], src, BIG, BIG + W, OP.add, OP.subtract), (ks,), (ka,), n, bank, note="i1")
-            V(lambda e: e.tensor_tensor(lu[:, c0:c0 + n], src, B("ia")[:, c0:c0 + n], OP.subtract), (ka, ks), wr, n, bank, note="i2")
+        def index(src, ks, bank, c0, n):
+            ka, wr = tuple(K("ia%d" % u) for u in range(c0 // 64, (c0 + n + 63) // 64)), tuple(K("lu%d" % u) for u in range(c0 // 64, (c0 + n + 63) // 64))
+            V(lambda e: e.tensor_scalar(B("ia")[:, c0:c0 + n], src, BIG, BIG + W, OP.add, OP.subtract), ks, ka, n, (bank,), note="i1")
+            V(lambda e: e.tensor_tensor(lu[:, c0:c0 + n], src, B("ia")[:, c0:c0 + n], OP.subtract), ka + ks, wr, n, (bank,), note="i2")
 
         def table(l):
             keys = tuple("x%d%d" % (k, c) for k in (l - 1, l) for c in range(TCH) if k >= 0)
             return T.xw[:, 2 * W + TW * l - W // 2:2 * W + TW * (l + 1)], keys + ("xw2",)
 
-        gather_pair(0, pieces(lt, 0, "lt%d%d" % (t, h), 0, 1024, CH[0]), T.xw[:, 0:W], ("xw",))
+        m = 2048 // CH[0]
+        for c in range(CH[0]):
+            either(lambda e, c=c, m=m: gather_on(e, fa[:, m * c:m * c + m], T.xw[:, 0:W].indirect(lt[:, m // 16 * c:m // 16 * (c + 1)])), (klt, "xw"), units("fa", m * c, m), gat(m), "g0")
+        for q in range(2):
+            x0 = 1024 * q
+            for s in range(2):
+                X, kX = T["X%d" % (2 * q + s)], "X%d" % (2 * q + s)
+                if s == 0:
+                    for b0 in (0, 2):
+                        def cols(e, X=X, x0=x0, b0=b0):
+                            for b in (b0, b0 + 1):
+                                e.matmul(X[:, :, 16 * b:16 * b + 16], T.ident[:, :], fa[:, x0 + 256 * b:x0 + 256 * b + 128], b == 0, False)
+                                o = e.matmul(X[:, :, 16 * b:16 * b + 16], T.nident[:, :], fa[:, x0 + 256 * b + 128:x0 + 256 * b + 256], False, b == 3)
+                            return o
+                        P(cols, units("fa", x0 + 256 * b0, 512) + ("ident", "nident"), (kX,), 512, (kX,), note="col", acc=b0 > 0)
+                else:
+                    def rows(e, X=X, x0=x0):
+                        for c in range(8):
+                            e.matmul(X[:, c, :], T.ident[:, :], fa[:, x0 + c:x0 + 1024:16], c == 0, False)
+                            o = e.matmul(X[:, c, :], T.nident[:, :], fa[:, x0 + c + 8:x0 + 1024:16], False, c == 7)
+                        return o
+                    P(rows, units("fa", x0, 1024) + ("ident", "nident"), (kX,), 1024, (kX,), note="row")
+                A(lambda e, X=X, s=s, q=q: e.activation(ac[:, 8 * s:8 * s + 8, 64 * q:64 * q + 64], X[:, :, :], AF.Abs), (kX,), units(("ac", "ad")[q], 1024 * s, 1024), 512, (kX,), note="abs0")
+            if OPT["J0"]:
+                def wq(e, q=q):
+                    for i in range(16):
+                        o = e.matmul(S[:, 0:16, 4 * q:4 * q + 4], zs(T.zw, i), ac[:, :, 64 * q + i:64 * q + 64:16], q + i == 0, q + i == 16)
+                    return o
+                P(wq, units(("ac", "ad")[q], 0, 2048) + ("zw",), (K("S0"),), 1024, (K("S"),), note="weigh", acc=q > 0)
 
-        def rows(bank, src, first, last):
+        def weigh(s, n):
             def fn(e):
-                for c in range(8):
-                    e.matmul(bank[:, :, 8 * c:8 * c + 8], T.ident[:, :], src[:, c:1024:16], first and c == 0, False)
-                    o = e.matmul(bank[:, :, 8 * c:8 * c + 8], T.nident[:, :], src[:, c + 8:1024:16], False, last and c == 7)
+                for i in range(16):
+                    o = e.matmul(SF[s][:, 0:n // 128, :], zs(T.zw, i), ac[:, 8 * s:8 * s + n // 128, i:128:16], i == 0, i == 15)
                 return o
-            return fn
-        fk, dk = units("fa", 0, 1024), units("dc", 0, 1024)
-        P(rows(X, fa, True, True), fk + ("ident", "nident"), (K("X"),), 1024, (K("X"),), note="row0")
-        P(rows(Y, fa, True, False), fk + ("ident", "nident"), (K("Y"),), 1024, (K("Y"),), note="row1")
-        P(rows(Y, dc, False, True), dk + ("ident", "nident"), (K("Y"),), 1024, (K("Y"),), note="row2")
-        for p0, p1 in RCUT:
-            bank, kk = (X, Y)[p0 // 8], K("XY"[p0 // 8])
-            A(lambda e, p0=p0, p1=p1, bank=bank: e.activation(ar[:, p0 // 8, p0 % 8 * 64:(p1 - p0 + p0 % 8) * 64], bank[:, p0 % 8:p1 - p0 + p0 % 8, :], AF.Abs),
-              (kk,), (K("ar%d" % p0),), 64 * (p1 - p0), (kk,), note="absr")
-        weigh(0, 1024)
-        for p0, p1 in RCUT:
-            def wrow(e, p0=p0, p1=p1):
-                for p in range(p0, p1):
-                    o = e.matmul(F[:, 256:320], zs(T.zw, p), ar[:, p // 8, p % 8 * 64:p % 8 * 64 + 64], p == 0, p == 15)
-                return o
-            P(wrow, ("zw", K("ar%d" % p0)), (K("S1"),), 64 * (p1 - p0), (K("F"),), note="weighr")
-        index(0, S[:, 0:64], K("S0"), (K("S"),), 0, 64, (K("lu0"),))
-        index(0, F[:, 256:320], K("S1"), (K("F"),), 64, 64, (K("lu1"),))
+            P(fn, both(1024 * s, n) + ("zw",), (K("S%d" % s),), 1024, (K("SF"[s]),), note="weigh")
+            index(SF[s][:, 0:n // 128, :], (K("S%d" % s),), K("SF"[s]), 64 * s, n // 16)
 
-        Z, GD, D, kZ, kD, nz = X[:, 7, :], Y[:, 7, 0:16], Y[:, 7, 8:16], K("X"), K("Y"), 24 if SP else 32
-        P(lambda e: e.matmul(Z[:, 0:nz], T.ident[:, :], T.cini[:, 0:nz], True, False), ("ident", "cini0", "cini1", "cini2"), (K("Z"),), 64, (kZ,), note="zini")
-
-        def dini(e):
-            e.matmul(GD, T.ident[:, :], T.cini[:, 24:40], True, False)
-            return e.matmul(D, T.ident[:, :], T.cini[:, 40:48], False, False)
-        P(dini, ("ident", "cini2", "tini0", "tini1"), (K("D"),), 128, (kD,), note="dini")
+        if OPT["J0"]:
+            index(S[:, 0:16, :], (K("S0"),), K("S"), 0, 128)
+        else:
+            for s in range(2):
+                weigh(s, 1024)
 
         for l, n in ((1, 512), (2, 256), (3, 128)):
-            if l < JOIN:
-                for s in range(2):
-                    if (l, s) in PL:
-                        gather_both(s, n, *table(l - 1))
-                    else:
-                        gather_pair(l, pieces(lu, 64 * s, K("lu%d" % s), 512 * s, n, CH[l] // 2), *table(l - 1))
-                    weigh(l, n, s)
-                    index(l, F[:, 256:256 + n // 16] if s else S[:, 0:n // 16], K("S%d" % s), (K("SF"[s]),), 64 * s, n // 16, (K("lu%d" % s),))
-                continue
-            if l > JOIN:
-                gather_pair(l, pieces(lu, 0, K("lu0"), 0, 2 * n, CH[l]), *table(l - 1))
-            else:
-                gather_pair(l, [p for s in range(2) for p in pieces(lu, 64 * s, K("lu%d" % s), 512 * s, n, CH[l] // 2)], *table(l - 1))
-            weigh(l, 2 * n)
-            index(l, S[:, 0:n // 8], K("S0"), (K("S"),), 0, n // 8, (K("lu0"),), l in HALF)
+            w, wk = table(l - 1)
+            m, k = n // CH[l], n // CH[l] // 16
+            for s in range(2):
+                kl = (K("lu%d" % s),) + wk
+                for c in range(CH[l]):
+                    either(lambda e, x0=512 * s + m * c, c0=64 * s + k * c, m=m, k=k, w=w: gather_on(e, fa[:, x0:x0 + m], w.indirect(lu[:, c0:c0 + k])),
+                           kl, units("fa", 512 * s + m * c, m), gat(m), "gA")
+                for c in range(CH[l]):
+                    V(lambda e, x0=512 * s + m * c, c0=64 * s + n // 16 + k * c, m=m, k=k, w=w: e.tensor_tensor(dc[:, x0:x0 + m], w.indirect(lu[:, c0:c0 + k]), fa[:, x0:x0 + m], OP.subtract),
+                      kl + units("fa", 512 * s + m * c, m), units("dc", 512 * s + m * c, m), gat(m), note="gB")
+                for c in range(CH[l]):
+                    A(lambda e, x0=512 * s + m * c, r0=8 * s + m * c // 128, m=m: e.activation(ac[:, r0:r0 + m // 128, :], dc[:, x0:x0 + m], AF.Abs),
+                      units("dc", 512 * s + m * c, m), both(1024 * s + m * c, m), m, note="abs")
+                weigh(s, n)
 
         w, wk = table(3)
-        wd, qi, fr, nn = B("wd"), B("qi"), B("fr"), T.nn
-        either(lambda e: gather_on(e, wd[:, 0, :], w.indirect(lu[:, 0:8])), wk + (K("lu0"),), (K("wc"),), gat(128), "gWC")
-        V(lambda e: e.tensor_tensor(wd[:, 1, :], w.indirect(lu[:, 8:16] if JOIN < 4 else lu[:, 64:72]), wd[:, 0, :], OP.subtract), wk + (K("lu%d" % (JOIN // 4)), K("wc")), (K("dw"),), gat(128), note="gWR")
-        A(lambda e: e.activation(wd[:, 2, :], wd[:, 1, :], AF.Abs), (K("dw"),), (K("aw"),), 128, note="absW")
+        wd, qi, fr, nn, wm = B("wd"), B("qi"), B("fr"), T.nn, B("wm")
+        Z, DG, Act, kS, kF = S[:, 32:35, :], F[:, 32:34, :], S[:, 40, :], K("S"), K("F")
+        P(lambda e: e.matmul(Z, T.ident[:, :], T.cini[:, 0:24], True, False), ("ident", "cini0", "cini1"), (K("Z"),), 64, (kS,), note="zini")
 
-        def donor(e):
-            e.matmul(Z[:, 0:8], T.bow[:, :], wd[:, 0, 0:128:16], False, False)
-            return e.matmul(Z[:, 8:16], T.bow[:, :], wd[:, 0, 0:128:16], False, False)
-        P(donor, (K("wc"), "bow", K("Z")), (K("Zd"),), 128, (kZ,), note="donor")
+        def dini(e):
+            e.matmul(DG, T.ident[:, :], T.cini[:, 24:40], True, False)
+            return e.matmul(F[:, 32, :], T.ident[:, :], T.cini[:, 40:48], False, False)
+        P(dini, ("ident", "cini2", "tini0", "tini1"), (K("D"),), 128, (kF,), note="dini")
+        either(lambda e: gather_on(e, wd[:, 0, :], w.indirect(lu[:, 0:8])), wk + (K("lu0"),), (K("wc"),), gat(128), "gWC")
+        V(lambda e: e.tensor_tensor(wd[:, 2, :], w.indirect(lu[:, 64:72]), wd[:, 0, :], OP.subtract), wk + (K("lu1"), K("wc")), (K("dw"),), gat(128), note="gWR")
+        A(lambda e: e.activation(wd[:, 1, :], wd[:, 2, :], AF.Abs), (K("dw"),), (K("aw"),), 128, note="absW")
 
         def asum(e):
+            e.matmul(S[:, 32, :], T.bow[:, :], wd[:, 0, 0:128:16], False, False)
+            e.matmul(S[:, 33, :], T.bow[:, :], wd[:, 0, 0:128:16], False, False)
             for i in range(16):
-                o = e.matmul(Z[:, 16:nz], zs(T.z16, i), wd[:, 0:nz // 8 - 2, i:128:16], False, i == 15)
+                o = e.matmul(S[:, 34, :], zs(T.z16, i), wd[:, 0, i:128:16], False, i == 15)
             return o
-        P(asum, (K("wc"), "z16", K("Z")) + (() if SP else (K("dw"),)), (K("Za"),), 1024, (kZ,), note="A")
+        P(asum, (K("wc"), "z16", "bow"), (K("Z"),), 1152, (kS,), note="A", acc=True)
 
         def dsum(e):
             for i in range(16):
-                o = e.matmul(GD if SP else D, zs(T.z16, i), wd[:, 1 if SP else 2:3, i:128:16], False, i == 15)
+                o = e.matmul(DG, zs(T.z16, i), wd[:, 1:3, i:128:16], False, i == 15)
             return o
-        P(dsum, (K("dw"), K("aw"), "z16"), (K("D"),), 1024, (kD,), note="D")
-        V(lambda e: e.tensor_copy(qi[:, 0:24], Z[:, 0:24]), (K("Zd"), K("Za")), (K("qi"),), 24, (kZ,), note="q")
-        V(lambda e: e.tensor_tensor(fr[:, 0:nz], Z[:, 0:nz], qi[:, 0:nz], OP.subtract), (K("Zd"), K("Za"), K("Z"), K("qi"), K("qiz")), (K("fr"),), 32, (kZ,), note="frac")
+        P(dsum, (K("dw"), K("aw"), "z16"), (K("D"),), 1024, (kF,), note="D", acc=True)
+        V(lambda e: e.tensor_copy(qi[:, :], Z), (K("Z"),), (K("qi"),), 24, (kS,), note="q")
+        V(lambda e: e.tensor_tensor(fr[:, 0:24], Z, qi[:, :], OP.subtract), (K("Z"), K("qi")), (K("fr"),), 24, (kS,), note="frac")
         V(lambda e: e.tensor_tensor_scan(nn[:, 8 * h + 1:8 * h + 9], fr[:, 0:8], fr[:, 0:8], nn[:, 8 * h:8 * h + 1], OP.min, OP.min),
           (K("fr"), "nn0" if h else "nn"), ("nn%d" % h,), 16, note="scan")
-        if not SP:
-            A(lambda e: e.activation(B("sn")[:, :], fr[:, 24:32], AF.Sign), (K("fr"),), (K("sn"),), 8, note="sign")
         V(lambda e: e.tensor_scalar(B("go")[:, :], fr[:, 8:16], 256.0, col(GOC), OP.mult, OP.add), (K("fr"), "goc"), (K("go"),), 8, note="go")
 
         def act(e):
-            e.matmul(Act, T.bo64[:, :], nn[:, 8 * h:8 * h + 8], True, False)
-            e.matmul(Act, T.nbo64[:, :], nn[:, 8 * h + 1:8 * h + 9], False, False)
-            if SP:
-                return e.matmul(Act, T.nbo64[:, :], T.cini[:, 48:56], False, True)
-            return e.matmul(Act, T.ident[:, :], B("sn")[:, :], False, not ZA)
-        Act, kA = (X[:, 6, 0:8], K("X")) if SP else (F[:, 0:8], K("F"))
-        P(act, ("nn", "nn0", "nn%d" % h, K("sn"), "bo64", "nbo64", "ident", "cini3"), (K("Fa"),), 192, (kA,), note="act")
-        qa = T["qr%d" % t][:, 8 * h:8 * h + 8]
-        if SP:
-            V(lambda e: e.tensor_tensor(fr[:, 24:32], fr[:, 16:24], Act, OP.subtract), (K("Fa"), K("fr")), (K("fra"),), 8, (kA,), note="fra")
-            V(lambda e: e.tensor_tensor(fr[:, 32:40], D, fr[:, 24:32], OP.is_gt), (K("D"), K("fra")), (K("qa"),), 8, (kD,), note="qa")
-            V(lambda e: e.tensor_tensor(B("zz")[:, :], GD[:, 0:8], fr[:, 32:40], OP.mult), (K("D"), K("qa")), (K("zz"),), 8, (kD,), note="zz")
-        V(lambda e: e.tensor_tensor(qa, D, fr[:, 16:24], OP.is_gt), (K("D"), K("fr")), ("qr%d%d" % (t, h),), 8, (kD,), note="qr" if SP else "qa")
-        neg = t == 2
-        onpe = TPE and t > 0
-        if onpe:
-            either(lambda e: gather_on(e, B("tb")[:, :], cw[:, :].indirect(B("go")[:, :])), ("cw%d" % t, K("go")), (K("tb"),), gat(128), "T")
-
-            def less(e):
-                e.matmul(Y[:, 0:2, :], T.i32[:, 0 if neg else 1, :], bn, True, False)
-                return e.matmul(Y[:, 0:2, :], T.i32[:, 0, :], B("tb")[:, :], False, True)
-            P(less, (K("tb"), kbn, "i320", "i321"), (K("Y"),), 1024, (K("Y"),), note="Tp")
-        else:
-            V(lambda e: e.tensor_tensor(B("tb")[:, :], cw[:, :].indirect(B("go")[:, :]), bn, OP.add if neg else OP.subtract), ("cw%d" % t, K("go"), kbn), (K("tb"),), gat(128), note="T")
-        if ZA:
-            P(lambda e: e.matmul(Act, T.ident[:, :], qa, False, True), (K("Fa"), "qr%d%d" % (t, h)), (K("Fb"),), 64, (kA,), note="act2")
-
-            def zcopy(e):
-                return e.tensor_copy(B("zz")[:, :], Act) if e is VEC[0] else e.activation(B("zz")[:, :], Act, AF.Identity)
-            A(zcopy, (K("Fb"),), (K("zz"),), 8, (K("F"),), note="zz")
-        elif not SP:
-            V(lambda e: e.tensor_tensor(B("zz")[:, :], Act, qa, OP.add), (K("Fa"), "qr%d%d" % (t, h)), (K("zz"),), 8, (K("F"),), note="zz")
-        spread = B("zz")[:, 0:8].indirect(T.bl[:, 0:8])
-
-        def colmask(e):
-            if e is VEC[0]:
-                return e.tensor_scalar(B("ee")[:, 128:256], spread, 6.0, None, OP.is_equal)
-            return e.activation(B("ee")[:, 128:256], spread, AF.Relu, bias=-5.0)
-        if SP:
-            V(lambda e: e.tensor_tensor(B("ee")[:, 0:128], spread, T.cmpc[:, 0:128], OP.is_lt), (K("zz"), "bl", "cmpc"), (K("er"),), gat(128), note="er")
-            A(lambda e: e.activation(B("ee")[:, 128:256], spread, AF.Sign, bias=-1.0 / 64), (K("zz"), "bl"), (K("ec"),), gat(128), note="ec")
-        else:
-            V(lambda e: e.tensor_tensor(B("ee")[:, 0:128], spread, T.cmpc[:, 0:128], OP.is_equal), (K("zz"), "bl", "cmpc"), (K("er"),), gat(128), note="er")
-            either(colmask, (K("zz"), "bl"), (K("ec"),), gat(128), "ec")
-        Xm, M = X[:, 0:2, :], Y[:, 0:2, :]
-
-        def xm(e):
-            e.matmul(Xm, T.bo[:, :], B("ee")[:, 0:128], True, False)
-            return e.matmul(Xm, (T.hident if SP else T.nident)[:, :], B("ee")[:, 128:256], False, True)
-        P(xm, (K("er"), K("ec"), "bo", "nident", "hident"), (K("X"),), 256, (K("X"),), note="X")
-        b3, kb3 = T["b3%d%d" % (t, h)], "b3%d%d" % (t, h)
-        ms = T.ms[:, 128 * h:128 * h + 128]
-        if onpe:
-            A(lambda e: e.activation(B("mk")[:, :], Xm, AF.Abs, bias=-0.5 * SP), (K("X"),), (K("mk"),), 128, (K("X"),), note="M")
-            a, b, ks = M, B("mk")[:, :], (K("mk"), K("Y"))
-        else:
-            A(lambda e: e.activation(M, Xm, AF.Abs, bias=-0.5 * SP), (K("X"),), (K("Y"),), 128, (K("X"), K("Y")), note="M")
-            a, b, ks = B("tb")[:, :], M, (K("tb"), K("Y"))
-        if t in BPE:
-            V(lambda e: e.tensor_tensor(ms, a, b, OP.mult), ks, (K("ms"),), 128, (K("Y"),), note="MT")
-            P(lambda e: e.matmul(S[:, 128:256], T.i32[:, 0, :], bn, True, False), (kbn, "i320"), (K("S0"),), 512, (K("S"),), note="B0")
-            P(lambda e: e.matmul(S[:, 128:256], T.i32[:, t - 1, :], ms, False, True), (K("ms"), "i320", "i321"), (K("S0"),), 512, (K("S"),), note="Bp")
-            A(lambda e: e.activation(b3[:, :], S[:, 128:256], AF.Identity), (K("S0"),), (kb3,), 128, (K("S"),), note="B")
-        elif t < R - 1 and LS:
-            mb, kmb = (ms, K("ms")) if t else (B("mk")[:, :], K("mk"))
-            V(lambda e: e.tensor_tensor(mb, a, b, OP.mult), ks, (kmb,), 128, (K("Y"),), note="MT")
-            V(lambda e: e.tensor_tensor(T["ls%d%d" % (t, h)][:, :], mb.indirect(T.pm[:, :]), lt[:, :], OP.add), (kmb, "pm", "lt%d%d" % (t, h)), ("ls%d%d" % (t, h),), gat(128), note="ls")
-            V(lambda e: e.tensor_tensor(b3[:, :], bn, mb, OP.add), (kbn, kmb), (kb3,), 256, note="B")
-            if t == 0:
-                A(lambda e: e.activation(ms, mb, AF.Identity, scale=-1.0), (kmb,), (K("ms"),), 128, note="MS")
-        elif t < R - 1:
-            mp = Y[:, 2:4, :]
-            V(lambda e: e.tensor_tensor(mp, a, b, OP.mult), ks, (K("mp"),), 128, (K("Y"),), note="MT")
-            V(lambda e: e.tensor_tensor(b3[:, :], bn, mp, OP.add), (kbn, K("mp")), (kb3,), 128, (K("Y"),), note="B")
-            A(lambda e: e.activation(ms, mp, AF.Identity, scale=1.0 if t else -1.0), (K("mp"),), (K("ms"),), 128, (K("Y"),), note="MS")
-        else:
-            V(lambda e: e.tensor_tensor(ms, a, b, OP.mult), ks, (K("ms"),), 128, (K("Y"),), note="MT")
-            V(lambda e: e.tensor_tensor(b3[:, :], bn, ms, OP.subtract), (kbn, K("ms")), (kb3,), 256, note="B")
+            e.matmul(Act, T.ident[:, :], T.cini[:, 48:56], True, False)
+            e.matmul(Act, T.bok[:, :], nn[:, 8 * h:8 * h + 8], False, False)
+            return e.matmul(Act, T.nbok[:, :], nn[:, 8 * h + 1:8 * h + 9], False, True)
+        P(act, ("nn", "nn0", "nn%d" % h, "bok", "nbok", "ident", "cini3"), (K("Act"),), 192, (kS,), note="act")
+        qr, kq = T["qr%d" % t], "qr%d%d" % (t, h)
+        neg = t % 2 == 0
+        V(lambda e: e.tensor_tensor(B("tb")[:, :], cw[:, :].indirect(B("go")[:, :]), lt[:, :], OP.add if neg else OP.subtract), ("cw%d" % t, K("go"), klt), (K("tb"),), gat(128), note="T")
+        V(lambda e: e.tensor_tensor(qr[:, h, :], DG, fr[:, 16:32], OP.is_gt), (K("D"), K("fr"), K("frz")), (kq,), 16, (kF,), note="qs")
+        V(lambda e: e.tensor_tensor(B("rr")[:, :], qr[:, h, 0:8], qr[:, h, 8:16], OP.is_gt), (kq,), (K("rr"),), 16, note="r")
+        V(lambda e: e.tensor_tensor(wm[:, 16:32:2], qr[:, h, 0:8], qr[:, h, 8:16], OP.min), (kq,), (K("wc1"),), 16, note="c")
+        V(lambda e: e.tensor_tensor(B("lo")[:, :], Act, B("rr")[:, :], OP.add), (K("Act"), K("rr")), (K("lo"),), 8, (kS,), note="o")
+        either(lambda e: scale_on(e, wm[:, 17:32:2], wm[:, 16:32:2], -1.0, 1.0), (K("wc1"),), (K("wc0"),), 8, "nc")
+        ms, ls, kls = T.ms[:, 128 * h:128 * h + 128], T["ls%d%d" % (t, h)], "ls%d%d" % (t, h)
+        V(lambda e: e.tensor_tensor(ms, wm[:, :].indirect(B("lo")[:, :]), B("tb")[:, :], OP.mult), (K("wc0"), K("wc1"), K("wmz"), K("lo"), K("tb")), (K("ms"),), gat(128), note="M")
+        V(lambda e: e.tensor_tensor(ls[:, :], lt[:, :], ms, OP.subtract if neg else OP.add), (klt, K("ms")), (kls,), 256, note="ls")
         if t < R - 1:
-            ls = T["ls%d%d" % (t, h)]
-            if not LS:
-                V(lambda e: e.tensor_copy(ls[:, :], b3[:, :].indirect(T.pm[:, :])), (kb3, "pm"), ("ls%d%d" % (t, h),), gat(128), note="ls")
             dst = T.cores[(T.rank_of(core) + HOP) % len(T.cores)]
             rid, pid, _ = topo.addr(dst)
             engines = topo.engines(core, dst)
-            el, eb = engines[::2] if t == 0 else engines, engines[1::2]
-            mask = lambda es: sum(1 << en for en in es)
-            o = add("G", lambda e: e.remote_dma(T["lt%d%d" % (t + 1, h)][:, :], ls[:, :], T.sem["al%d%d" % (t + 1, h)], T.sem["sent"], pid, rid, mask(el)),
-                    ("ls%d%d" % (t, h),), (), (), 0.3, sem="-sent", n=len(el), note="send")
-            arr = add(None, None, (), ("lt%d%d" % (t + 1, h),), (), 2.0 + (FIRST if t + h == 0 else 0.0), sem="al%d%d" % (t + 1, h), n=len(el))
-            ops[arr]["order"].add(o)
-            o = add("G", lambda e: e.remote_dma(T["bn%d%d" % (t + 1, h)][:, :], b3[:, :], T.sem["ab%d%d" % (t + 1, h)], T.sem["sent"], pid, rid, mask(eb)),
-                    (kb3,), (), (), 0.3, sem="-sent", n=len(eb), note="send2")
-            ops[o]["order"].add(arr - 1)
-            arr = add(None, None, (), ("bn%d%d" % (t + 1, h),), (), 2.5, sem="ab%d%d" % (t + 1, h), n=len(eb))
+            el = engines[h::2] if t == 0 else engines
+            o = add("G", lambda e: e.remote_dma(T["lt%d%d" % (t + 1, h)][:, :], ls[:, :], T.sem["al%d%d" % (t + 1, h)], T.sem["sent"], pid, rid, sum(1 << en for en in el)),
+                    (kls,), (), (), 0.3, sem="-sent", n=len(el), note="send")
+            arr = add(None, None, (), ("lt%d%d" % (t + 1, h),), (), 2.0 + (OPT["FIRST"] if t + h == 0 else 0.0), sem="al%d%d" % (t + 1, h), n=len(el))
             ops[arr]["order"].add(o)
         else:
-            add("Y", lambda e: e.dma_start(T.yb[:, 128 * h:128 * h + 128], b3[:, :]), (kb3,), (), (), 2.0, sem="st%d" % h, n=16)
+            add("Y", lambda e: e.dma_start(T.yb[:, 128 * h:128 * h + 128], ls[:, :]), (kls,), (), (), 2.0, sem="st%d" % h, n=16)
         if h == 1:
             A(lambda e: e.activation(T.nd[:, :], nn[:, 1:17], AF.Identity, bias=15.0 / 32, accum_out=T.ns[:, 0:1]), ("nn0", "nn1"), ("ns",), 90, note="nsum")
             either(lambda e: scale_on(e, T.sp[:, :], T.diag[:, :], T.ns[:, 0:1]), ("diag", "ns"), ("sp",), 16, "spread")
-            P(lambda e: e.matmul(S[:, 0:16], T.bo64[:, :], T.sp[:, :], True, True), ("sp", "bo64"), (K("S0"),), 64, (K("S"),), note="inv_p")
-            V(lambda e: e.tensor_scalar(T.inv[:, :], S[:, 0:16], col(ICOL), None, OP.add), (K("S0"), "icol"), ("inv",), 16, (K("S"),), note="inv")
-            V(lambda e: e.tensor_tensor(T["cw%d" % (t + 1)][:, :], T.ms[:, :].indirect(T.inv[:, :]), cw[:, :], OP.add if t == 0 else OP.subtract),
+            P(lambda e: e.matmul(F[:, 0:2, :], T.bok[:, :], T.sp[:, :], True, True), ("sp", "bok"), (K("S1"),), 64, (kF,), note="inv_p")
+            V(lambda e: e.tensor_scalar(T.inv[:, :], F[:, 0:2, :], col(ICOL), None, OP.add), (K("S1"), "icol"), ("inv",), 16, (kF,), note="inv")
+            V(lambda e: e.tensor_tensor(T["cw%d" % (t + 1)][:, :], T.ms[:, :].indirect(T.inv[:, :]), cw[:, :], OP.subtract),
               ("ms_0", "ms_1", "msz", "inv", "cw%d" % t), ("cw%d" % (t + 1),), gat(256), note="C")
 
     for t in range(R):
@@ -518,160 +376,16 @@ def build(core, T, topo, VEC):
             for o in ops[k0:]:
                 o["cls"] = 2 * t + h
         if t == 1:
-            V(lambda e: e.tensor_tensor(T.qs[:, :], T.qr0[:, :], T.qr1[:, :], OP.add), ("qr00", "qr01", "qr10", "qr11"), ("qs",), 32)
-    V(lambda e: e.tensor_tensor(T.qf[:, :], T.qs[:, :], T.qr2[:, :], OP.add), ("qs", "qr20", "qr21"), ("qf",), 32)
+            V(lambda e: e.tensor_tensor(T.qs[:, :], T.qr0[:, :, 0:8], T.qr1[:, :, 0:8], OP.add), ("qr00", "qr01", "qr10", "qr11"), ("qs",), 32)
+    V(lambda e: e.tensor_tensor(T.qf[:, :], T.qs[:, :], T.qr2[:, :, 0:8], OP.add), ("qs", "qr20", "qr21"), ("qf",), 32)
     add("Y", lambda e: e.dma_start(T.yq[:, :], T.qf[:, :]), ("qf",), (), (), 2.0, sem="st2", n=16)
     add("Q", lambda e: e.dma_start(T.yc[:, :], T["cw%d" % R][:, :]), ("cw%d" % R,), (), (), 2.0, sem="st3", n=16)
     return ops
 
 
-def schedule(ops, tries):
-    n = len(ops)
-    c = [[{q: cost(q, o["c"], C) for q in (("A", "V") if o["q"] == "AV" else (o["q"],))} for o in ops] for C in COSTS]
-    deps = [(tuple(sorted(o["deps"])), tuple(sorted(o["order"]))) for o in ops]
-    succ, needs = [[] for _ in range(n)], [len(a) + len(b) for a, b in deps]
-    for i, (a, b) in enumerate(deps):
-        for d in a:
-            succ[d].append((i, 0.15, 2))
-        for d in b:
-            succ[d].append((i, 0.0, 1))
-        if "after" in ops[i]:
-            succ[ops[i]["after"]].append((i, 0.0, 0))
-            needs[i] += 1
-    c0, cls, way, rank = c[0], [o.get("cls", -1) for o in ops], [0.0] * n, [0.0] * n
-    for i in range(n - 1, -1, -1):
-        way[i] = min(c0[i].values()) + max([way[s] + h for s, h, _ in succ[i] if cls[s] == cls[i]] or [0.0])
-    top = {k: max(way[i] for i in range(n) if cls[i] == k) for k in set(cls)}
-    for i in range(n - 1, -1, -1):
-        if cls[i] < 0:
-            rank[i] = min([rank[s] for s, _, _ in succ[i]] or [100.0]) - min(c0[i].values()) - 0.5
-        elif succ[i] and all(cls[s] != cls[i] for s, _, _ in succ[i]):
-            rank[i] = min(rank[s] for s, _, _ in succ[i]) - 2
-        else:
-            rank[i] = STRETCH * (top[cls[i]] - way[i]) + PERIOD * (cls[i] // 2) + LAG * (cls[i] % 2)
-    first = [i for i in range(n) if needs[i] == 0]
-    free_to_choose = [i for i in range(n) if ops[i]["q"] == "AV"]
-    queue, end = {"Q": "A"}, [0.0]
-    names = ("A", "V", "P", "G", "Y", "Q", None)
-    hops = [{a: {b: hop(a, b, C) for b in names} for a in names} for C in COSTS]
-
-    def listed(rank, pick):
-        est, order, need = [0.0] * n, [], needs[:]
-        free, low = dict.fromkeys("AVPGY", 0.0), dict.fromkeys("AVPGY", 1e9)
-        ready = {q: [] for q in "AVPGY"}
-        on = [queue.get(q, q) for q in pick]
-
-        def done(i, r, x):
-            order.append(i)
-            wake = hops[0][on[i]]
-            for s, h, k in succ[i]:
-                h = r + x + wake[on[s]] if k == 2 else r + k * x
-                if h > est[s]:
-                    est[s] = h
-                need[s] -= 1
-                if need[s] == 0:
-                    q = on[s]
-                    if q is None:
-                        done(s, est[s], c0[s][None])
-                    else:
-                        ready[q].append(s)
-                        if est[s] < low[q]:
-                            low[q] = est[s]
-        for i in first:
-            ready[on[i]].append(i)
-            low[on[i]] = 0.0
-        while True:
-            q, t = None, 1e8
-            for e in "AVPGY":
-                r = low[e] if low[e] > free[e] else free[e]
-                if r < t:
-                    q, t = e, r
-            if q is None:
-                return order
-            lst, b, bi = ready[q], 1e9, -1
-            for i in lst:
-                if est[i] - t <= 0.005 and rank[i] < b:
-                    b, bi = rank[i], i
-            lst.remove(bi)
-            low[q] = min([est[i] for i in lst]) if lst else 1e9
-            r = est[bi] if est[bi] > t else t
-            x = c0[bi][pick[bi]]
-            free[q] = r + (0.06 if pick[bi] in "YQ" else x)
-            end[0] = r + x
-            done(bi, r, x)
-
-    def spans(order, pick):
-        out = []
-        for wake, cc in zip(hops, c):
-            done, free = [0.0] * n, dict.fromkeys("AVPGY", 0.0)
-            for i in order:
-                r = 0.0
-                a, b = deps[i]
-                q = pick[i]
-                for d in a:
-                    x = done[d] + wake[pick[d]][q]
-                    if x > r:
-                        r = x
-                for d in b:
-                    if done[d] > r:
-                        r = done[d]
-                x = cc[i][q]
-                if q is not None:
-                    e = queue.get(q, q)
-                    if free[e] > r:
-                        r = free[e]
-                    free[e] = r + (0.06 if q in "YQ" else x)
-                done[i] = r + x
-            out.append(max(done))
-        return out, done
-
-    rng = np.random.default_rng(SEED)
-    pick = ["A" if o["q"] == "AV" else o["q"] for o in ops]
-    base = spans(listed(rank, pick), pick)[0]
-    seen, like = {}, {}
-    for i, o in enumerate(ops):
-        seen[cls[i], o["note"]] = seen.get((cls[i], o["note"]), 0) + 1
-        like.setdefault((cls[i] % 2 if cls[i] >= 0 else -1, o["note"], seen[cls[i], o["note"]]), []).append(i)
-    like = {i: v for v in like.values() for i in v}
-
-    def improved(rank, pick, tries):
-        order = listed(rank, pick)
-        sp = spans(order, pick)[0]
-        cur = sum(a / b for a, b in zip(sp, base)) / len(sp)
-        best, now = (cur, rank, pick, order, sp), end[0]
-        for k in range(tries):
-            s2, p2, u, tied = list(rank), list(pick), rng.random(), rng.random() < TIED
-            if u < 0.55:
-                for i in rng.integers(0, n, int(rng.choice([1, 2, 4, 10]))):
-                    d = float(0.5 * rng.normal())
-                    for j in like[i] if tied else (i,):
-                        s2[j] += d
-            elif u < 0.7:
-                a, d = int(rng.integers(0, n)), float(0.5 * rng.normal())
-                for i in range(a, min(n, a + int(rng.integers(5, 60)))):
-                    s2[i] += d
-            else:
-                for i in rng.choice(free_to_choose, int(rng.integers(1, 3))):
-                    q = "V" if p2[i] == "A" else "A"
-                    for j in like[i] if tied else (i,):
-                        p2[j] = q
-            order = listed(s2, p2)
-            if end[0] > 1.006 * now:
-                continue
-            sp = spans(order, p2)[0]
-            f = sum(a / b for a, b in zip(sp, base)) / len(sp)
-            if f < cur + HEAT * (1 - k / tries) * rng.random():
-                cur, rank, pick, now = f, s2, p2, end[0]
-                if f < best[0]:
-                    best = (f, rank, pick, order, sp)
-        return best
-    starts = [improved([r + d * (c % 2 if c >= 0 else 0) for r, c in zip(rank, cls)], pick, tries // 8) for d in (-2, -1, 0, 1)]
-    _, rank, pick, order, sp = improved(*min(starts, key=lambda s: s[0])[1:3], tries // 2)
-    return order, spans(order, pick)[1], pick, (base, sp)
-
-
-def schedule(ops, tries):
+def schedule(ops):
     n, names = len(ops), ("A", "V", "P", "G", "Y", None)
+    tries, PART, SEED, HEAT = OPT["TRIES"], OPT["PART"], OPT["SEED"], OPT["HEAT"]
     home = [names.index({"Q": "A", "AV": "A"}.get(o["q"], o["q"])) for o in ops]
     took = [[[cost(q, o["c"], C) for q in "AV"] if o["q"] == "AV" else [cost(o["q"], o["c"], C)] * 6 for o in ops] for C in COSTS]
     dma = [o["q"] in ("Y", "Q") for o in ops]
@@ -696,16 +410,16 @@ def schedule(ops, tries):
         elif succ[i] and all(cls[s] != cls[i] for s, _ in succ[i]):
             plan[i] = min(plan[s] for s, _ in succ[i]) - 2
         else:
-            plan[i] = STRETCH * (top[cls[i]] - way[i]) + PERIOD * (cls[i] // 2) + LAG * (cls[i] % 2)
+            plan[i] = OPT["STRETCH"] * (top[cls[i]] - way[i]) + OPT["PERIOD"] * (cls[i] // 2) + OPT["LAG"] * (cls[i] % 2)
     first = [i for i in range(n) if needs[i] == 0]
     free_to_choose = [i for i in range(n) if ops[i]["q"] == "AV"]
 
-    def listed(rank, on, hold):
-        est, order, need, last = hold[:], [], needs[:], 0.0
+    def listed(rank, on):
+        est, order, need, last = [0.0] * n, [], needs[:], 0.0
         free, low, ready, h0 = [0.0] * 5, [1e9] * 5, [[] for _ in range(5)], hops[0]
         for i in first:
             ready[on[i]].append(i)
-            low[on[i]] = min(low[on[i]], est[i])
+            low[on[i]] = 0.0
         while True:
             q, t = -1, 1e8
             for e in range(5):
@@ -768,43 +482,16 @@ def schedule(ops, tries):
                 free[q] = r + 0.06 if dma[i] else x
         return done
 
-    base = [max(span(listed(plan, home, [0.0] * n)[0], home, k)) for k in range(len(COSTS))]
+    base = [max(span(listed(plan, home)[0], home, k)) for k in range(len(COSTS))]
 
-    def held_up(order, on):
-        done, before, last, out = span(order, on, 0), {}, [-1] * 6, []
-        for i in order:
-            before[i], last[on[i]] = last[on[i]], i
-        j = done.index(max(done))
-        while j >= 0:
-            q = on[j]
-            t, i = max([(done[d] + hops[0][on[d]][q], d) for d in waits[j]] + [(done[d], d) for d in after[j]] + [(0.0, -1)])
-            if t < done[j] - c0[j][q] - 0.01 and q < 5:
-                i = before[j]
-                out.append((i, j, t))
-            j = i
-        return [x for x in out if x[0] >= 0]
-
-    def improved(rank, on, hold, tries, seed, guide=0.0):
+    def improved(rank, on, tries, seed):
         rng = np.random.default_rng(seed)
-        order, now = listed(rank, on, hold)
+        order, now = listed(rank, on)
         cur = sum(max(span(order, on, k)) / b for k, b in enumerate(base))
-        best, jam = (cur, rank, on, hold, order), held_up(order, on)
+        best = (cur, rank, on, order)
         for k in range(tries):
-            s2, p2, h2, u = rank[:], on, hold, rng.random()
-            if rng.random() < guide and jam:
-                i, j, t = jam[int(rng.integers(len(jam)))]
-                s2[j] = min(s2[j], s2[i] - 0.01)
-                if u < 0.6:
-                    h2 = hold[:]
-                    h2[i] = t + 0.01
-                elif u < 0.8 and ops[i]["q"] == "AV":
-                    p2 = on[:]
-                    p2[i] ^= 1
-            elif u < 0.05:
-                h2 = hold[:]
-                for i in rng.integers(0, n, 40).tolist():
-                    h2[i] = 0.0
-            elif u < 0.55:
+            s2, p2, u = rank[:], on, rng.random()
+            if u < 0.55:
                 for i, d in zip(rng.integers(0, n, (1, 2, 4, 10)[k % 4]).tolist(), rng.normal(0.0, 0.5, 10).tolist()):
                     s2[i] += d
             elif u < 0.7:
@@ -815,23 +502,172 @@ def schedule(ops, tries):
                 p2 = on[:]
                 for i in rng.integers(0, len(free_to_choose), 1 + k % 2).tolist():
                     p2[free_to_choose[i]] ^= 1
-            order, end = listed(s2, p2, h2)
-            if guide:
-                end = max(span(order, p2, 0))
+            order, end = listed(s2, p2)
             if end > 1.006 * now:
                 continue
             f, lim = end / base[0], cur + HEAT * (1 - k / tries) * rng.random()
             for j in range(1, len(base)):
                 f += max(span(order, p2, j)) / base[j]
             if f < lim:
-                cur, rank, on, hold, now, jam = f, s2, p2, h2, end, held_up(order, p2) if guide else []
+                cur, rank, on, now = f, s2, p2, end
                 if f < best[0]:
-                    best = (f, rank, on, hold, order)
+                    best = (f, rank, on, order)
         return best
-    starts = [improved([r + d * (c % 2 if c >= 0 else 0) for r, c in zip(plan, cls)], home, [0.0] * n, tries // PART, SEED + d + 2) for d in (-2, -1, 0, 1)]
-    _, rank, on, hold, order = improved(*min(starts, key=lambda s: s[0])[1:4], tries - 4 * (tries // PART), SEED + 9)
+    lags = OPT["LAGS"]
+    starts = [improved([r + d * (c % 2 if c >= 0 else 0) for r, c in zip(plan, cls)], home, tries // PART, SEED + k) for k, d in enumerate(lags)]
+    _, rank, on, order = improved(*min(starts, key=lambda s: s[0])[1:3], tries - len(lags) * (tries // PART), SEED + 9)
     pick = ["AV"[q] if o["q"] == "AV" else o["q"] for o, q in zip(ops, on)]
     return order, span(order, on, 0), pick, (base, [max(span(order, on, k)) for k in range(len(COSTS))])
+
+
+def refine(ops, order, pick, tries, seed, heat, costs=COSTS):
+    n, names, nm = len(ops), ("A", "V", "P", "G", "Y", None), len(costs)
+    on = [names.index({"Q": "A"}.get(q, q)) for q in pick]
+    took = [[[cost(q, o["c"], C) for q in "AV"] if o["q"] == "AV" else [cost(o["q"], o["c"], C)] * 6 for o in ops] for C in costs]
+    dma = [o["q"] in ("Y", "Q") for o in ops]
+    hops = [[[hop(a, b, C) for b in names] for a in names] for C in costs]
+    anc, waits, after, pred, succ = [0] * n, [], [], [], [set() for _ in range(n)]
+    for i, o in enumerate(ops):
+        m = 0
+        for d in o["deps"] | o["order"]:
+            m |= anc[d]
+        waits.append([d for d in sorted(o["deps"]) if not m >> d & 1])
+        after.append([d for d in sorted(o["order"]) if not m >> d & 1])
+        pred.append(set(waits[i] + after[i] + ([o["after"]] if "after" in o else [])))
+        for d in pred[i]:
+            m |= 1 << d
+            succ[d].add(i)
+        anc[i] = m
+    flex = [o["q"] == "AV" for o in ops]
+
+    def span(order, on, k, p0, old):
+        wake, cc, done, free = hops[k], took[k], old[:], [0.0] * 6
+        seen = 0
+        for p in range(p0 - 1, -1, -1):
+            i = order[p]
+            q = on[i]
+            if q < 5 and not seen >> q & 1:
+                seen |= 1 << q
+                free[q] = done[i] - cc[i][q] + 0.06 if dma[i] else done[i]
+                if seen & 7 == 7 and p0 > 90:
+                    break
+        for i in order[p0:]:
+            q = on[i]
+            r = free[q]
+            for d in waits[i]:
+                x = done[d] + wake[on[d]][q]
+                if x > r:
+                    r = x
+            if q > 1 or dma[i]:
+                for d in after[i]:
+                    if done[d] > r:
+                        r = done[d]
+                done[i] = x = r + cc[i][q]
+                if q < 5:
+                    free[q] = r + 0.06 if dma[i] else x
+            else:
+                free[q] = done[i] = r + cc[i][q]
+        return done
+
+    def jams(order, on, k, done):
+        before, last, out = {}, [-1] * 6, []
+        for i in order:
+            before[i], last[on[i]] = last[on[i]], i
+        j = done.index(max(done))
+        wake, cc = hops[k], took[k]
+        while j >= 0:
+            q, t, i = on[j], 0.0, -1
+            for d in waits[j]:
+                x = done[d] + wake[on[d]][q]
+                if x > t:
+                    t, i = x, d
+            for d in after[j]:
+                if done[d] > t:
+                    t, i = done[d], d
+            if t < done[j] - cc[j][q] - 1e-6 and q < 5:
+                i = before[j]
+                if i >= 0:
+                    out.append((i, j))
+            j = i
+        return out
+
+    def shifted(order, pi, pj, back):
+        x0, link = (order[pi], succ) if back else (order[pj], pred)
+        need, tied, rest = set(link[x0]), [x0], []
+        for x in order[pi + 1:pj + 1] if back else order[pi:pj][::-1]:
+            if x in need:
+                tied.append(x)
+                need |= link[x]
+            else:
+                rest.append(x)
+        if tied[-1] == order[pj if back else pi]:
+            return None
+        return order[:pi] + (rest + tied if back else tied[::-1] + rest[::-1]) + order[pj + 1:]
+
+    rng = np.random.default_rng(seed)
+    zero = [0.0] * n
+    done = [span(order, on, k, 0, zero) for k in range(nm)]
+    base = [max(d) for d in done]
+    val = lambda d, k: (max(d) + 0.02 * sum(d) / n) / base[k]
+    vals = [val(done[k], k) for k in range(nm)]
+    best, jam, age = (sum(vals), order, on), {}, 99
+    for it, u in enumerate(rng.random((tries, 6)).tolist()):
+        if age > 8:
+            st = [done[0][i] - took[0][i][on[i]] for i in range(n)]
+            order, age = sorted(order, key=lambda i: st[i]), 0
+        on2, x = on, -1
+        if u[1] < 0.7:
+            k = int(u[0] * nm)
+            if k not in jam:
+                jam[k] = jams(order, on, k, done[k])
+            i, j = jam[k][int(u[2] * len(jam[k]))]
+            if u[3] < 0.25 and (flex[i] or flex[j]):
+                x = i if flex[i] and (not flex[j] or u[4] < 0.5) else j
+                p0 = order.index(x)
+            else:
+                p0, q, far = order.index(i), on[i], int(u[4] * 3)
+                p1 = order.index(j, p0)
+                while far and u[3] < 0.6 and p0 > 0:
+                    p0 -= 1
+                    far -= on[order[p0]] == q
+                while far and u[3] >= 0.6 and p1 < n - 1:
+                    p1 += 1
+                    far -= on[order[p1]] == q
+                o2 = shifted(order, p0, p1, u[3] >= 0.6)
+        else:
+            p0 = p1 = int(u[2] * n)
+            if flex[order[p0]] and u[3] < 0.4:
+                x = order[p0]
+            elif u[3] < 0.7:
+                p0 = max(0, p1 - 1 - int(u[4] * 12))
+                o2 = shifted(order, p0, p1, False)
+            else:
+                o2 = shifted(order, p0, min(n - 1, p0 + 1 + int(u[4] * 12)), True)
+        if x >= 0:
+            on2, o2 = on[:], order
+            on2[x] ^= 1
+        if o2 is None:
+            continue
+        slack = -heat * (1 - it / tries) * np.log(u[5])
+        d2, v2 = [], []
+        for k in range(nm):
+            d2.append(span(o2, on2, k, p0, done[k]))
+            v2.append(val(d2[k], k))
+            if sum(v2) - sum(vals[:k + 1]) > slack + 0.002 * (nm - 1 - k):
+                break
+        else:
+            order, on, done, vals, jam, age = o2, on2, d2, v2, {}, age + 1
+            if sum(vals) < best[0]:
+                best = (sum(vals), order, on)
+    _, order, on = best
+    pick = ["AV"[q] if o["q"] == "AV" else o["q"] for o, q in zip(ops, on)]
+    done = [span(order, on, k, 0, zero) for k in range(nm)]
+    return order, done[0], pick, [max(d) for d in done]
+
+
+def planned(ops):
+    order, _, pick, _ = schedule(ops)
+    return refine(ops, order, pick, OPT["MOVES"], OPT["SEED"], OPT["WARM"])
 
 
 _CACHE = {}
@@ -842,7 +678,7 @@ def rank_program(g, core, T, topo):
         return
     ops = build(core, T, topo, [g.vector])
     if "order" not in _CACHE:
-        _CACHE["order"] = schedule(ops, TRIES)
+        _CACHE["order"] = planned(ops)
     order, done, pick, _ = _CACHE["order"]
     for i, o in enumerate(ops):
         o["q"] = pick[i]

import numpy as np
from concourse.mybir import AluOpType, ActivationFunctionType

OP = AluOpType
AF = ActivationFunctionType
R, NB, HOP = 3, 16, 3
KAP = (101, 1303, 2717, 3911)
W = 2048
TW = W + 16
BIG = 1.5 * 2.0 ** 34

SCRATCH = {
    "xw": ("sbuf", [128, 2 * W + 4 * TW], "bfloat16"),
    "tu": ("sbuf", [128, 130], "float32"),
    "sq": ("sbuf", [128, 130], "float32"),
    "xa": ("sbuf", [128, 130], "int32"),
    "xb": ("sbuf", [128, 130], "int32"),
    "xl": ("sbuf", [128, 4 * 130], "uint16"),
    "bni": ("sbuf", [128, 256], "int32"),
    "cni": ("sbuf", [128, 256], "int32"),
    "wti": ("sbuf", [128, 1], "int32"),
    "thi": ("sbuf", [128, 1], "int32"),
    "pi": ("sbuf", [128, 8], "int32"),
    "pj": ("sbuf", [128, 8], "int32"),
    "pf": ("sbuf", [128, 8], "float32"),
    "col": ("sbuf", [128, 16], "float32"),
    "ones": ("sbuf", [128, 128], "bfloat16"),
    "m1": ("sbuf", [128, 128], "bfloat16"),
    "bo": ("sbuf", [128, 128], "bfloat16"),
    "bok": ("sbuf", [128, 128], "bfloat16"),
    "nbok": ("sbuf", [128, 128], "bfloat16"),
    "bow": ("sbuf", [128, 128], "bfloat16"),
    "ident": ("sbuf", [128, 128], "bfloat16"),
    "nident": ("sbuf", [128, 128], "bfloat16"),
    "zw": ("sbuf", [128, 144], "bfloat16"),
    "z16": ("sbuf", [128, 144], "bfloat16"),
    "prow": ("sbuf", [128, 16], "float32"),
    "diag": ("sbuf", [128, 16], "bfloat16"),
    "cini": ("sbuf", [128, 56], "bfloat16"),
    "nn": ("sbuf", [128, 24], "bfloat16"),
    "nd": ("sbuf", [128, 16], "bfloat16"),
    "ns": ("sbuf", [128, 8], "float32"),
    "sp": ("sbuf", [128, 16], "bfloat16"),
    "inv": ("sbuf", [128, 16], "uint16"),
    "ms": ("sbuf", [128, 272], "float32"),
    "qs": ("sbuf", [128, 16], "float32"),
    "qf": ("sbuf", [128, 16], "float32"),
}
for _t in range(R + 1):
    SCRATCH["cw%d" % _t] = ("sbuf", [128, 256], "float32")
for _t in range(R):
    SCRATCH["qr%d" % _t] = ("sbuf", [128, 2, 16], "bfloat16")
    for _h in range(2):
        SCRATCH["lt%d%d" % (_t, _h)] = ("sbuf", [128, 128], "uint16")
        SCRATCH["ls%d%d" % (_t, _h)] = ("sbuf", [128, 128], "uint16" if _t < R - 1 else "float32")
for _h in range(2):
    for _n, _s, _d in (("fa", [128, 2048], "bfloat16"), ("dc", [128, 1024], "bfloat16"), ("ac", [128, 16, 128], "bfloat16"),
                       ("ia", [128, 128], "float32"), ("lu", [128, 128], "uint16"),
                       ("wd", [128, 3, 128], "bfloat16"), ("qi", [128, 24], "int32"), ("fr", [128, 32], "float32"),
                       ("go", [128, 8], "uint16"), ("rr", [128, 8], "float32"), ("tb", [128, 128], "float32"),
                       ("lo", [128, 8], "uint16"), ("wm", [128, 32], "float32")):
        SCRATCH["%s_%d" % (_n, _h)] = ("sbuf", _s, _d)
    for _n in ("S", "F"):
        SCRATCH["%s_%d" % (_n, _h)] = ("psum", [128, 64, 8], "float32")
for _k in range(4):
    SCRATCH["X%d" % _k] = ("psum", [128, 8, 64], "float32")

DMAS = ["ld%d" % _k for _k in range(7)] + ["st%d" % _k for _k in range(4)]
SEMAPHORES = ["V", "A", "P", "G", "sent"] + DMAS + ["al%d%d" % (_t, _h) for _t in (1, 2) for _h in (0, 1)]

COSTS = ({"cy": 0.00083, "V": 0.04, "A": 0.06, "P": 0.00048, "g": 1.56, "hop": (0.19, 0.15, 0.14), "dma": 0.8},
         {"cy": 0.00104, "V": 0.04, "A": 0.07, "P": 0.00056, "g": 1.3, "hop": (0.20, 0.17, 0.17), "dma": 0.8},
         {"cy": 0.00100, "V": 0.05, "A": 0.07, "P": 0.00058, "g": 1.9, "hop": (0.18, 0.14, 0.11), "dma": 0.7},
         {"cy": 0.00116, "V": 0.05, "A": 0.08, "P": 0.00066, "g": 1.6, "hop": (0.22, 0.16, 0.16), "dma": 1.0})


def hop(a, b, c):
    return c["hop"][0 if a == b else 1 if a == "V" else 2]


def cost(q, n, c):
    if q == "G":
        return n
    if q not in ("A", "V", "P"):
        return n * c["dma"]
    if q == "P":
        return n * c["P"]
    if isinstance(n, tuple):
        if n[0] == "h":
            return c[q] + max(64, n[1] if q == "A" else n[1] // 2) * c["cy"]
        return (0.065 if q == "A" else 0.05) + n[1] * c[n[0]] * c["cy"]
    return c[q] + max(64, n) * c["cy"]


OPT = {"CH": (4, 2, 1, 1),
       "J0": False, "TCH": 4, "FIRST": 0.6,
       "PERIOD": 22.0, "LAG": 3.0, "LAGS": (-1, 0, 1), "STRETCH": 1.15, "HEAT": 0.006, "PART": 8, "SEED": 7, "TRIES": 1200,
       "MOVES": 120000, "WARM": 0.002}


def build(core, T, topo, VEC):
    ops, lastw, readers, banks = [], {}, {}, {}
    CH, TCH = OPT["CH"], OPT["TCH"]

    def add(q, fn, rd=(), wr=(), bk=(), c=0.1, sem=None, n=1, note="", acc=False):
        deps, order = set(), set()
        for k in rd:
            if k in lastw:
                deps.add(lastw[k])
        for k in wr:
            if k in lastw:
                deps.add(lastw[k])
            deps.update(readers.get(k, ()))
        for b in bk:
            for e, o in banks.get(b, {}).items():
                if e != q:
                    deps.add(o)
                else:
                    order.add(o)
        me = len(ops)
        for k in wr:
            lastw[k], readers[k] = me, []
        for k in rd:
            readers.setdefault(k, []).append(me)
        for b in bk:
            banks.setdefault(b, {})[q] = me
        if acc:
            order |= {d for d in deps if ops[d]["q"] == "P"}
            deps -= order
        ops.append({"q": q, "fn": fn, "deps": deps, "order": order - deps, "c": c, "sem": sem, "n": n, "note": note})
        return me

    def V(fn, rd, wr, n, bk=(), note=""):
        return add("V", fn, rd, wr, bk, n, note=note)

    def A(fn, rd, wr, n, bk=(), note=""):
        return add("A", fn, rd, wr, bk, n, note=note)

    def P(fn, rd, wr, n, bk=(), note="", acc=False):
        return add("P", fn, rd, wr, bk, n, note=note, acc=acc)

    def G(fn, rd, wr, c, note=""):
        return add("G", fn, rd, wr, (), c, note=note)

    def load(q, k, out, in_, wr, c):
        return add(q, lambda e: e.dma_start(out, in_), (), wr, (), c, sem="ld%d" % k, n=16, note="load")

    gat = lambda n: ("g", n)

    def gather_on(e, out, ind):
        if e is VEC[0]:
            return e.tensor_copy(out, ind)
        return e.activation(out, ind, AF.Identity)

    def scale_on(e, out, in_, s, b=None):
        if e is VEC[0]:
            return e.tensor_scalar(out, in_, s, None, OP.mult) if b is None else e.tensor_scalar(out, in_, s, b, OP.mult, OP.add)
        return e.activation(out, in_, AF.Identity, scale=s) if b is None else e.activation(out, in_, AF.Identity, bias=b, scale=s)

    def either(fn, rd, wr, n, note=""):
        add("AV", fn, rd, wr, (), n, note=note)

    prev = load("Y", 0, T.bni[:, 0:128], T.bn[:, 0:128], ("bn0",), 2.2)
    load("Q", 1, T.xw[:, 0:W], T.xf[:, :], ("xw",), 4.0)
    for k, out, in_, key, c in ((2, T.wti[:, :], T.wt[:, :], "wti", 4.2), (4, T.bni[:, 128:256], T.bn[:, 128:256], "bn1", 4.5),
                                (6, T.xw[:, W:2 * W], T.xf[:, :], "xw2", 7.0),
                                (3, T.thi[:, :], T.th[:, :], "thi", 7.2), (5, T.cni[:, :], T.cn[:, :], "cni", 7.7)):
        o = load("Y", k, out, in_, (key,), c)
        ops[o]["after"] = prev
        prev = o

    col = lambda k: T.col[:, k:k + 1]
    ICOL, SQB, WCOL, W16, THC, GOC = range(6)
    whole = lambda out, pattern, base, cm, key, c=0.2: G(lambda e: e.iota(out, pattern, base, cm, allow_small_or_imprecise_dtypes=True), (), (key,), c)
    fill = lambda out, n, v, key: G(lambda e: e.affine_select(out, T.ones[:, 0:n], [[0, n]], OP.is_ge, v, -1, 0), ("ones",), (key,), 0.2)
    G(lambda e: e.iota(T.pi[:, 0:1], [[0, 1]], 0, 1), (), ("pi",), 0.2)
    whole(T.pf[:, 0:1], [[0, 1]], 592, -1, "pf")
    whole(T.tu[:, 0:128], [[-1024, 2], [16, 64]], 1024, 1, "tu", 0.34)
    whole(T.tu[:, 128:130], [[0, 2]], 1024, 1, "tu2")
    V(lambda e: e.memset(T.ones[:, :], 1.0), (), ("ones",), 64)
    G(lambda e: e.affine_select(T.ident[:, :], T.ones[:, :], [[-1, 128]], OP.is_equal, 0.0, 0, 1), ("ones",), ("ident",), 0.4)
    G(lambda e: e.affine_select(T.m1[:, :], T.ones[:, :], [[-16, 8], [0, 16]], OP.is_ge, 0.0, 0, 1), ("ones",), ("m1",), 0.4)
    G(lambda e: e.affine_select(T.bo[:, :], T.m1[:, :], [[16, 8], [0, 16]], OP.is_ge, 0.0, 15, -1), ("m1",), ("bo",), 0.4)
    whole(T.prow[:, :], [[1, 16]], 0, 0, "prow")
    V(lambda e: e.memset(T.z16[:, :], 0.0), (), ("z16",), 72)
    V(lambda e: e.tensor_scalar(T.pj[:, 0:1], T.pi[:, 0:1], 15, None, OP.bitwise_and), ("pi",), ("pj",), 8)
    V(lambda e: e.tensor_copy(col(ICOL), T.pj[:, 0:1]), ("pj",), ("icol",), 8)
    for h in range(2):
        V(lambda e, h=h: e.tensor_copy(T["lt0%d" % h][:, :], T.bni[:, 128 * h:128 * h + 128]), ("bn%d" % h,), ("lt0%d" % h,), 128)
    A(lambda e: e.activation(col(SQB), col(ICOL), AF.Identity, bias=T.pf[:, 0:1]), ("icol", "pf"), ("sqb",), 8)
    A(lambda e: e.activation(T.sq[:, :], T.tu[:, :], AF.Square, bias=col(SQB)), ("tu", "tu2", "sqb"), ("sq",), 128)
    V(lambda e: e.tensor_scalar(T.xa[:, :], T.sq[:, :], float((32 * KAP[0] - 592 * 592) % 65536), None, OP.add), ("sq",), ("xa",), 128)
    V(lambda e: e.tensor_scalar(T.xb[:, :], T.xa[:, :], 5, W - 1, OP.arith_shift_right, OP.bitwise_and), ("xa",), ("xb",), 128)
    for l in range(4):
        V(lambda e, l=l: e.tensor_scalar(T.xl[:, 130 * l:130 * l + 130], T.xb[:, :], float((KAP[l] - KAP[0]) % W), None, OP.add), ("xb",), ("xl%d" % l,), 128)
        for c in range(TCH):
            k0, k1, x0 = 128 // TCH * c, 128 // TCH * (c + 1) + (c == TCH - 1), 2 * W + TW * l
            either(lambda e, l=l, k0=k0, k1=k1, x0=x0: gather_on(e, T.xw[:, x0 + 16 * k0:x0 + 16 * k1], T.xw[:, 0:2 * W if l else W].indirect(T.xl[:, 130 * l + k0:130 * l + k1])),
                   ("xw", "xl%d" % l) + (("xw2",) if l else ()), ("x%d%d" % (l, c),), gat(16 * (k1 - k0)), "table")
    either(lambda e: scale_on(e, T.nident[:, :], T.ident[:, :], -1.0), ("ident",), ("nident",), ("h", 128))
    either(lambda e: scale_on(e, T.z16[:, 15:128:16], T.bo[:, 0:128:16], 0.0625), ("bo",), ("z16",), 8)
    V(lambda e: e.tensor_scalar(col(WCOL), T.wti[:, :], 16.0, None, OP.mult), ("wti",), ("wcol",), 8)
    either(lambda e: scale_on(e, T.zw[:, :], T.z16[:, :], col(WCOL)), ("z16", "wcol"), ("zw",), ("h", 144))
    V(lambda e: e.tensor_scalar(col(THC), T.thi[:, :], -0.0625, -15.0 / 32, OP.mult, OP.add), ("thi",), ("thc",), 8)
    either(lambda e: scale_on(e, T.cini[:, 24:32], T.ones[:, 0:8], col(THC)), ("ones", "thc"), ("tini0",), 8)
    A(lambda e: e.activation(T.cini[:, 40:48], T.cini[:, 24:32], AF.Identity, bias=col(THC), scale=-1.0), ("tini0", "thc"), ("tini1",), 8)
    V(lambda e: e.tensor_scalar(T.bow[:, :], T.bo[:, :], col(WCOL), 1.0 / 256, OP.mult, OP.mult), ("bo", "wcol"), ("bow",), 64)
    either(lambda e: scale_on(e, T.bok[:, :], T.bo[:, :], 256.0), ("bo",), ("bok",), ("h", 128))
    either(lambda e: scale_on(e, T.nbok[:, :], T.bo[:, :], -256.0), ("bo",), ("nbok",), ("h", 128))
    V(lambda e: e.tensor_scalar(T.diag[:, :], T.prow[:, :], col(ICOL), None, OP.is_equal), ("prow", "icol"), ("diag",), 16)
    fill(T.cini[:, 8:24], 16, -15.0 / 32, "cini1")
    fill(T.cini[:, 32:40], 8, 1.0 / 32, "cini2")
    whole(T.cini[:, 48:56], [[2, 8]], 0, 0, "cini3")
    A(lambda e: e.activation(col(W16), col(ICOL), AF.Identity, bias=-15.0 / 32, scale=-0.0625), ("icol",), ("w16",), 8)
    either(lambda e: scale_on(e, T.cini[:, 0:8], T.ones[:, 0:8], col(W16)), ("ones", "w16"), ("cini0",), 8)
    A(lambda e: e.activation(col(GOC), col(ICOL), AF.Identity, bias=120.0), ("icol",), ("goc",), 8)
    fill(T.nn[:, 0:1], 1, -13.0 / 32, "nn")
    whole(T.ms[:, 256:272], [[0, 16]], 0, 0, "msz")
    for h in range(2):
        whole(T["fr_%d" % h][:, 24:32], [[0, 8]], 0, 0, "frz_%d" % h)
        whole(T["wm_%d" % h][:, 0:16], [[0, 16]], 0, 0, "wmz_%d" % h)
    V(lambda e: e.tensor_scalar(T.cw0[:, :], T.cni[:, :], -1.0, None, OP.mult), ("cni",), ("cw0",), 256)

    def half(t, h):
        B = lambda n: T["%s_%d" % (n, h)]
        K = lambda n: "%s_%d" % (n, h)
        SF = (B("S"), B("F"))
        S, F = SF
        lt, klt = T["lt%d%d" % (t, h)], "lt%d%d" % (t, h)
        cw = T["cw%d" % t]
        fa, dc, ac, lu = B("fa"), B("dc"), B("ac"), B("lu")
        zs = lambda z, i: z[:, 15 - i:143 - i]
        units = lambda name, x0, m: tuple(K("%s%d" % (name, u)) for u in range(x0 // 128, (x0 + m) // 128))
        both = lambda x0, m: units("ac", x0, m) + units("ad", x0, m)

        def index(src, ks, bank, c0, n):
            ka, wr = tuple(K("ia%d" % u) for u in range(c0 // 64, (c0 + n + 63) // 64)), tuple(K("lu%d" % u) for u in range(c0 // 64, (c0 + n + 63) // 64))
            V(lambda e: e.tensor_scalar(B("ia")[:, c0:c0 + n], src, BIG, BIG + W, OP.add, OP.subtract), ks, ka, n, (bank,), note="i1")
            V(lambda e: e.tensor_tensor(lu[:, c0:c0 + n], src, B("ia")[:, c0:c0 + n], OP.subtract), ka + ks, wr, n, (bank,), note="i2")

        def table(l):
            keys = tuple("x%d%d" % (k, c) for k in (l - 1, l) for c in range(TCH) if k >= 0)
            return T.xw[:, 2 * W + TW * l - W // 2:2 * W + TW * (l + 1)], keys + ("xw2",)

        m = 2048 // CH[0]
        for c in range(CH[0]):
            either(lambda e, c=c, m=m: gather_on(e, fa[:, m * c:m * c + m], T.xw[:, 0:W].indirect(lt[:, m // 16 * c:m // 16 * (c + 1)])), (klt, "xw"), units("fa", m * c, m), gat(m), "g0")
        for q in range(2):
            x0 = 1024 * q
            for s in range(2):
                X, kX = T["X%d" % (2 * q + s)], "X%d" % (2 * q + s)
                if s == 0:
                    for b0 in (0, 2):
                        def cols(e, X=X, x0=x0, b0=b0):
                            for b in (b0, b0 + 1):
                                e.matmul(X[:, :, 16 * b:16 * b + 16], T.ident[:, :], fa[:, x0 + 256 * b:x0 + 256 * b + 128], b == 0, False)
                                o = e.matmul(X[:, :, 16 * b:16 * b + 16], T.nident[:, :], fa[:, x0 + 256 * b + 128:x0 + 256 * b + 256], False, b == 3)
                            return o
                        P(cols, units("fa", x0 + 256 * b0, 512) + ("ident", "nident"), (kX,), 512, (kX,), note="col", acc=b0 > 0)
                else:
                    def rows(e, X=X, x0=x0):
                        for c in range(8):
                            e.matmul(X[:, c, :], T.ident[:, :], fa[:, x0 + c:x0 + 1024:16], c == 0, False)
                            o = e.matmul(X[:, c, :], T.nident[:, :], fa[:, x0 + c + 8:x0 + 1024:16], False, c == 7)
                        return o
                    P(rows, units("fa", x0, 1024) + ("ident", "nident"), (kX,), 1024, (kX,), note="row")
                A(lambda e, X=X, s=s, q=q: e.activation(ac[:, 8 * s:8 * s + 8, 64 * q:64 * q + 64], X[:, :, :], AF.Abs), (kX,), units(("ac", "ad")[q], 1024 * s, 1024), 512, (kX,), note="abs0")
            if OPT["J0"]:
                def wq(e, q=q):
                    for i in range(16):
                        o = e.matmul(S[:, 0:16, 4 * q:4 * q + 4], zs(T.zw, i), ac[:, :, 64 * q + i:64 * q + 64:16], q + i == 0, q + i == 16)
                    return o
                P(wq, units(("ac", "ad")[q], 0, 2048) + ("zw",), (K("S0"),), 1024, (K("S"),), note="weigh", acc=q > 0)

        def weigh(s, n):
            def fn(e):
                for i in range(16):
                    o = e.matmul(SF[s][:, 0:n // 128, :], zs(T.zw, i), ac[:, 8 * s:8 * s + n // 128, i:128:16], i == 0, i == 15)
                return o
            P(fn, both(1024 * s, n) + ("zw",), (K("S%d" % s),), 1024, (K("SF"[s]),), note="weigh")
            index(SF[s][:, 0:n // 128, :], (K("S%d" % s),), K("SF"[s]), 64 * s, n // 16)

        if OPT["J0"]:
            index(S[:, 0:16, :], (K("S0"),), K("S"), 0, 128)
        else:
            for s in range(2):
                weigh(s, 1024)

        for l, n in ((1, 512), (2, 256), (3, 128)):
            w, wk = table(l - 1)
            m, k = n // CH[l], n // CH[l] // 16
            for s in range(2):
                kl = (K("lu%d" % s),) + wk
                for c in range(CH[l]):
                    either(lambda e, x0=512 * s + m * c, c0=64 * s + k * c, m=m, k=k, w=w: gather_on(e, fa[:, x0:x0 + m], w.indirect(lu[:, c0:c0 + k])),
                           kl, units("fa", 512 * s + m * c, m), gat(m), "gA")
                for c in range(CH[l]):
                    V(lambda e, x0=512 * s + m * c, c0=64 * s + n // 16 + k * c, m=m, k=k, w=w: e.tensor_tensor(dc[:, x0:x0 + m], w.indirect(lu[:, c0:c0 + k]), fa[:, x0:x0 + m], OP.subtract),
                      kl + units("fa", 512 * s + m * c, m), units("dc", 512 * s + m * c, m), gat(m), note="gB")
                for c in range(CH[l]):
                    A(lambda e, x0=512 * s + m * c, r0=8 * s + m * c // 128, m=m: e.activation(ac[:, r0:r0 + m // 128, :], dc[:, x0:x0 + m], AF.Abs),
                      units("dc", 512 * s + m * c, m), both(1024 * s + m * c, m), m, note="abs")
                weigh(s, n)

        w, wk = table(3)
        wd, qi, fr, nn, wm = B("wd"), B("qi"), B("fr"), T.nn, B("wm")
        Z, DG, Act, kS, kF = S[:, 32:35, :], F[:, 32:34, :], S[:, 40, :], K("S"), K("F")
        P(lambda e: e.matmul(Z, T.ident[:, :], T.cini[:, 0:24], True, False), ("ident", "cini0", "cini1"), (K("Z"),), 64, (kS,), note="zini")

        def dini(e):
            e.matmul(DG, T.ident[:, :], T.cini[:, 24:40], True, False)
            return e.matmul(F[:, 32, :], T.ident[:, :], T.cini[:, 40:48], False, False)
        P(dini, ("ident", "cini2", "tini0", "tini1"), (K("D"),), 128, (kF,), note="dini")
        either(lambda e: gather_on(e, wd[:, 0, :], w.indirect(lu[:, 0:8])), wk + (K("lu0"),), (K("wc"),), gat(128), "gWC")
        V(lambda e: e.tensor_tensor(wd[:, 2, :], w.indirect(lu[:, 64:72]), wd[:, 0, :], OP.subtract), wk + (K("lu1"), K("wc")), (K("dw"),), gat(128), note="gWR")
        A(lambda e: e.activation(wd[:, 1, :], wd[:, 2, :], AF.Abs), (K("dw"),), (K("aw"),), 128, note="absW")

        def asum(e):
            e.matmul(S[:, 32, :], T.bow[:, :], wd[:, 0, 0:128:16], False, False)
            e.matmul(S[:, 33, :], T.bow[:, :], wd[:, 0, 0:128:16], False, False)
            for i in range(16):
                o = e.matmul(S[:, 34, :], zs(T.z16, i), wd[:, 0, i:128:16], False, i == 15)
            return o
        P(asum, (K("wc"), "z16", "bow"), (K("Z"),), 1152, (kS,), note="A", acc=True)

        def dsum(e):
            for i in range(16):
                o = e.matmul(DG, zs(T.z16, i), wd[:, 1:3, i:128:16], False, i == 15)
            return o
        P(dsum, (K("dw"), K("aw"), "z16"), (K("D"),), 1024, (kF,), note="D", acc=True)
        V(lambda e: e.tensor_copy(qi[:, :], Z), (K("Z"),), (K("qi"),), 24, (kS,), note="q")
        V(lambda e: e.tensor_tensor(fr[:, 0:24], Z, qi[:, :], OP.subtract), (K("Z"), K("qi")), (K("fr"),), 24, (kS,), note="frac")
        V(lambda e: e.tensor_tensor_scan(nn[:, 8 * h + 1:8 * h + 9], fr[:, 0:8], fr[:, 0:8], nn[:, 8 * h:8 * h + 1], OP.min, OP.min),
          (K("fr"), "nn0" if h else "nn"), ("nn%d" % h,), 16, note="scan")
        V(lambda e: e.tensor_scalar(B("go")[:, :], fr[:, 8:16], 256.0, col(GOC), OP.mult, OP.add), (K("fr"), "goc"), (K("go"),), 8, note="go")

        def act(e):
            e.matmul(Act, T.ident[:, :], T.cini[:, 48:56], True, False)
            e.matmul(Act, T.bok[:, :], nn[:, 8 * h:8 * h + 8], False, False)
            return e.matmul(Act, T.nbok[:, :], nn[:, 8 * h + 1:8 * h + 9], False, True)
        P(act, ("nn", "nn0", "nn%d" % h, "bok", "nbok", "ident", "cini3"), (K("Act"),), 192, (kS,), note="act")
        qr, kq = T["qr%d" % t], "qr%d%d" % (t, h)
        neg = t % 2 == 0
        V(lambda e: e.tensor_tensor(B("tb")[:, :], cw[:, :].indirect(B("go")[:, :]), lt[:, :], OP.add if neg else OP.subtract), ("cw%d" % t, K("go"), klt), (K("tb"),), gat(128), note="T")
        V(lambda e: e.tensor_tensor(qr[:, h, :], DG, fr[:, 16:32], OP.is_gt), (K("D"), K("fr"), K("frz")), (kq,), 16, (kF,), note="qs")
        V(lambda e: e.tensor_tensor(B("rr")[:, :], qr[:, h, 0:8], qr[:, h, 8:16], OP.is_gt), (kq,), (K("rr"),), 16, note="r")
        V(lambda e: e.tensor_tensor(wm[:, 16:32:2], qr[:, h, 0:8], qr[:, h, 8:16], OP.min), (kq,), (K("wc1"),), 16, note="c")
        V(lambda e: e.tensor_tensor(B("lo")[:, :], Act, B("rr")[:, :], OP.add), (K("Act"), K("rr")), (K("lo"),), 8, (kS,), note="o")
        either(lambda e: scale_on(e, wm[:, 17:32:2], wm[:, 16:32:2], -1.0, 1.0), (K("wc1"),), (K("wc0"),), 8, "nc")
        ms, ls, kls = T.ms[:, 128 * h:128 * h + 128], T["ls%d%d" % (t, h)], "ls%d%d" % (t, h)
        V(lambda e: e.tensor_tensor(ms, wm[:, :].indirect(B("lo")[:, :]), B("tb")[:, :], OP.mult), (K("wc0"), K("wc1"), K("wmz"), K("lo"), K("tb")), (K("ms"),), gat(128), note="M")
        V(lambda e: e.tensor_tensor(ls[:, :], lt[:, :], ms, OP.subtract if neg else OP.add), (klt, K("ms")), (kls,), 256, note="ls")
        if t < R - 1:
            dst = T.cores[(T.rank_of(core) + HOP) % len(T.cores)]
            rid, pid, _ = topo.addr(dst)
            engines = topo.engines(core, dst)
            el = engines[h::2] if t == 0 else engines
            o = add("G", lambda e: e.remote_dma(T["lt%d%d" % (t + 1, h)][:, :], ls[:, :], T.sem["al%d%d" % (t + 1, h)], T.sem["sent"], pid, rid, sum(1 << en for en in el)),
                    (kls,), (), (), 0.3, sem="-sent", n=len(el), note="send")
            arr = add(None, None, (), ("lt%d%d" % (t + 1, h),), (), 2.0 + (OPT["FIRST"] if t + h == 0 else 0.0), sem="al%d%d" % (t + 1, h), n=len(el))
            ops[arr]["order"].add(o)
        else:
            add("Y", lambda e: e.dma_start(T.yb[:, 128 * h:128 * h + 128], ls[:, :]), (kls,), (), (), 2.0, sem="st%d" % h, n=16)
        if h == 1:
            A(lambda e: e.activation(T.nd[:, :], nn[:, 1:17], AF.Identity, bias=15.0 / 32, accum_out=T.ns[:, 0:1]), ("nn0", "nn1"), ("ns",), 90, note="nsum")
            either(lambda e: scale_on(e, T.sp[:, :], T.diag[:, :], T.ns[:, 0:1]), ("diag", "ns"), ("sp",), 16, "spread")
            P(lambda e: e.matmul(F[:, 0:2, :], T.bok[:, :], T.sp[:, :], True, True), ("sp", "bok"), (K("S1"),), 64, (kF,), note="inv_p")
            V(lambda e: e.tensor_scalar(T.inv[:, :], F[:, 0:2, :], col(ICOL), None, OP.add), (K("S1"), "icol"), ("inv",), 16, (kF,), note="inv")
            V(lambda e: e.tensor_tensor(T["cw%d" % (t + 1)][:, :], T.ms[:, :].indirect(T.inv[:, :]), cw[:, :], OP.subtract),
              ("ms_0", "ms_1", "msz", "inv", "cw%d" % t), ("cw%d" % (t + 1),), gat(256), note="C")

    for t in range(R):
        for h in range(2):
            k0 = len(ops)
            half(t, h)
            for o in ops[k0:]:
                o["cls"] = 2 * t + h
        if t == 1:
            V(lambda e: e.tensor_tensor(T.qs[:, :], T.qr0[:, :, 0:8], T.qr1[:, :, 0:8], OP.add), ("qr00", "qr01", "qr10", "qr11"), ("qs",), 32)
    V(lambda e: e.tensor_tensor(T.qf[:, :], T.qs[:, :], T.qr2[:, :, 0:8], OP.add), ("qs", "qr20", "qr21"), ("qf",), 32)
    add("Y", lambda e: e.dma_start(T.yq[:, :], T.qf[:, :]), ("qf",), (), (), 2.0, sem="st2", n=16)
    add("Q", lambda e: e.dma_start(T.yc[:, :], T["cw%d" % R][:, :]), ("cw%d" % R,), (), (), 2.0, sem="st3", n=16)
    return ops


def schedule(ops):
    n, names = len(ops), ("A", "V", "P", "G", "Y", None)
    tries, PART, SEED, HEAT = OPT["TRIES"], OPT["PART"], OPT["SEED"], OPT["HEAT"]
    home = [names.index({"Q": "A", "AV": "A"}.get(o["q"], o["q"])) for o in ops]
    took = [[[cost(q, o["c"], C) for q in "AV"] if o["q"] == "AV" else [cost(o["q"], o["c"], C)] * 6 for o in ops] for C in COSTS]
    dma = [o["q"] in ("Y", "Q") for o in ops]
    hops = [[[hop(a, b, C) for b in names] for a in names] for C in COSTS]
    waits, after = [sorted(o["deps"]) for o in ops], [sorted(o["order"]) for o in ops]
    succ, needs = [[] for _ in range(n)], [len(a) + len(b) for a, b in zip(waits, after)]
    for i in range(n):
        for d in waits[i]:
            succ[d].append((i, 2))
        for d in after[i]:
            succ[d].append((i, 1))
        if "after" in ops[i]:
            succ[ops[i]["after"]].append((i, 0))
            needs[i] += 1
    c0, cls, way, plan = took[0], [o.get("cls", -1) for o in ops], [0.0] * n, [0.0] * n
    for i in range(n - 1, -1, -1):
        way[i] = min(c0[i]) + max([way[s] + 0.15 * (k == 2) for s, k in succ[i] if cls[s] == cls[i]] or [0.0])
    top = {k: max(way[i] for i in range(n) if cls[i] == k) for k in set(cls)}
    for i in range(n - 1, -1, -1):
        if cls[i] < 0:
            plan[i] = min([plan[s] for s, _ in succ[i]] or [100.0]) - min(c0[i]) - 0.5
        elif succ[i] and all(cls[s] != cls[i] for s, _ in succ[i]):
            plan[i] = min(plan[s] for s, _ in succ[i]) - 2
        else:
            plan[i] = OPT["STRETCH"] * (top[cls[i]] - way[i]) + OPT["PERIOD"] * (cls[i] // 2) + OPT["LAG"] * (cls[i] % 2)
    first = [i for i in range(n) if needs[i] == 0]
    free_to_choose = [i for i in range(n) if ops[i]["q"] == "AV"]

    def listed(rank, on):
        est, order, need, last = [0.0] * n, [], needs[:], 0.0
        free, low, ready, h0 = [0.0] * 5, [1e9] * 5, [[] for _ in range(5)], hops[0]
        for i in first:
            ready[on[i]].append(i)
            low[on[i]] = 0.0
        while True:
            q, t = -1, 1e8
            for e in range(5):
                r = low[e]
                if r < free[e]:
                    r = free[e]
                if r < t:
                    q, t = e, r
            if q < 0:
                return order, last
            lst = ready[q]
            if len(lst) == 1:
                i = lst.pop()
                low[q] = 1e9
            else:
                b, i, lim = 1e9, -1, t + 0.005
                for j in lst:
                    if rank[j] < b and est[j] <= lim:
                        b, i = rank[j], j
                lst.remove(i)
                low[q] = min([est[j] for j in lst])
            r = est[i] if est[i] > t else t
            free[q] = r + (0.06 if dma[i] else c0[i][q])
            todo = [(i, r)]
            while todo:
                i, r = todo.pop()
                order.append(i)
                q = on[i]
                x, wake = r + c0[i][q], h0[q]
                if x > last:
                    last = x
                for s, k in succ[i]:
                    h = x + wake[on[s]] if k == 2 else x if k else r
                    if h > est[s]:
                        est[s] = h
                    need[s] -= 1
                    if not need[s]:
                        e = on[s]
                        if e == 5:
                            todo.append((s, est[s]))
                        else:
                            ready[e].append(s)
                            if est[s] < low[e]:
                                low[e] = est[s]

    def span(order, on, k):
        wake, cc, done, free = hops[k], took[k], [0.0] * n, [0.0] * 6
        for i in order:
            q = on[i]
            r = free[q]
            for d in waits[i]:
                x = done[d] + wake[on[d]][q]
                if x > r:
                    r = x
            for d in after[i]:
                if done[d] > r:
                    r = done[d]
            done[i] = x = r + cc[i][q]
            if q < 5:
                free[q] = r + 0.06 if dma[i] else x
        return done

    base = [max(span(listed(plan, home)[0], home, k)) for k in range(len(COSTS))]

    def improved(rank, on, tries, seed):
        rng = np.random.default_rng(seed)
        order, now = listed(rank, on)
        cur = sum(max(span(order, on, k)) / b for k, b in enumerate(base))
        best = (cur, rank, on, order)
        for k in range(tries):
            s2, p2, u = rank[:], on, rng.random()
            if u < 0.55:
                for i, d in zip(rng.integers(0, n, (1, 2, 4, 10)[k % 4]).tolist(), rng.normal(0.0, 0.5, 10).tolist()):
                    s2[i] += d
            elif u < 0.7:
                a, d = int(rng.integers(0, n)), float(rng.normal(0.0, 0.5))
                for i in range(a, min(n, a + int(rng.integers(5, 60)))):
                    s2[i] += d
            else:
                p2 = on[:]
                for i in rng.integers(0, len(free_to_choose), 1 + k % 2).tolist():
                    p2[free_to_choose[i]] ^= 1
            order, end = listed(s2, p2)
            if end > 1.006 * now:
                continue
            f, lim = end / base[0], cur + HEAT * (1 - k / tries) * rng.random()
            for j in range(1, len(base)):
                f += max(span(order, p2, j)) / base[j]
            if f < lim:
                cur, rank, on, now = f, s2, p2, end
                if f < best[0]:
                    best = (f, rank, on, order)
        return best
    lags = OPT["LAGS"]
    starts = [improved([r + d * (c % 2 if c >= 0 else 0) for r, c in zip(plan, cls)], home, tries // PART, SEED + k) for k, d in enumerate(lags)]
    _, rank, on, order = improved(*min(starts, key=lambda s: s[0])[1:3], tries - len(lags) * (tries // PART), SEED + 9)
    pick = ["AV"[q] if o["q"] == "AV" else o["q"] for o, q in zip(ops, on)]
    return order, span(order, on, 0), pick, (base, [max(span(order, on, k)) for k in range(len(COSTS))])


def refine(ops, order, pick, tries, seed, heat, costs=COSTS):
    n, names, nm = len(ops), ("A", "V", "P", "G", "Y", None), len(costs)
    on = [names.index({"Q": "A"}.get(q, q)) for q in pick]
    took = [[[cost(q, o["c"], C) for q in "AV"] if o["q"] == "AV" else [cost(o["q"], o["c"], C)] * 6 for o in ops] for C in costs]
    dma = [o["q"] in ("Y", "Q") for o in ops]
    hops = [[[hop(a, b, C) for b in names] for a in names] for C in costs]
    anc, waits, after, pred, succ = [0] * n, [], [], [], [set() for _ in range(n)]
    for i, o in enumerate(ops):
        m = 0
        for d in o["deps"] | o["order"]:
            m |= anc[d]
        waits.append([d for d in sorted(o["deps"]) if not m >> d & 1])
        after.append([d for d in sorted(o["order"]) if not m >> d & 1])
        pred.append(set(waits[i] + after[i] + ([o["after"]] if "after" in o else [])))
        for d in pred[i]:
            m |= 1 << d
            succ[d].add(i)
        anc[i] = m
    flex = [o["q"] == "AV" for o in ops]

    def span(order, on, k, p0, old):
        wake, cc, done, free = hops[k], took[k], old[:], [0.0] * 6
        seen = 0
        for p in range(p0 - 1, -1, -1):
            i = order[p]
            q = on[i]
            if q < 5 and not seen >> q & 1:
                seen |= 1 << q
                free[q] = done[i] - cc[i][q] + 0.06 if dma[i] else done[i]
                if seen & 7 == 7 and p0 > 90:
                    break
        for i in order[p0:]:
            q = on[i]
            r = free[q]
            for d in waits[i]:
                x = done[d] + wake[on[d]][q]
                if x > r:
                    r = x
            if q > 1 or dma[i]:
                for d in after[i]:
                    if done[d] > r:
                        r = done[d]
                done[i] = x = r + cc[i][q]
                if q < 5:
                    free[q] = r + 0.06 if dma[i] else x
            else:
                free[q] = done[i] = r + cc[i][q]
        return done

    def jams(order, on, k, done):
        before, last, out = {}, [-1] * 6, []
        for i in order:
            before[i], last[on[i]] = last[on[i]], i
        j = done.index(max(done))
        wake, cc = hops[k], took[k]
        while j >= 0:
            q, t, i = on[j], 0.0, -1
            for d in waits[j]:
                x = done[d] + wake[on[d]][q]
                if x > t:
                    t, i = x, d
            for d in after[j]:
                if done[d] > t:
                    t, i = done[d], d
            if t < done[j] - cc[j][q] - 1e-6 and q < 5:
                i = before[j]
                if i >= 0:
                    out.append((i, j))
            j = i
        return out

    def shifted(order, pi, pj, back):
        x0, link = (order[pi], succ) if back else (order[pj], pred)
        need, tied, rest = set(link[x0]), [x0], []
        for x in order[pi + 1:pj + 1] if back else order[pi:pj][::-1]:
            if x in need:
                tied.append(x)
                need |= link[x]
            else:
                rest.append(x)
        if tied[-1] == order[pj if back else pi]:
            return None
        return order[:pi] + (rest + tied if back else tied[::-1] + rest[::-1]) + order[pj + 1:]

    rng = np.random.default_rng(seed)
    zero = [0.0] * n
    done = [span(order, on, k, 0, zero) for k in range(nm)]
    base = [max(d) for d in done]
    val = lambda d, k: (max(d) + 0.02 * sum(d) / n) / base[k]
    vals = [val(done[k], k) for k in range(nm)]
    best, jam, age = (sum(vals), order, on), {}, 99
    for it, u in enumerate(rng.random((tries, 6)).tolist()):
        if age > 8:
            st = [done[0][i] - took[0][i][on[i]] for i in range(n)]
            order, age = sorted(order, key=lambda i: st[i]), 0
        on2, x = on, -1
        if u[1] < 0.7:
            k = int(u[0] * nm)
            if k not in jam:
                jam[k] = jams(order, on, k, done[k])
            i, j = jam[k][int(u[2] * len(jam[k]))]
            if u[3] < 0.25 and (flex[i] or flex[j]):
                x = i if flex[i] and (not flex[j] or u[4] < 0.5) else j
                p0 = order.index(x)
            else:
                p0, q, far = order.index(i), on[i], int(u[4] * 3)
                p1 = order.index(j, p0)
                while far and u[3] < 0.6 and p0 > 0:
                    p0 -= 1
                    far -= on[order[p0]] == q
                while far and u[3] >= 0.6 and p1 < n - 1:
                    p1 += 1
                    far -= on[order[p1]] == q
                o2 = shifted(order, p0, p1, u[3] >= 0.6)
        else:
            p0 = p1 = int(u[2] * n)
            if flex[order[p0]] and u[3] < 0.4:
                x = order[p0]
            elif u[3] < 0.7:
                p0 = max(0, p1 - 1 - int(u[4] * 12))
                o2 = shifted(order, p0, p1, False)
            else:
                o2 = shifted(order, p0, min(n - 1, p0 + 1 + int(u[4] * 12)), True)
        if x >= 0:
            on2, o2 = on[:], order
            on2[x] ^= 1
        if o2 is None:
            continue
        slack = -heat * (1 - it / tries) * np.log(u[5])
        d2, v2 = [], []
        for k in range(nm):
            d2.append(span(o2, on2, k, p0, done[k]))
            v2.append(val(d2[k], k))
            if sum(v2) - sum(vals[:k + 1]) > slack + 0.002 * (nm - 1 - k):
                break
        else:
            order, on, done, vals, jam, age = o2, on2, d2, v2, {}, age + 1
            if sum(vals) < best[0]:
                best = (sum(vals), order, on)
    _, order, on = best
    pick = ["AV"[q] if o["q"] == "AV" else o["q"] for o, q in zip(ops, on)]
    done = [span(order, on, k, 0, zero) for k in range(nm)]
    return order, done[0], pick, [max(d) for d in done]


def planned(ops):
    order, _, pick, _ = schedule(ops)
    return refine(ops, order, pick, OPT["MOVES"], OPT["SEED"], OPT["WARM"])


_CACHE = {}


def rank_program(g, core, T, topo):
    if T.rank_of(core) is None:
        return
    ops = build(core, T, topo, [g.vector])
    if "order" not in _CACHE:
        _CACHE["order"] = planned(ops)
    order, done, pick, _ = _CACHE["order"]
    for i, o in enumerate(ops):
        o["q"] = pick[i]
    eng = {"V": g.vector, "A": g.scalar, "P": g.tensor, "G": g, "Y": g.sync, "Q": g.scalar}
    queue = {"V": "V", "A": "A", "Q": "A", "P": "P", "G": "G", "Y": "Y"}
    total, at, clock = {}, {}, {}
    known = {q: {} for q in ("V", "A", "P", "G", "Y")}
    for i in order:
        o = ops[i]
        if o["q"] is None:
            at[i] = (o["sem"], o["n"])
            clock[i] = {o["sem"]: o["n"]}
            continue
        qn = queue[o["q"]]
        e = eng[o["q"]]
        kn = known[qn]
        for d in sorted(o["deps"], key=lambda d: -done[d]):
            s, c = at[d]
            if kn.get(s, 0) < c:
                e.wait_ge(T.sem[s], c)
                for s2, c2 in clock[d].items():
                    kn[s2] = max(kn.get(s2, 0), c2)
        ins = o["fn"](e)
        if o["sem"] is None:
            s, n = o["q"], 1
            total[s] = total.get(s, 0) + n
            ins.then_inc(T.sem[s], n)
        elif o["sem"] == "-sent":
            s = "sent"
            total[s] = total.get(s, 0) + o["n"]
        else:
            s, n = o["sem"], o["n"]
            total[s] = total.get(s, 0) + n
            ins.then_inc(T.sem[s], n)
        at[i] = (s, total[s])
        clock[i] = dict(kn)
        clock[i][s] = total[s]
    for s, c in total.items():
        if known["G"].get(s, 0) < c:
            g.wait_ge(T.sem[s], c)
